import numpy as np
import ml_dtypes


def mxq(x, axis, fmt="e4m3"):
    dtype, down = {"e4m3": (ml_dtypes.float8_e4m3fn, 7), "e5m2": (ml_dtypes.float8_e5m2, 14)}[fmt]
    v = np.moveaxis(np.asarray(x, np.float32).astype(ml_dtypes.bfloat16).astype(np.float64), axis, -1)
    blocks = v.reshape(v.shape[:-1] + (-1, 32))
    amax = np.abs(blocks).max(-1, keepdims=True)
    byte = np.maximum(np.where(amax > 0, np.frexp(amax)[1] - 1 + 127, 0) - down, 1)
    scale = np.exp2(byte - 127.0)
    codes = (blocks / scale).astype(np.float32).astype(dtype).astype(np.float64)
    return np.moveaxis((codes * scale).reshape(v.shape), -1, axis)


WIDE = False


def mx_kscale(k):
    if not WIDE:
        return np.ones(k)
    levels = np.array([10, -10, 5, -5, 0])
    if k % 512:
        return np.exp2(np.random.permutation(np.resize(levels, k // 32))).repeat(32)
    a = np.empty((k // 512, 16))
    for p in range(k // 512):
        a[p, :8] = np.random.permutation(np.resize(levels, 8))
        for g in range(8):
            far = levels[np.abs(levels - a[p, g]) >= 10]
            a[p, g + 8] = far[np.random.randint(len(far))]
    return np.exp2(a.ravel()).repeat(32)


def f64(x):
    return np.asarray(x).astype(np.float64)


def striped(idx):
    return np.tile(np.asarray(idx).reshape(-1, 16).T, (8, 1)).astype(np.uint16)


def unstriped(offs):
    return offs[:16].T.reshape(-1).astype(np.int64)


E2M1 = np.array([0.0, 0.5, 1.0, 1.5, 2.0, 3.0, 4.0, 6.0, -0.0, -0.5, -1.0, -1.5, -2.0, -3.0, -4.0, -6.0])


def pack_weight(w, fmt):
    k, n = w.shape
    w = f64(np.asarray(w, np.float32).astype(ml_dtypes.bfloat16)).reshape(k // 32, 32, n)
    amax = np.abs(w).max(1)
    if fmt == "e4m3":
        byte = np.frexp(amax)[1] - 1 + 127 - 7
    else:
        mant, ex = np.frexp(amax / 6.0)
        byte = np.where(mant > 0.5, ex, ex - 1) + 127
    byte = np.clip(np.where(amax > 0, byte, 1), 1, 254)
    scaled = (w * np.exp2(127.0 - byte)[:, None, :]).reshape(k, n).astype(np.float32)
    by_word = np.ascontiguousarray(scaled.reshape(k // 512, 128, 4, n).transpose(0, 1, 3, 2))
    if fmt == "e4m3":
        words = by_word.astype(ml_dtypes.float8_e4m3fn).view(np.uint8)
    else:
        c = by_word.astype(ml_dtypes.float4_e2m1fn).view(np.uint8) & 0xF
        words = (c[..., 0::2] | (c[..., 1::2] << 4)).reshape(k // 512, 128, 2 * n)
    return np.ascontiguousarray(words), np.ascontiguousarray(byte.astype(np.uint8).reshape(k // 512, 16, n))


def unpack_weight(words, scales, fmt):
    g, _, n = scales.shape
    words = np.ascontiguousarray(words).reshape(g, 128, n, -1)
    if fmt == "e4m3":
        vals = words.view(ml_dtypes.float8_e4m3fn).astype(np.float64)
    else:
        nib = np.empty((g, 128, n, 4), np.uint8)
        nib[..., 0::2] = words & 0xF
        nib[..., 1::2] = words >> 4
        vals = E2M1[nib]
    vals = vals * np.repeat(np.exp2(scales.astype(np.float64) - 127.0), 8, axis=1)[..., None]
    return vals.transpose(0, 1, 3, 2).reshape(g * 512, n)


def bf(x):
    return np.asarray(x, np.float32).astype(ml_dtypes.bfloat16)


def planes(Y):
    r, m = Y.shape
    b = f64(bf(Y)).reshape(r // 32, 32, m)
    amax = np.abs(b).max(1)
    byte = np.clip(np.where(amax > 0, np.frexp(amax)[1] - 1 + 127 - 7, 1), 1, 254)
    codes = (b * np.exp2(127.0 - byte)[:, None, :]).reshape(r, m).astype(np.float32).astype(ml_dtypes.float8_e4m3fn).view(np.uint8)
    words = codes.reshape(r // 512, 128, 4, m).transpose(0, 1, 3, 2)
    return np.ascontiguousarray(words), np.ascontiguousarray(byte.astype(np.uint8).reshape(r // 512, 16, m))


D, T, I, Q, E, G = 512, 2048, 1024, 256, 512, 64


def setup_inputs():
    n = np.random.standard_normal
    idx = (np.random.permutation(T // 16)[:I // 16, None] * 16 + np.arange(16)).reshape(-1)
    fd = mx_kscale(D)
    fi = mx_kscale(I)
    ti = np.ones(T)
    ti[idx] = fi
    keysp = pack_weight(n((D, T)) / fd[:, None], "e2m1")
    return {
        "query": (n((D, Q)) * 0.6 / np.sqrt(D) * fd[:, None]).astype(np.float32),
        "keys_words": keysp[0],
        "keys_scales": keysp[1],
        "size": (np.random.uniform(0.5, 2.0, (1, I)) * fi).astype(np.float32),
        "vals": (n((E, T)) / ti).astype(np.float32),
        "offs": striped(idx),
    }


def reference(query, keys_words, keys_scales, size, vals, offs):
    idx = unstriped(offs)
    keysu = unpack_weight(keys_words, keys_scales, "e2m1")
    queryq = mxq(f64(query), 0, "e4m3")
    keysidxg = keysu[:, idx]
    a = queryq.T @ keysidxg
    m = a.reshape(Q, G, I // G).max(axis=2)
    r = np.exp(m - np.max(m, axis=1, keepdims=True))
    p = np.exp(a)
    z = p.reshape(Q, G, I // G).sum(axis=2)
    f = r / np.sum(r, axis=1, keepdims=True) / z
    fr = np.repeat(f, I // G, axis=1)
    w = p * fr * f64(size)
    wt = w.T
    vt = f64(vals)[:, idx].T
    vtq = mxq(vt, 0, "e4m3")
    wtq = mxq(wt, 0, "e4m3")
    o = vtq.T @ wtq
    words, scales = planes(o)
    return o, words, scales

@@ -1,0 +1,263 @@
+from contextlib import ExitStack
+
+import concourse.mybir as mybir
+from concourse.masks import make_identity
+
+D, T, I, Q, E, G = 512, 2048, 1024, 256, 512, 64
+FLOPS = 2 * D * Q * I + 2 * I * E * Q
+
+F32 = mybir.dt.float32
+BF16 = mybir.dt.bfloat16
+I32 = mybir.dt.int32
+U32 = mybir.dt.uint32
+U16 = mybir.dt.uint16
+U8 = mybir.dt.uint8
+FP8X4 = mybir.dt.float8_e4m3fn_x4
+FP4X4 = mybir.dt.float4_e2m1fn_x4
+ALU = mybir.AluOpType
+ACT = mybir.ActivationFunctionType
+AXIS_X = mybir.AxisListType.X
+
+P = 128
+PACK = 4
+PASS = P * PACK
+RUN = I // G
+PASSES = I // PASS
+QTILES = Q // P
+PAIRS = 2
+CHUNK = 512
+TINY = 1e-30
+
+
+def tile_attend_docmix_pl_kernel(tc, query, keys_words, keys_scales, size, vals, offs, out_0, out_1, out_2):
+    nc = tc.nc
+    with ExitStack() as ctx:
+        sb = ctx.enter_context(tc.tile_pool(name="sb", bufs=1))
+        ps = ctx.enter_context(tc.psum_pool(name="ps", bufs=1))
+
+        def tile(shape, dtype, name):
+            return sb.tile(shape, dtype, name=name, align_bytes=64)
+
+        def bank(shape, number, name):
+            return ps.tile(shape, F32, name=name, tag="bank%d" % number)
+
+        offsets = sb.tile([P, I // 16], U16, name="offsets")
+        key_pool = tile([P, T], U16, "key_pool")
+        scale_pool = tile([P, T], U8, "scale_pool")
+        warm_in = tile([P, 1], F32, "warm_in")
+        warm_out = tile([P, 1], F32, "warm_out")
+        nc.vector.memset(scale_pool[:].bitcast(I32), 0)
+        nc.vector.memset(warm_in[:], 0.0)
+        nc.sync.dma_start(offsets[:], offs)
+        nc.sync.dma_start(key_pool[:].bitcast(I32), keys_words[0].bitcast(I32))
+        for quad in range(4):
+            nc.sync.dma_start(
+                scale_pool[32 * quad : 32 * quad + 4, :].bitcast(I32),
+                keys_scales[0, 4 * quad : 4 * quad + 4, :].bitcast(I32),
+            )
+        nc.scalar.activation(warm_out[:], warm_in[:], ACT.Exp)
+        q_raw = tile([P, PACK, Q], F32, "q_raw")
+        nc.sync.dma_start(q_raw[:], query.rearrange("(p j) q -> p j q", j=PACK))
+        size_cols = tile([P, I // P], F32, "size_cols")
+        nc.sync.dma_start(size_cols[:], size.rearrange("o (p c) -> (o p) c", p=P))
+        vals_rows = vals.rearrange("(p t) n -> p t n", t=PACK)
+        v_raw = {}
+        for pair in range(PAIRS):
+            for c in range(T // CHUNK):
+                v_raw[pair, c] = tile([P, 2, CHUNK], F32, "v_raw%d_%d" % (pair, c))
+                nc.sync.dma_start(
+                    v_raw[pair, c][:], vals_rows[:, 2 * pair : 2 * pair + 2, c * CHUNK : (c + 1) * CHUNK]
+                )
+
+        ident = tile([P, P], F32, "ident")
+        make_identity(nc, ident[:])
+
+        cols = PASS // 16
+        key_words = []
+        for g in range(PASSES):
+            key_words.append(tile([P, PASS], U16, "key_words%d" % g))
+        key_scales = tile([P, I], U8, "key_scales")
+        nc.vector.tensor_copy(key_words[0][:], key_pool[:].indirect(offsets[:, 0:cols]))
+        nc.vector.tensor_copy(key_scales[:], scale_pool[:].indirect(offsets[:]))
+
+        q_bf = tile([P, Q, PACK], BF16, "q_bf")
+        nc.scalar.copy(
+            q_bf[:].rearrange("p (c i) j -> p c j i", i=4), q_raw[:].rearrange("p j (c i) -> p c j i", i=4)
+        )
+        q_codes = tile([P, Q], U32, "q_codes")
+        q_scales = tile([P, Q], U8, "q_scales")
+        nc.vector.quantize_mx(
+            out=q_codes[:].bitcast(FP8X4), scales=q_scales[:], in_=q_bf[:].rearrange("p q j -> p (q j)")
+        )
+        nc.vector.tensor_copy(key_words[1][:], key_pool[:].indirect(offsets[:, cols : 2 * cols]))
+
+        size_all = tile([P, P, I // P], F32, "size_all")
+        for half in range(2):
+            spread = bank([P, 4, P], 4 + half, "spread%d" % half)
+            for c in range(4):
+                col = 4 * half + c
+                nc.tensor.transpose(spread[:, c, :], size_cols[:, col : col + 1].to_broadcast([P, P]), ident[:])
+            nc.scalar.copy(size_all[:, :, 4 * half : 4 * half + 4], spread[:].rearrange("p c r -> p r c"))
+        size_row = size_all[:].rearrange("p r c -> p (r c)")
+
+        scores = {}
+        for g in range(PASSES):
+            for qt in range(QTILES):
+                scores[qt, g] = bank([P, PASS], 2 * qt + g, "scores%d_%d" % (qt, g))
+                nc.tensor.matmul_mx(
+                    out=scores[qt, g][:],
+                    lhsT=q_codes[:, qt * P : (qt + 1) * P].bitcast(FP8X4),
+                    lhsT_scale=q_scales[:, qt * P : (qt + 1) * P],
+                    rhs=key_words[g][:].bitcast(FP4X4),
+                    rhs_scale=key_scales[:, g * PASS : (g + 1) * PASS],
+                    start=True,
+                    stop=True,
+                )
+
+        windows = []
+        for pair in range(PAIRS):
+            windows.append(tile([P, T], F32, "window%d" % pair))
+
+        def cast(pair, c):
+            dst = windows[pair][:, c * CHUNK : (c + 1) * CHUNK].bitcast(BF16)
+            nc.scalar.activation(
+                dst.rearrange("p (m h j) -> p m h j", h=2, j=PACK),
+                v_raw[pair, c][:].rearrange("p h (m j) -> p m h j", j=PACK),
+                ACT.Copy,
+            )
+
+        v_codes, v_scales, v_bf = {}, {}, {}
+
+        def gather_values(pair, g, number):
+            picked = tile([P, PASS], F32, "picked%d_%d" % (pair, g))
+            nc.vector.tensor_copy(picked[:], windows[pair][:].indirect(offsets[:, g * cols : (g + 1) * cols]))
+            turned = bank([P, 4, P], number, "v_turned%d_%d" % (pair, g))
+            for c in range(4):
+                nc.tensor.transpose(turned[:, c, :], picked[:, c:PASS:4], ident[:])
+            v_bf[pair, g] = tile([P, PASS], F32, "v_bf%d_%d" % (pair, g))
+            nc.scalar.copy(
+                v_bf[pair, g][:].rearrange("p (h e u) -> p h e u", h=2, u=2),
+                turned[:].rearrange("p (h u) e -> p h e u", u=2),
+            )
+
+        def quantize_values(pair, g):
+            v_codes[pair, g] = tile([P, 2 * P], U32, "v_codes%d_%d" % (pair, g))
+            v_scales[pair, g] = tile([P, 2 * P], U8, "v_scales%d_%d" % (pair, g))
+            nc.vector.quantize_mx(
+                out=v_codes[pair, g][:].bitcast(FP8X4), scales=v_scales[pair, g][:], in_=v_bf[pair, g][:].bitcast(BF16)
+            )
+
+        for c in range(T // CHUNK):
+            cast(0, c)
+
+        per = PASS // RUN
+        best, neg_top, probs, share_sum, share, total, factor = {}, {}, {}, {}, {}, {}, {}
+        for qt in range(QTILES):
+            best[qt] = tile([P, G], F32, "best%d" % qt)
+            for g in range(PASSES):
+                nc.vector.tensor_reduce(
+                    best[qt][:, g * per : (g + 1) * per],
+                    scores[qt, g][:].rearrange("p (s i) -> p s i", i=RUN),
+                    AXIS_X,
+                    ALU.max,
+                )
+            neg_top[qt] = tile([P, 1], F32, "neg_top%d" % qt)
+            nc.vector.tensor_reduce(neg_top[qt][:], best[qt][:], AXIS_X, ALU.max, negate=True)
+            for g in range(PASSES):
+                probs[qt, g] = tile([P, PASS], F32, "probs%d_%d" % (qt, g))
+                nc.scalar.activation(probs[qt, g][:], scores[qt, g][:], ACT.Exp, bias=neg_top[qt][:])
+            share[qt] = tile([P, G], F32, "share%d" % qt)
+            share_sum[qt] = tile([P, 1], F32, "share_sum%d" % qt)
+            nc.scalar.activation(share[qt][:], best[qt][:], ACT.Exp, bias=neg_top[qt][:], accum_out=share_sum[qt][:])
+
+        for c in range(T // CHUNK):
+            cast(1, c)
+
+        sized, w_bf = {}, {}
+        for qt in range(QTILES):
+            total[qt] = tile([P, G], F32, "total%d" % qt)
+            for g in range(PASSES):
+                nc.vector.tensor_reduce(
+                    total[qt][:, g * per : (g + 1) * per],
+                    probs[qt, g][:].rearrange("p (s i) -> p s i", i=RUN),
+                    AXIS_X,
+                    ALU.add,
+                )
+            denom = tile([P, G], F32, "denom%d" % qt)
+            nc.vector.tensor_scalar(denom[:], total[qt][:], TINY, share_sum[qt][:], ALU.max, ALU.mult)
+            sized[qt, 0] = tile([P, PASS], F32, "sized%d_0" % qt)
+            nc.vector.tensor_tensor(sized[qt, 0][:], probs[qt, 0][:], size_row[:, 0:PASS], ALU.mult)
+            inverse = tile([P, G], F32, "inverse%d" % qt)
+            nc.vector.reciprocal(inverse[:], denom[:])
+            sized[qt, 1] = tile([P, PASS], F32, "sized%d_1" % qt)
+            nc.vector.tensor_tensor(sized[qt, 1][:], probs[qt, 1][:], size_row[:, PASS : 2 * PASS], ALU.mult)
+            factor[qt] = tile([P, G], F32, "factor%d" % qt)
+            nc.vector.tensor_tensor(factor[qt][:], share[qt][:], inverse[:], ALU.mult)
+            gather_values(0, qt, 6 + qt)
+            for g in range(PASSES):
+                w_bf[qt, g] = tile([P, PASS // 2], F32, "w_bf%d_%d" % (qt, g))
+                nc.vector.tensor_tensor(
+                    w_bf[qt, g][:].bitcast(BF16).rearrange("p (s i) -> p s i", i=RUN),
+                    sized[qt, g][:].rearrange("p (s i) -> p s i", i=RUN),
+                    factor[qt][:, g * per : (g + 1) * per].unsqueeze(2).to_broadcast([P, per, RUN]),
+                    ALU.mult,
+                )
+
+        wt_bf = {}
+        for g in range(PASSES):
+            turned = bank([P, QTILES, 2, P], 4 + g, "w_turned%d" % g)
+            for qt in range(QTILES):
+                for u in range(2):
+                    nc.tensor.transpose(turned[:, qt, u, :], w_bf[qt, g][:, u : PASS // 2 : 2], ident[:])
+            wt_bf[g] = tile([P, 2 * Q], F32, "wt_bf%d" % g)
+            nc.scalar.copy(
+                wt_bf[g][:].rearrange("p (a q u) -> p a q u", a=QTILES, u=2),
+                turned[:].rearrange("p a u q -> p a q u"),
+            )
+
+        gather_values(1, 0, 0)
+        for g in range(PASSES):
+            quantize_values(0, g)
+        gather_values(1, 1, 1)
+        w_codes, w_scales = {}, {}
+        for g in range(PASSES):
+            w_codes[g] = tile([P, Q], U32, "w_codes%d" % g)
+            w_scales[g] = tile([P, Q], U8, "w_scales%d" % g)
+            nc.vector.quantize_mx(out=w_codes[g][:].bitcast(FP8X4), scales=w_scales[g][:], in_=wt_bf[g][:].bitcast(BF16))
+        for g in range(PASSES):
+            quantize_values(1, g)
+
+        y = tile([P, PACK, Q], F32, "y")
+        out_rows = out_0.rearrange("(p t) q -> p t q", t=PACK)
+        for pair in range(PAIRS):
+            acc = bank([P, 2, Q], 2 + pair, "acc%d" % pair)
+            for h in range(2):
+                for g in range(PASSES):
+                    nc.tensor.matmul_mx(
+                        out=acc[:, h, :],
+                        lhsT=v_codes[pair, g][:, h * P : (h + 1) * P].bitcast(FP8X4),
+                        lhsT_scale=v_scales[pair, g][:, h * P : (h + 1) * P],
+                        rhs=w_codes[g][:].bitcast(FP8X4),
+                        rhs_scale=w_scales[g][:],
+                        start=(g == 0),
+                        stop=(g == PASSES - 1),
+                    )
+            nc.scalar.copy(y[:, 2 * pair : 2 * pair + 2, :], acc[:])
+            nc.sync.dma_start(out_rows[:, 2 * pair : 2 * pair + 2, :], y[:, 2 * pair : 2 * pair + 2, :])
+
+        y_bf = tile([P, Q, PACK], BF16, "y_bf")
+        nc.vector.tensor_copy(
+            y_bf[:].rearrange("p (c i) t -> p c t i", i=4), y[:].rearrange("p t (c i) -> p c t i", i=4)
+        )
+        y_codes = tile([P, Q], U32, "y_codes")
+        y_scales = tile([P, Q], U8, "y_scales")
+        nc.vector.quantize_mx(
+            out=y_codes[:].bitcast(FP8X4), scales=y_scales[:], in_=y_bf[:].rearrange("p q t -> p (q t)")
+        )
+        nc.sync.dma_start(out_1[0].rearrange("p q t -> p (q t)").bitcast(I32), y_codes[:].bitcast(I32))
+        for quad in range(4):
+            queue = nc.scalar if quad % 2 == 0 else nc.sync
+            queue.dma_start(
+                out_2[0, 4 * quad : 4 * quad + 4, :].bitcast(I32),
+                y_scales[32 * quad : 32 * quad + 4, :].bitcast(I32),
+            )

@@ -35,109 +35,118 @@ def tile_attend_docmix_pl_kernel(tc, query, keys_words, keys_scales, size, vals,
         sb = ctx.enter_context(tc.tile_pool(name="sb", bufs=1))
         ps = ctx.enter_context(tc.psum_pool(name="ps", bufs=1))
 
-        def tile(shape, dtype, name):
-            return sb.tile(shape, dtype, name=name, align_bytes=64)
+        def tile(shape, dtype, name, tag=None):
+            return sb.tile(shape, dtype, name=name, tag=tag or name, align_bytes=64)
 
         def bank(shape, number, name):
             return ps.tile(shape, F32, name=name, tag="bank%d" % number)
 
+        cols = PASS // 16
+        per = PASS // RUN
         offsets = sb.tile([P, I // 16], U16, name="offsets")
         key_pool = tile([P, T], U16, "key_pool")
         scale_pool = tile([P, T], U8, "scale_pool")
         warm_in = tile([P, 1], F32, "warm_in")
         warm_out = tile([P, 1], F32, "warm_out")
-        nc.vector.memset(scale_pool[:].bitcast(I32), 0)
-        nc.vector.memset(warm_in[:], 0.0)
-        nc.sync.dma_start(offsets[:], offs)
-        nc.sync.dma_start(key_pool[:].bitcast(I32), keys_words[0].bitcast(I32))
-        for quad in range(4):
-            nc.sync.dma_start(
-                scale_pool[32 * quad : 32 * quad + 4, :].bitcast(I32),
-                keys_scales[0, 4 * quad : 4 * quad + 4, :].bitcast(I32),
-            )
-        nc.scalar.activation(warm_out[:], warm_in[:], ACT.Exp)
-        q_raw = tile([P, PACK, Q], F32, "q_raw")
-        nc.sync.dma_start(q_raw[:], query.rearrange("(p j) q -> p j q", j=PACK))
         size_cols = tile([P, I // P], F32, "size_cols")
-        nc.sync.dma_start(size_cols[:], size.rearrange("o (p c) -> (o p) c", p=P))
+        q_raw = tile([P, PACK, Q], F32, "q_raw")
+        ident = tile([P, P], F32, "ident")
         vals_rows = vals.rearrange("(p t) n -> p t n", t=PACK)
-        v_raw = {}
-        for pair in range(PAIRS):
-            for c in range(T // CHUNK):
-                v_raw[pair, c] = tile([P, 2, CHUNK], F32, "v_raw%d_%d" % (pair, c))
+        out_rows = out_0.rearrange("(p t) q -> p t q", t=PACK)
+        v_raw, windows, key_words, key_scales, scores = {}, {}, {}, {}, {}
+        v_codes, v_scales, v_bf, v_turned = {}, {}, {}, {}
+        best, neg_top, probs, share_sum, share, total, factor, denom, inverse = {}, {}, {}, {}, {}, {}, {}, {}, {}
+        sized, w_bf, wt_bf, w_codes, w_scales, acc, back = {}, {}, {}, {}, {}, {}, {}
+        tags = {"probs0_0": "v_raw0_2", "probs0_1": "v_raw0_3"}
+
+        def load_vals(pair, c):
+            v_raw[pair, c] = tile([P, 2, CHUNK], F32, "v_raw%d_%d" % (pair, c))
+            nc.sync.dma_start(v_raw[pair, c][:], vals_rows[:, 2 * pair : 2 * pair + 2, c * CHUNK : (c + 1) * CHUNK])
+
+        def load_q():
+            nc.sync.dma_start(q_raw[:], query.rearrange("(p j) q -> p j q", j=PACK))
+
+        def load_size():
+            nc.sync.dma_start(size_cols[:], size.rearrange("o (p c) -> (o p) c", p=P))
+
+        def load_keys():
+            nc.sync.dma_start(key_pool[:].bitcast(I32), keys_words[0].bitcast(I32))
+
+        def load_scales():
+            for quad in range(4):
                 nc.sync.dma_start(
-                    v_raw[pair, c][:], vals_rows[:, 2 * pair : 2 * pair + 2, c * CHUNK : (c + 1) * CHUNK]
+                    scale_pool[32 * quad : 32 * quad + 4, :].bitcast(I32),
+                    keys_scales[0, 4 * quad : 4 * quad + 4, :].bitcast(I32),
                 )
 
-        ident = tile([P, P], F32, "ident")
-        make_identity(nc, ident[:])
+        def gather_words(g):
+            key_words[g] = tile([P, PASS], U16, "key_words%d" % g)
+            nc.vector.tensor_copy(key_words[g][:], key_pool[:].indirect(offsets[:, g * cols : (g + 1) * cols]))
 
-        cols = PASS // 16
-        key_words = []
-        for g in range(PASSES):
-            key_words.append(tile([P, PASS], U16, "key_words%d" % g))
-        key_scales = tile([P, I], U8, "key_scales")
-        nc.vector.tensor_copy(key_words[0][:], key_pool[:].indirect(offsets[:, 0:cols]))
-        nc.vector.tensor_copy(key_scales[:], scale_pool[:].indirect(offsets[:]))
+        def gather_scales(g):
+            key_scales[g] = tile([P, PASS], U8, "key_scales%d" % g)
+            nc.vector.tensor_copy(key_scales[g][:], scale_pool[:].indirect(offsets[:, g * cols : (g + 1) * cols]))
 
         q_bf = tile([P, Q, PACK], BF16, "q_bf")
-        nc.scalar.copy(
-            q_bf[:].rearrange("p (c i) j -> p c j i", i=4), q_raw[:].rearrange("p j (c i) -> p c j i", i=4)
-        )
         q_codes = tile([P, Q], U32, "q_codes")
         q_scales = tile([P, Q], U8, "q_scales")
-        nc.vector.quantize_mx(
-            out=q_codes[:].bitcast(FP8X4), scales=q_scales[:], in_=q_bf[:].rearrange("p q j -> p (q j)")
-        )
-        nc.vector.tensor_copy(key_words[1][:], key_pool[:].indirect(offsets[:, cols : 2 * cols]))
 
-        size_all = tile([P, P, I // P], F32, "size_all")
-        for half in range(2):
-            spread = bank([P, 4, P], 4 + half, "spread%d" % half)
-            for c in range(4):
-                col = 4 * half + c
-                nc.tensor.transpose(spread[:, c, :], size_cols[:, col : col + 1].to_broadcast([P, P]), ident[:])
-            nc.scalar.copy(size_all[:, :, 4 * half : 4 * half + 4], spread[:].rearrange("p c r -> p r c"))
-        size_row = size_all[:].rearrange("p r c -> p (r c)")
-
-        scores = {}
-        for g in range(PASSES):
-            for qt in range(QTILES):
-                scores[qt, g] = bank([P, PASS], 2 * qt + g, "scores%d_%d" % (qt, g))
-                nc.tensor.matmul_mx(
-                    out=scores[qt, g][:],
-                    lhsT=q_codes[:, qt * P : (qt + 1) * P].bitcast(FP8X4),
-                    lhsT_scale=q_scales[:, qt * P : (qt + 1) * P],
-                    rhs=key_words[g][:].bitcast(FP4X4),
-                    rhs_scale=key_scales[:, g * PASS : (g + 1) * PASS],
-                    start=True,
-                    stop=True,
-                )
-
-        windows = []
-        for pair in range(PAIRS):
-            windows.append(tile([P, T], F32, "window%d" % pair))
-
-        def cast(pair, c):
-            dst = windows[pair][:, c * CHUNK : (c + 1) * CHUNK].bitcast(BF16)
-            nc.scalar.activation(
-                dst.rearrange("p (m h j) -> p m h j", h=2, j=PACK),
-                v_raw[pair, c][:].rearrange("p h (m j) -> p m h j", j=PACK),
-                ACT.Copy,
+        def quantize_q():
+            nc.scalar.copy(
+                q_bf[:].rearrange("p (c i) j -> p c j i", i=4), q_raw[:].rearrange("p j (c i) -> p c j i", i=4)
+            )
+            nc.vector.quantize_mx(
+                out=q_codes[:].bitcast(FP8X4), scales=q_scales[:], in_=q_bf[:].rearrange("p q j -> p (q j)")
             )
 
-        v_codes, v_scales, v_bf = {}, {}, {}
+        size_all = tile([P, P, I // P], F32, "size_all")
+        size_row = size_all[:].rearrange("p r c -> p (r c)")
+
+        def spread_size():
+            for half in range(2):
+                spread = bank([P, 4, P], 4 + half, "spread%d" % half)
+                for c in range(4):
+                    col = 4 * half + c
+                    nc.tensor.transpose(spread[:, c, :], size_cols[:, col : col + 1].to_broadcast([P, P]), ident[:])
+                nc.scalar.copy(size_all[:, :, 4 * half : 4 * half + 4], spread[:].rearrange("p c r -> p r c"))
+
+        def score(qt, g):
+            scores[qt, g] = bank([P, PASS], 2 * qt + g, "scores%d_%d" % (qt, g))
+            nc.tensor.matmul_mx(
+                out=scores[qt, g][:],
+                lhsT=q_codes[:, qt * P : (qt + 1) * P].bitcast(FP8X4),
+                lhsT_scale=q_scales[:, qt * P : (qt + 1) * P],
+                rhs=key_words[g][:].bitcast(FP4X4),
+                rhs_scale=key_scales[g][:],
+                start=True,
+                stop=True,
+            )
+
+        for pair in range(PAIRS):
+            windows[pair] = tile([P, T], F32, "window%d" % pair)
+
+        def cast(pair, c, engine="scalar"):
+            dst = windows[pair][:, c * CHUNK : (c + 1) * CHUNK].bitcast(BF16).rearrange("p (m h j) -> p m h j", h=2, j=PACK)
+            src = v_raw[pair, c][:].rearrange("p h (m j) -> p m h j", j=PACK)
+            if engine == "scalar":
+                nc.scalar.activation(dst, src, ACT.Copy)
+            else:
+                nc.vector.tensor_copy(dst, src)
 
         def gather_values(pair, g, number):
-            picked = tile([P, PASS], F32, "picked%d_%d" % (pair, g))
+            name = "picked%d_%d" % (pair, g)
+            picked = tile([P, PASS], F32, name, tags.get(name))
             nc.vector.tensor_copy(picked[:], windows[pair][:].indirect(offsets[:, g * cols : (g + 1) * cols]))
-            turned = bank([P, 4, P], number, "v_turned%d_%d" % (pair, g))
+            v_turned[pair, g] = bank([P, 4, P], number, "v_turned%d_%d" % (pair, g))
             for c in range(4):
-                nc.tensor.transpose(turned[:, c, :], picked[:, c:PASS:4], ident[:])
-            v_bf[pair, g] = tile([P, PASS], F32, "v_bf%d_%d" % (pair, g))
+                nc.tensor.transpose(v_turned[pair, g][:, c, :], picked[:, c:PASS:4], ident[:])
+
+        def copy_values(pair, g):
+            name = "v_bf%d_%d" % (pair, g)
+            v_bf[pair, g] = tile([P, PASS], F32, name, tags.get(name))
             nc.scalar.copy(
                 v_bf[pair, g][:].rearrange("p (h e u) -> p h e u", h=2, u=2),
-                turned[:].rearrange("p (h u) e -> p h e u", u=2),
+                v_turned[pair, g][:].rearrange("p (h u) e -> p h e u", u=2),
             )
 
         def quantize_values(pair, g):
@@ -147,12 +156,7 @@ def tile_attend_docmix_pl_kernel(tc, query, keys_words, keys_scales, size, vals,
                 out=v_codes[pair, g][:].bitcast(FP8X4), scales=v_scales[pair, g][:], in_=v_bf[pair, g][:].bitcast(BF16)
             )
 
-        for c in range(T // CHUNK):
-            cast(0, c)
-
-        per = PASS // RUN
-        best, neg_top, probs, share_sum, share, total, factor = {}, {}, {}, {}, {}, {}, {}
-        for qt in range(QTILES):
+        def maxima(qt):
             best[qt] = tile([P, G], F32, "best%d" % qt)
             for g in range(PASSES):
                 nc.vector.tensor_reduce(
@@ -163,18 +167,22 @@ def tile_attend_docmix_pl_kernel(tc, query, keys_words, keys_scales, size, vals,
                 )
             neg_top[qt] = tile([P, 1], F32, "neg_top%d" % qt)
             nc.vector.tensor_reduce(neg_top[qt][:], best[qt][:], AXIS_X, ALU.max, negate=True)
+
+        def exps(qt):
             for g in range(PASSES):
-                probs[qt, g] = tile([P, PASS], F32, "probs%d_%d" % (qt, g))
+                name = "probs%d_%d" % (qt, g)
+                probs[qt, g] = tile([P, PASS], F32, name, tags.get(name))
                 nc.scalar.activation(probs[qt, g][:], scores[qt, g][:], ACT.Exp, bias=neg_top[qt][:])
             share[qt] = tile([P, G], F32, "share%d" % qt)
             share_sum[qt] = tile([P, 1], F32, "share_sum%d" % qt)
             nc.scalar.activation(share[qt][:], best[qt][:], ACT.Exp, bias=neg_top[qt][:], accum_out=share_sum[qt][:])
 
-        for c in range(T // CHUNK):
-            cast(1, c)
+        def times_size(qt):
+            for g in range(PASSES):
+                sized[qt, g] = tile([P, PASS], F32, "sized%d_%d" % (qt, g))
+                nc.gpsimd.tensor_tensor(sized[qt, g][:], probs[qt, g][:], size_row[:, g * PASS : (g + 1) * PASS], ALU.mult)
 
-        sized, w_bf = {}, {}
-        for qt in range(QTILES):
+        def sums(qt):
             total[qt] = tile([P, G], F32, "total%d" % qt)
             for g in range(PASSES):
                 nc.vector.tensor_reduce(
@@ -183,81 +191,169 @@ def tile_attend_docmix_pl_kernel(tc, query, keys_words, keys_scales, size, vals,
                     AXIS_X,
                     ALU.add,
                 )
-            denom = tile([P, G], F32, "denom%d" % qt)
-            nc.vector.tensor_scalar(denom[:], total[qt][:], TINY, share_sum[qt][:], ALU.max, ALU.mult)
-            sized[qt, 0] = tile([P, PASS], F32, "sized%d_0" % qt)
-            nc.vector.tensor_tensor(sized[qt, 0][:], probs[qt, 0][:], size_row[:, 0:PASS], ALU.mult)
-            inverse = tile([P, G], F32, "inverse%d" % qt)
-            nc.vector.reciprocal(inverse[:], denom[:])
-            sized[qt, 1] = tile([P, PASS], F32, "sized%d_1" % qt)
-            nc.vector.tensor_tensor(sized[qt, 1][:], probs[qt, 1][:], size_row[:, PASS : 2 * PASS], ALU.mult)
-            factor[qt] = tile([P, G], F32, "factor%d" % qt)
-            nc.vector.tensor_tensor(factor[qt][:], share[qt][:], inverse[:], ALU.mult)
-            gather_values(0, qt, 6 + qt)
-            for g in range(PASSES):
-                w_bf[qt, g] = tile([P, PASS // 2], F32, "w_bf%d_%d" % (qt, g))
-                nc.vector.tensor_tensor(
-                    w_bf[qt, g][:].bitcast(BF16).rearrange("p (s i) -> p s i", i=RUN),
-                    sized[qt, g][:].rearrange("p (s i) -> p s i", i=RUN),
-                    factor[qt][:, g * per : (g + 1) * per].unsqueeze(2).to_broadcast([P, per, RUN]),
-                    ALU.mult,
-                )
 
-        wt_bf = {}
-        for g in range(PASSES):
-            turned = bank([P, QTILES, 2, P], 4 + g, "w_turned%d" % g)
-            for qt in range(QTILES):
-                for u in range(2):
-                    nc.tensor.transpose(turned[:, qt, u, :], w_bf[qt, g][:, u : PASS // 2 : 2], ident[:])
-            wt_bf[g] = tile([P, 2 * Q], F32, "wt_bf%d" % g)
-            nc.scalar.copy(
-                wt_bf[g][:].rearrange("p (a q u) -> p a q u", a=QTILES, u=2),
-                turned[:].rearrange("p a u q -> p a q u"),
+        def sums_end(qt):
+            pass
+
+        def denominators(qt):
+            denom[qt] = tile([P, G], F32, "denom%d" % qt)
+            nc.vector.tensor_scalar(denom[qt][:], total[qt][:], TINY, share_sum[qt][:], ALU.max, ALU.mult)
+
+        def inverses(qt):
+            inverse[qt] = tile([P, G], F32, "inverse%d" % qt)
+            nc.vector.reciprocal(inverse[qt][:], denom[qt][:])
+
+        def factors(qt):
+            factor[qt] = tile([P, G], F32, "factor%d" % qt)
+            nc.vector.tensor_tensor(factor[qt][:], share[qt][:], inverse[qt][:], ALU.mult)
+
+        def weights(qt, g, engine):
+            w_bf[qt, g] = tile([P, PASS // 2], F32, "w_bf%d_%d" % (qt, g))
+            engine.tensor_tensor(
+                w_bf[qt, g][:].bitcast(BF16).rearrange("p (s i) -> p s i", i=RUN),
+                sized[qt, g][:].rearrange("p (s i) -> p s i", i=RUN),
+                factor[qt][:, g * per : (g + 1) * per].unsqueeze(2).to_broadcast([P, per, RUN]),
+                ALU.mult,
             )
 
-        gather_values(1, 0, 0)
-        for g in range(PASSES):
-            quantize_values(0, g)
-        gather_values(1, 1, 1)
-        w_codes, w_scales = {}, {}
-        for g in range(PASSES):
-            w_codes[g] = tile([P, Q], U32, "w_codes%d" % g)
-            w_scales[g] = tile([P, Q], U8, "w_scales%d" % g)
-            nc.vector.quantize_mx(out=w_codes[g][:].bitcast(FP8X4), scales=w_scales[g][:], in_=wt_bf[g][:].bitcast(BF16))
-        for g in range(PASSES):
-            quantize_values(1, g)
+        def turn_weights(qt):
+            turned = bank([P, PASSES, 2, P], 4 + qt, "w_turned%d" % qt)
+            for g in range(PASSES):
+                for u in range(2):
+                    nc.tensor.transpose(turned[:, g, u, :], w_bf[qt, g][:, u : PASS // 2 : 2], ident[:])
+            wt_bf[qt] = tile([P, PASSES, P, 2], F32, "wt_bf%d" % qt)
+            nc.scalar.copy(wt_bf[qt][:], turned[:].rearrange("p g u q -> p g q u"))
+
+        def quantize_weights(qt):
+            w_codes[qt] = tile([P, PASSES * P], U32, "w_codes%d" % qt)
+            w_scales[qt] = tile([P, PASSES * P], U8, "w_scales%d" % qt)
+            nc.vector.quantize_mx(
+                out=w_codes[qt][:].bitcast(FP8X4),
+                scales=w_scales[qt][:],
+                in_=wt_bf[qt][:].rearrange("p g q u -> p (g q u)").bitcast(BF16),
+            )
 
         y = tile([P, PACK, Q], F32, "y")
-        out_rows = out_0.rearrange("(p t) q -> p t q", t=PACK)
-        for pair in range(PAIRS):
-            acc = bank([P, 2, Q], 2 + pair, "acc%d" % pair)
+        y_bf = tile([P, Q, PACK], BF16, "y_bf")
+        for qt in range(QTILES):
+            acc[qt] = bank([P, PACK, P], 2 + qt, "acc%d" % qt)
+
+        def product(pair, qt):
             for h in range(2):
                 for g in range(PASSES):
                     nc.tensor.matmul_mx(
-                        out=acc[:, h, :],
+                        out=acc[qt][:, 2 * pair + h, :],
                         lhsT=v_codes[pair, g][:, h * P : (h + 1) * P].bitcast(FP8X4),
                         lhsT_scale=v_scales[pair, g][:, h * P : (h + 1) * P],
-                        rhs=w_codes[g][:].bitcast(FP8X4),
-                        rhs_scale=w_scales[g][:],
+                        rhs=w_codes[qt][:, g * P : (g + 1) * P].bitcast(FP8X4),
+                        rhs_scale=w_scales[qt][:, g * P : (g + 1) * P],
                         start=(g == 0),
                         stop=(g == PASSES - 1),
                     )
-            nc.scalar.copy(y[:, 2 * pair : 2 * pair + 2, :], acc[:])
-            nc.sync.dma_start(out_rows[:, 2 * pair : 2 * pair + 2, :], y[:, 2 * pair : 2 * pair + 2, :])
 
-        y_bf = tile([P, Q, PACK], BF16, "y_bf")
-        nc.vector.tensor_copy(
-            y_bf[:].rearrange("p (c i) t -> p c t i", i=4), y[:].rearrange("p t (c i) -> p c t i", i=4)
-        )
-        y_codes = tile([P, Q], U32, "y_codes")
-        y_scales = tile([P, Q], U8, "y_scales")
-        nc.vector.quantize_mx(
-            out=y_codes[:].bitcast(FP8X4), scales=y_scales[:], in_=y_bf[:].rearrange("p q t -> p (q t)")
-        )
-        nc.sync.dma_start(out_1[0].rearrange("p q t -> p (q t)").bitcast(I32), y_codes[:].bitcast(I32))
-        for quad in range(4):
-            queue = nc.scalar if quad % 2 == 0 else nc.sync
-            queue.dma_start(
-                out_2[0, 4 * quad : 4 * quad + 4, :].bitcast(I32),
-                y_scales[32 * quad : 32 * quad + 4, :].bitcast(I32),
+        def copy_y(pair, qt):
+            rows = slice(2 * pair, 2 * pair + 2)
+            nc.scalar.copy(y[:, rows, qt * P : (qt + 1) * P], acc[qt][:, rows, :])
+
+        def store_y(pair):
+            rows = slice(2 * pair, 2 * pair + 2)
+            nc.sync.dma_start(out_rows[:, rows, :], y[:, rows, :])
+
+        def planes():
+            y_codes = tile([P, Q], U32, "y_codes")
+            y_scales = tile([P, Q], U8, "y_scales")
+            nc.vector.quantize_mx(
+                out=y_codes[:].bitcast(FP8X4), scales=y_scales[:], in_=y_bf[:].rearrange("p q t -> p (q t)")
             )
+            nc.sync.dma_start(out_1[0].rearrange("p q t -> p (q t)").bitcast(I32), y_codes[:].bitcast(I32))
+            for quad in range(4):
+                queue = nc.scalar if quad % 2 == 0 else nc.sync
+                queue.dma_start(
+                    out_2[0, 4 * quad : 4 * quad + 4, :].bitcast(I32),
+                    y_scales[32 * quad : 32 * quad + 4, :].bitcast(I32),
+                )
+
+        nc.gpsimd.memset(scale_pool[:].bitcast(I32), 0)
+        nc.vector.memset(warm_in[:], 0.0)
+        nc.sync.dma_start(offsets[:], offs)
+        nc.scalar.activation(warm_out[:], warm_in[:], ACT.Exp)
+        make_identity(nc, ident[:])
+        load_size()
+        load_keys()
+        load_scales()
+        load_q()
+        load_vals(0, 0)
+        load_vals(0, 1)
+        load_vals(0, 2)
+        load_vals(0, 3)
+        load_vals(1, 0)
+        load_vals(1, 1)
+        load_vals(1, 2)
+        load_vals(1, 3)
+        spread_size()
+        gather_words(0)
+        gather_words(1)
+        gather_scales(0)
+        quantize_q()
+        gather_scales(1)
+        score(0, 0)
+        score(1, 0)
+        score(0, 1)
+        score(1, 1)
+        cast(0, 0)
+        cast(0, 1)
+        cast(0, 2)
+        cast(0, 3)
+        maxima(0)
+        maxima(1)
+        exps(0)
+        times_size(0)
+        exps(1)
+        times_size(1)
+        sums(0)
+        gather_values(0, 0, 6)
+        sums(1)
+        gather_values(0, 1, 7)
+        sums_end(0)
+        denominators(0)
+        inverses(0)
+        sums_end(1)
+        factors(0)
+        denominators(1)
+        weights(0, 0, nc.gpsimd)
+        inverses(1)
+        weights(0, 1, nc.gpsimd)
+        factors(1)
+        weights(1, 0, nc.vector)
+        weights(1, 1, nc.vector)
+        cast(1, 0)
+        cast(1, 1)
+        cast(1, 2)
+        cast(1, 3)
+        copy_values(0, 0)
+        copy_values(0, 1)
+        gather_values(1, 0, 0)
+        turn_weights(0)
+        quantize_values(0, 0)
+        quantize_values(0, 1)
+        gather_values(1, 1, 1)
+        copy_values(1, 0)
+        turn_weights(1)
+        quantize_weights(0)
+        product(0, 0)
+        quantize_values(1, 0)
+        quantize_weights(1)
+        product(0, 1)
+        copy_values(1, 1)
+        quantize_values(1, 1)
+        copy_y(0, 0)
+        copy_y(0, 1)
+        store_y(0)
+        product(1, 0)
+        product(1, 1)
+        nc.vector.tensor_copy(y_bf[:, 0:P, :], acc[0][:].rearrange("p t q -> p q t"))
+        nc.scalar.copy(y_bf[:, P:Q, :], acc[1][:].rearrange("p t q -> p q t"))
+        copy_y(1, 1)
+        copy_y(1, 0)
+        planes()
+        store_y(1)

@@ -57,7 +57,7 @@ def tile_attend_docmix_pl_kernel(tc, query, keys_words, keys_scales, size, vals,
         v_codes, v_scales, v_bf, v_turned = {}, {}, {}, {}
         best, neg_top, probs, share_sum, share, total, factor, denom, inverse = {}, {}, {}, {}, {}, {}, {}, {}, {}
         sized, w_bf, wt_bf, w_codes, w_scales, acc, back = {}, {}, {}, {}, {}, {}, {}
-        tags = {"probs0_0": "v_raw0_2", "probs0_1": "v_raw0_3"}
+        tags = {"key_words1": "q_raw", "picked1_0": "sized0", "picked1_1": "inverse1", "window1": "neg_all"}
 
         def load_vals(pair, c):
             v_raw[pair, c] = tile([P, 2, CHUNK], F32, "v_raw%d_%d" % (pair, c))
@@ -80,12 +80,13 @@ def tile_attend_docmix_pl_kernel(tc, query, keys_words, keys_scales, size, vals,
                 )
 
         def gather_words(g):
-            key_words[g] = tile([P, PASS], U16, "key_words%d" % g)
+            key_words[g] = tile([P, PASS], U16, "key_words%d" % g, tags.get("key_words%d" % g))
             nc.vector.tensor_copy(key_words[g][:], key_pool[:].indirect(offsets[:, g * cols : (g + 1) * cols]))
 
-        def gather_scales(g):
-            key_scales[g] = tile([P, PASS], U8, "key_scales%d" % g)
-            nc.vector.tensor_copy(key_scales[g][:], scale_pool[:].indirect(offsets[:, g * cols : (g + 1) * cols]))
+        key_scales = tile([P, I], U8, "key_scales")
+
+        def gather_scales():
+            nc.vector.tensor_copy(key_scales[:], scale_pool[:].indirect(offsets[:]))
 
         q_bf = tile([P, Q, PACK], BF16, "q_bf")
         q_codes = tile([P, Q], U32, "q_codes")
@@ -99,16 +100,14 @@ def tile_attend_docmix_pl_kernel(tc, query, keys_words, keys_scales, size, vals,
                 out=q_codes[:].bitcast(FP8X4), scales=q_scales[:], in_=q_bf[:].rearrange("p q j -> p (q j)")
             )
 
-        size_all = tile([P, P, I // P], F32, "size_all")
-        size_row = size_all[:].rearrange("p r c -> p (r c)")
+        spread = {}
 
         def spread_size():
             for half in range(2):
-                spread = bank([P, 4, P], 4 + half, "spread%d" % half)
+                spread[half] = bank([P, 4, P], 4 + half, "spread%d" % half)
                 for c in range(4):
                     col = 4 * half + c
-                    nc.tensor.transpose(spread[:, c, :], size_cols[:, col : col + 1].to_broadcast([P, P]), ident[:])
-                nc.scalar.copy(size_all[:, :, 4 * half : 4 * half + 4], spread[:].rearrange("p c r -> p r c"))
+                    nc.tensor.transpose(spread[half][:, c, :], size_cols[:, col : col + 1].to_broadcast([P, P]), ident[:])
 
         def score(qt, g):
             scores[qt, g] = bank([P, PASS], 2 * qt + g, "scores%d_%d" % (qt, g))
@@ -117,15 +116,15 @@ def tile_attend_docmix_pl_kernel(tc, query, keys_words, keys_scales, size, vals,
                 lhsT=q_codes[:, qt * P : (qt + 1) * P].bitcast(FP8X4),
                 lhsT_scale=q_scales[:, qt * P : (qt + 1) * P],
                 rhs=key_words[g][:].bitcast(FP4X4),
-                rhs_scale=key_scales[g][:],
+                rhs_scale=key_scales[:, g * PASS : (g + 1) * PASS],
                 start=True,
                 stop=True,
             )
 
-        for pair in range(PAIRS):
-            windows[pair] = tile([P, T], F32, "window%d" % pair)
 
         def cast(pair, c, engine="scalar"):
+            if c == 0:
+                windows[pair] = tile([P, T], F32, "window%d" % pair, tags.get("window%d" % pair))
             dst = windows[pair][:, c * CHUNK : (c + 1) * CHUNK].bitcast(BF16).rearrange("p (m h j) -> p m h j", h=2, j=PACK)
             src = v_raw[pair, c][:].rearrange("p h (m j) -> p m h j", j=PACK)
             if engine == "scalar":
@@ -156,44 +155,73 @@ def tile_attend_docmix_pl_kernel(tc, query, keys_words, keys_scales, size, vals,
                 out=v_codes[pair, g][:].bitcast(FP8X4), scales=v_scales[pair, g][:], in_=v_bf[pair, g][:].bitcast(BF16)
             )
 
-        def maxima(qt):
-            best[qt] = tile([P, G], F32, "best%d" % qt)
-            for g in range(PASSES):
-                nc.vector.tensor_reduce(
-                    best[qt][:, g * per : (g + 1) * per],
-                    scores[qt, g][:].rearrange("p (s i) -> p s i", i=RUN),
-                    AXIS_X,
-                    ALU.max,
-                )
-            neg_top[qt] = tile([P, 1], F32, "neg_top%d" % qt)
-            nc.vector.tensor_reduce(neg_top[qt][:], best[qt][:], AXIS_X, ALU.max, negate=True)
+        best_all = tile([P, QTILES, G], F32, "best_all")
+
+        def maxima(qt, g):
+            nc.vector.tensor_reduce(
+                best_all[:, qt, g * per : (g + 1) * per],
+                scores[qt, g][:].rearrange("p (s i) -> p s i", i=RUN),
+                AXIS_X,
+                ALU.max,
+            )
+
+        def tops():
+            neg_all = tile([P, QTILES], F32, "neg_all", tags.get("neg_all"))
+            nc.vector.tensor_reduce(neg_all[:], best_all[:], AXIS_X, ALU.max, negate=True)
+            for qt in range(QTILES):
+                neg_top[qt] = neg_all[:, qt : qt + 1]
+                best[qt] = best_all[:, qt, :]
+
+        probs_all = []
 
         def exps(qt):
+            if qt == 0:
+                probs_all.append(tile([P, QTILES * I], F32, "probs_all", "v_raw0_3"))
             for g in range(PASSES):
-                name = "probs%d_%d" % (qt, g)
-                probs[qt, g] = tile([P, PASS], F32, name, tags.get(name))
-                nc.scalar.activation(probs[qt, g][:], scores[qt, g][:], ACT.Exp, bias=neg_top[qt][:])
+                probs[qt] = probs_all[0][:, qt * I : (qt + 1) * I]
+                nc.scalar.activation(
+                    probs[qt].rearrange("p (a g s b) -> p a g s b", a=4, g=PASSES, b=4)[:, :, g, :, :],
+                    scores[qt, g][:].rearrange("p (s a b) -> p a s b", a=4, b=4),
+                    ACT.Exp,
+                    bias=neg_top[qt],
+                )
             share[qt] = tile([P, G], F32, "share%d" % qt)
             share_sum[qt] = tile([P, 1], F32, "share_sum%d" % qt)
-            nc.scalar.activation(share[qt][:], best[qt][:], ACT.Exp, bias=neg_top[qt][:], accum_out=share_sum[qt][:])
+            nc.scalar.activation(share[qt][:], best[qt], ACT.Exp, bias=neg_top[qt], accum_out=share_sum[qt][:])
 
         def times_size(qt):
-            for g in range(PASSES):
-                sized[qt, g] = tile([P, PASS], F32, "sized%d_%d" % (qt, g))
-                nc.gpsimd.tensor_tensor(sized[qt, g][:], probs[qt, g][:], size_row[:, g * PASS : (g + 1) * PASS], ALU.mult)
+            sized[qt] = tile([P, I], F32, "sized%d" % qt)
+            for half in range(2):
+                nc.vector.tensor_tensor(
+                    sized[qt][:].rearrange("p (a h s b) -> p a h s b", a=2, h=2, b=4)[:, :, half, :, :],
+                    probs[qt].rearrange("p (a h s b) -> p a h s b", a=2, h=2, b=4)[:, :, half, :, :],
+                    spread[half][:].rearrange("p b (s a) -> p a s b", a=2),
+                    ALU.mult,
+                )
 
         def sums(qt):
             total[qt] = tile([P, G], F32, "total%d" % qt)
+            partial = bank([P, PASSES, P], qt, "partial%d" % qt)
             for g in range(PASSES):
-                nc.vector.tensor_reduce(
-                    total[qt][:, g * per : (g + 1) * per],
-                    probs[qt, g][:].rearrange("p (s i) -> p s i", i=RUN),
-                    AXIS_X,
-                    ALU.add,
-                )
+                for a in range(4):
+                    nc.tensor.matmul(
+                        out=partial[:, g, :],
+                        lhsT=probs[qt][:, (PASSES * a + g) * P : (PASSES * a + g + 1) * P],
+                        rhs=ident[:],
+                        start=(a == 0),
+                        stop=(a == 3),
+                        is_transpose=True,
+                    )
+            partial_sb = tile([P, PASSES, P], F32, "partial_sb%d" % qt)
+            nc.scalar.copy(partial_sb[:], partial[:])
+            back[qt] = bank([P, PASSES, P], qt, "back%d" % qt)
+            for g in range(PASSES):
+                nc.tensor.transpose(back[qt][:, g, :], partial_sb[:, g, :], ident[:])
 
         def sums_end(qt):
-            pass
+            nc.vector.tensor_reduce(
+                total[qt][:], back[qt][:].rearrange("p g (s b) -> p (g s) b", b=4), AXIS_X, ALU.add
+            )
 
         def denominators(qt):
             denom[qt] = tile([P, G], F32, "denom%d" % qt)
@@ -207,12 +235,12 @@ def tile_attend_docmix_pl_kernel(tc, query, keys_words, keys_scales, size, vals,
             factor[qt] = tile([P, G], F32, "factor%d" % qt)
             nc.vector.tensor_tensor(factor[qt][:], share[qt][:], inverse[qt][:], ALU.mult)
 
-        def weights(qt, g, engine):
-            w_bf[qt, g] = tile([P, PASS // 2], F32, "w_bf%d_%d" % (qt, g))
-            engine.tensor_tensor(
-                w_bf[qt, g][:].bitcast(BF16).rearrange("p (s i) -> p s i", i=RUN),
-                sized[qt, g][:].rearrange("p (s i) -> p s i", i=RUN),
-                factor[qt][:, g * per : (g + 1) * per].unsqueeze(2).to_broadcast([P, per, RUN]),
+        def weights(qt):
+            w_bf[qt] = tile([P, I // 2], F32, "w_bf%d" % qt)
+            nc.vector.tensor_tensor(
+                w_bf[qt][:].bitcast(BF16).rearrange("p (s a b) -> p s a b", a=4, b=4),
+                sized[qt][:].rearrange("p (a s b) -> p s a b", a=4, b=4),
+                factor[qt][:].unsqueeze(2).unsqueeze(3).to_broadcast([P, G, 4, 4]),
                 ALU.mult,
             )
 
@@ -220,7 +248,7 @@ def tile_attend_docmix_pl_kernel(tc, query, keys_words, keys_scales, size, vals,
             turned = bank([P, PASSES, 2, P], 4 + qt, "w_turned%d" % qt)
             for g in range(PASSES):
                 for u in range(2):
-                    nc.tensor.transpose(turned[:, g, u, :], w_bf[qt, g][:, u : PASS // 2 : 2], ident[:])
+                    nc.tensor.transpose(turned[:, g, u, :], w_bf[qt][:, g * PASS // 2 + u : (g + 1) * PASS // 2 : 2], ident[:])
             wt_bf[qt] = tile([P, PASSES, P, 2], F32, "wt_bf%d" % qt)
             nc.scalar.copy(wt_bf[qt][:], turned[:].rearrange("p g u q -> p g q u"))
 
@@ -235,14 +263,13 @@ def tile_attend_docmix_pl_kernel(tc, query, keys_words, keys_scales, size, vals,
 
         y = tile([P, PACK, Q], F32, "y")
         y_bf = tile([P, Q, PACK], BF16, "y_bf")
-        for qt in range(QTILES):
-            acc[qt] = bank([P, PACK, P], 2 + qt, "acc%d" % qt)
 
         def product(pair, qt):
+            acc[pair, qt] = bank([P, 2, P], 6 - 2 * pair + qt, "acc%d_%d" % (pair, qt))
             for h in range(2):
                 for g in range(PASSES):
                     nc.tensor.matmul_mx(
-                        out=acc[qt][:, 2 * pair + h, :],
+                        out=acc[pair, qt][:, h, :],
                         lhsT=v_codes[pair, g][:, h * P : (h + 1) * P].bitcast(FP8X4),
                         lhsT_scale=v_scales[pair, g][:, h * P : (h + 1) * P],
                         rhs=w_codes[qt][:, g * P : (g + 1) * P].bitcast(FP8X4),
@@ -253,11 +280,16 @@ def tile_attend_docmix_pl_kernel(tc, query, keys_words, keys_scales, size, vals,
 
         def copy_y(pair, qt):
             rows = slice(2 * pair, 2 * pair + 2)
-            nc.scalar.copy(y[:, rows, qt * P : (qt + 1) * P], acc[qt][:, rows, :])
+            nc.scalar.copy(y[:, rows, qt * P : (qt + 1) * P], acc[pair, qt][:])
 
         def store_y(pair):
             rows = slice(2 * pair, 2 * pair + 2)
             nc.sync.dma_start(out_rows[:, rows, :], y[:, rows, :])
+
+        def store_half(qt):
+            half = tile([P, PACK, P], F32, "y%d" % qt)
+            nc.scalar.copy(half[:], acc[qt][:])
+            nc.sync.dma_start(out_rows[:, :, qt * P : (qt + 1) * P], half[:])
 
         def planes():
             y_codes = tile([P, Q], U32, "y_codes")
@@ -279,8 +311,8 @@ def tile_attend_docmix_pl_kernel(tc, query, keys_words, keys_scales, size, vals,
         nc.scalar.activation(warm_out[:], warm_in[:], ACT.Exp)
         make_identity(nc, ident[:])
         load_size()
-        load_keys()
         load_scales()
+        load_keys()
         load_q()
         load_vals(0, 0)
         load_vals(0, 1)
@@ -291,11 +323,10 @@ def tile_attend_docmix_pl_kernel(tc, query, keys_words, keys_scales, size, vals,
         load_vals(1, 2)
         load_vals(1, 3)
         spread_size()
+        gather_scales()
         gather_words(0)
-        gather_words(1)
-        gather_scales(0)
         quantize_q()
-        gather_scales(1)
+        gather_words(1)
         score(0, 0)
         score(1, 0)
         score(0, 1)
@@ -304,56 +335,57 @@ def tile_attend_docmix_pl_kernel(tc, query, keys_words, keys_scales, size, vals,
         cast(0, 1)
         cast(0, 2)
         cast(0, 3)
-        maxima(0)
-        maxima(1)
+        maxima(0, 0)
+        maxima(1, 0)
+        maxima(0, 1)
+        maxima(1, 1)
+        tops()
         exps(0)
-        times_size(0)
         exps(1)
-        times_size(1)
         sums(0)
-        gather_values(0, 0, 6)
         sums(1)
-        gather_values(0, 1, 7)
         sums_end(0)
         denominators(0)
         inverses(0)
-        sums_end(1)
         factors(0)
+        sums_end(1)
         denominators(1)
-        weights(0, 0, nc.gpsimd)
         inverses(1)
-        weights(0, 1, nc.gpsimd)
         factors(1)
-        weights(1, 0, nc.vector)
-        weights(1, 1, nc.vector)
+        gather_values(0, 0, 2)
+        gather_values(0, 1, 3)
+        times_size(0)
+        times_size(1)
+        weights(0)
+        weights(1)
         cast(1, 0)
         cast(1, 1)
         cast(1, 2)
         cast(1, 3)
         copy_values(0, 0)
         copy_values(0, 1)
-        gather_values(1, 0, 0)
         turn_weights(0)
+        gather_values(1, 0, 2)
+        turn_weights(1)
+        gather_values(1, 1, 3)
+        copy_values(1, 0)
         quantize_values(0, 0)
         quantize_values(0, 1)
-        gather_values(1, 1, 1)
-        copy_values(1, 0)
-        turn_weights(1)
         quantize_weights(0)
-        product(0, 0)
-        quantize_values(1, 0)
         quantize_weights(1)
-        product(0, 1)
         copy_values(1, 1)
+        quantize_values(1, 0)
         quantize_values(1, 1)
+        product(0, 0)
+        product(0, 1)
         copy_y(0, 0)
         copy_y(0, 1)
         store_y(0)
         product(1, 0)
         product(1, 1)
-        nc.vector.tensor_copy(y_bf[:, 0:P, :], acc[0][:].rearrange("p t q -> p q t"))
-        nc.scalar.copy(y_bf[:, P:Q, :], acc[1][:].rearrange("p t q -> p q t"))
-        copy_y(1, 1)
         copy_y(1, 0)
-        planes()
+        copy_y(1, 1)
         store_y(1)
+        nc.vector.tensor_copy(y_bf[:, 0:P, :].rearrange("p (c i) t -> p c t i", i=4), y[:, :, 0:P].rearrange("p t (c i) -> p c t i", i=4))
+        nc.vector.tensor_copy(y_bf[:, P:Q, :].rearrange("p (c i) t -> p c t i", i=4), y[:, :, P:Q].rearrange("p t (c i) -> p c t i", i=4))
+        planes()

@@ -46,8 +46,6 @@ def tile_attend_docmix_pl_kernel(tc, query, keys_words, keys_scales, size, vals,
         offsets = sb.tile([P, I // 16], U16, name="offsets")
         key_pool = tile([P, T], U16, "key_pool")
         scale_pool = tile([P, T], U8, "scale_pool")
-        warm_in = tile([P, 1], F32, "warm_in")
-        warm_out = tile([P, 1], F32, "warm_out")
         size_cols = tile([P, I // P], F32, "size_cols")
         q_raw = tile([P, PACK, Q], F32, "q_raw")
         ident = tile([P, P], F32, "ident")
@@ -306,9 +304,7 @@ def tile_attend_docmix_pl_kernel(tc, query, keys_words, keys_scales, size, vals,
                 )
 
         nc.gpsimd.memset(scale_pool[:].bitcast(I32), 0)
-        nc.vector.memset(warm_in[:], 0.0)
         nc.sync.dma_start(offsets[:], offs)
-        nc.scalar.activation(warm_out[:], warm_in[:], ACT.Exp)
         make_identity(nc, ident[:])
         load_size()
         load_scales()

@@ -26,6 +26,7 @@ PASSES = I // PASS
 QTILES = Q // P
 PAIRS = 2
 CHUNK = 512
+CHUNKS = T // CHUNK
 TINY = 1e-30
 
 
@@ -46,69 +47,33 @@ def tile_attend_docmix_pl_kernel(tc, query, keys_words, keys_scales, size, vals,
         offsets = sb.tile([P, I // 16], U16, name="offsets")
         key_pool = tile([P, T], U16, "key_pool")
         scale_pool = tile([P, T], U8, "scale_pool")
-        size_cols = tile([P, I // P], F32, "size_cols")
+        size_cols = tile([P, PASSES, PACK], F32, "size_cols")
         q_raw = tile([P, PACK, Q], F32, "q_raw")
         ident = tile([P, P], F32, "ident")
         vals_rows = vals.rearrange("(p t) n -> p t n", t=PACK)
         out_rows = out_0.rearrange("(p t) q -> p t q", t=PACK)
-        v_raw, windows, key_words, key_scales, scores = {}, {}, {}, {}, {}
-        v_codes, v_scales, v_bf, v_turned = {}, {}, {}, {}
-        best, neg_top, probs, share_sum, share, total, factor, denom, inverse = {}, {}, {}, {}, {}, {}, {}, {}, {}
-        sized, w_bf, wt_bf, w_codes, w_scales, acc, back = {}, {}, {}, {}, {}, {}, {}
-        tags = {"key_words1": "q_raw", "picked1_0": "sized0", "picked1_1": "inverse1", "window1": "neg_all"}
+        v_raw, windows, key_words, scores, neg_top, probs = {}, {}, {}, {}, {}, {}
+        picked, v_turned, v_bf, v_codes, v_scales = {}, {}, {}, {}, {}
+        p_turned, sized, w_bf, w_codes, w_scales, acc, y, y_bf = {}, {}, {}, {}, {}, {}, {}, {}
 
         def load_vals(pair, c):
             v_raw[pair, c] = tile([P, 2, CHUNK], F32, "v_raw%d_%d" % (pair, c))
             nc.sync.dma_start(v_raw[pair, c][:], vals_rows[:, 2 * pair : 2 * pair + 2, c * CHUNK : (c + 1) * CHUNK])
 
-        def load_q():
-            nc.sync.dma_start(q_raw[:], query.rearrange("(p j) q -> p j q", j=PACK))
+        def cast(pair, c, on_vector):
+            dst = windows[pair][:, c * CHUNK : (c + 1) * CHUNK].bitcast(BF16).rearrange("p (m h j) -> p m h j", h=2, j=PACK)
+            src = v_raw[pair, c][:].rearrange("p h (m j) -> p m h j", j=PACK)
+            if on_vector:
+                nc.vector.tensor_copy(dst, src)
+            else:
+                nc.scalar.activation(dst, src, ACT.Copy)
 
-        def load_size():
-            nc.sync.dma_start(size_cols[:], size.rearrange("o (p c) -> (o p) c", p=P))
-
-        def load_keys():
-            nc.sync.dma_start(key_pool[:].bitcast(I32), keys_words[0].bitcast(I32))
-
-        def load_scales():
-            for quad in range(4):
-                nc.sync.dma_start(
-                    scale_pool[32 * quad : 32 * quad + 4, :].bitcast(I32),
-                    keys_scales[0, 4 * quad : 4 * quad + 4, :].bitcast(I32),
-                )
-
-        def gather_words(g):
-            key_words[g] = tile([P, PASS], U16, "key_words%d" % g, tags.get("key_words%d" % g))
+        def gather_words(g, tag):
+            key_words[g] = tile([P, PASS], U16, "key_words%d" % g, tag)
             nc.vector.tensor_copy(key_words[g][:], key_pool[:].indirect(offsets[:, g * cols : (g + 1) * cols]))
 
-        key_scales = tile([P, I], U8, "key_scales")
-
-        def gather_scales():
-            nc.vector.tensor_copy(key_scales[:], scale_pool[:].indirect(offsets[:]))
-
-        q_bf = tile([P, Q, PACK], BF16, "q_bf")
-        q_codes = tile([P, Q], U32, "q_codes")
-        q_scales = tile([P, Q], U8, "q_scales")
-
-        def quantize_q():
-            nc.scalar.copy(
-                q_bf[:].rearrange("p (c i) j -> p c j i", i=4), q_raw[:].rearrange("p j (c i) -> p c j i", i=4)
-            )
-            nc.vector.quantize_mx(
-                out=q_codes[:].bitcast(FP8X4), scales=q_scales[:], in_=q_bf[:].rearrange("p q j -> p (q j)")
-            )
-
-        spread = {}
-
-        def spread_size():
-            for half in range(2):
-                spread[half] = bank([P, 4, P], 4 + half, "spread%d" % half)
-                for c in range(4):
-                    col = 4 * half + c
-                    nc.tensor.transpose(spread[half][:, c, :], size_cols[:, col : col + 1].to_broadcast([P, P]), ident[:])
-
         def score(qt, g):
-            scores[qt, g] = bank([P, PASS], 2 * qt + g, "scores%d_%d" % (qt, g))
+            scores[qt, g] = bank([P, PASS], 2 * g + qt, "scores%d_%d" % (qt, g))
             nc.tensor.matmul_mx(
                 out=scores[qt, g][:],
                 lhsT=q_codes[:, qt * P : (qt + 1) * P].bitcast(FP8X4),
@@ -119,28 +84,60 @@ def tile_attend_docmix_pl_kernel(tc, query, keys_words, keys_scales, size, vals,
                 stop=True,
             )
 
+        def maxima(qt, g):
+            nc.vector.tensor_reduce(
+                best[:, qt, g * per : (g + 1) * per],
+                scores[qt, g][:].rearrange("p (s i) -> p s i", i=RUN),
+                AXIS_X,
+                ALU.max,
+            )
 
-        def cast(pair, c, engine="scalar"):
-            if c == 0:
-                windows[pair] = tile([P, T], F32, "window%d" % pair, tags.get("window%d" % pair))
-            dst = windows[pair][:, c * CHUNK : (c + 1) * CHUNK].bitcast(BF16).rearrange("p (m h j) -> p m h j", h=2, j=PACK)
-            src = v_raw[pair, c][:].rearrange("p h (m j) -> p m h j", j=PACK)
-            if engine == "scalar":
-                nc.scalar.activation(dst, src, ACT.Copy)
-            else:
-                nc.vector.tensor_copy(dst, src)
+        def top(g):
+            neg_top[g] = tile([P, QTILES], F32, "neg_top%d" % g)
+            nc.vector.tensor_reduce(neg_top[g][:], best[:, :, g * per : (g + 1) * per], AXIS_X, ALU.max, negate=True)
 
-        def gather_values(pair, g, number):
-            name = "picked%d_%d" % (pair, g)
-            picked = tile([P, PASS], F32, name, tags.get(name))
-            nc.vector.tensor_copy(picked[:], windows[pair][:].indirect(offsets[:, g * cols : (g + 1) * cols]))
+        def exps(qt, g):
+            probs[qt, g] = tile([P, PACK, P], F32, "probs%d_%d" % (qt, g))
+            nc.scalar.activation(
+                probs[qt, g][:],
+                scores[qt, g][:].rearrange("q (p t) -> q t p", t=PACK),
+                ACT.Exp,
+                bias=neg_top[g][:, qt : qt + 1],
+            )
+
+        def quarter_sums(qt, g):
+            for t in range(PACK):
+                nc.tensor.matmul(
+                    out=partial[:, qt, g, :],
+                    lhsT=probs[qt, g][:, t, :],
+                    rhs=ident[:],
+                    start=(t == 0),
+                    stop=(t == PACK - 1),
+                    is_transpose=True,
+                )
+
+        def turn_probs(g, half):
+            p_turned[g, half] = bank([P, 2, Q], (4, 5, 0, 1)[2 * g + half], "p_turned%d_%d" % (g, half))
+            for qt in range(QTILES):
+                for u in range(2):
+                    nc.tensor.transpose(p_turned[g, half][:, u, qt * P : (qt + 1) * P], probs[qt, g][:, 2 * half + u, :], ident[:])
+
+        def times_size(g, t):
+            nc.scalar.activation(
+                sized[g][:, t, :], p_turned[g, t // 2][:, t % 2, :], ACT.Copy, scale=size_cols[:, g, t : t + 1]
+            )
+
+        def gather_values(pair, g, tag):
+            picked[pair, g] = tile([P, PASS], F32, "picked%d_%d" % (pair, g), tag)
+            nc.vector.tensor_copy(picked[pair, g][:], windows[pair][:].indirect(offsets[:, g * cols : (g + 1) * cols]))
+
+        def turn_values(pair, g, number):
             v_turned[pair, g] = bank([P, 4, P], number, "v_turned%d_%d" % (pair, g))
             for c in range(4):
-                nc.tensor.transpose(v_turned[pair, g][:, c, :], picked[:, c:PASS:4], ident[:])
+                nc.tensor.transpose(v_turned[pair, g][:, c, :], picked[pair, g][:, c:PASS:4], ident[:])
 
         def copy_values(pair, g):
-            name = "v_bf%d_%d" % (pair, g)
-            v_bf[pair, g] = tile([P, PASS], F32, name, tags.get(name))
+            v_bf[pair, g] = tile([P, PASS], F32, "v_bf%d_%d" % (pair, g))
             nc.scalar.copy(
                 v_bf[pair, g][:].rearrange("p (h e u) -> p h e u", h=2, u=2),
                 v_turned[pair, g][:].rearrange("p (h u) e -> p h e u", u=2),
@@ -153,235 +150,211 @@ def tile_attend_docmix_pl_kernel(tc, query, keys_words, keys_scales, size, vals,
                 out=v_codes[pair, g][:].bitcast(FP8X4), scales=v_scales[pair, g][:], in_=v_bf[pair, g][:].bitcast(BF16)
             )
 
-        best_all = tile([P, QTILES, G], F32, "best_all")
-
-        def maxima(qt, g):
-            nc.vector.tensor_reduce(
-                best_all[:, qt, g * per : (g + 1) * per],
-                scores[qt, g][:].rearrange("p (s i) -> p s i", i=RUN),
-                AXIS_X,
-                ALU.max,
-            )
-
-        def tops():
-            neg_all = tile([P, QTILES], F32, "neg_all", tags.get("neg_all"))
-            nc.vector.tensor_reduce(neg_all[:], best_all[:], AXIS_X, ALU.max, negate=True)
-            for qt in range(QTILES):
-                neg_top[qt] = neg_all[:, qt : qt + 1]
-                best[qt] = best_all[:, qt, :]
-
-        probs_all = []
-
-        def exps(qt):
-            if qt == 0:
-                probs_all.append(tile([P, QTILES * I], F32, "probs_all", "v_raw0_3"))
-            for g in range(PASSES):
-                probs[qt] = probs_all[0][:, qt * I : (qt + 1) * I]
-                nc.scalar.activation(
-                    probs[qt].rearrange("p (a g s b) -> p a g s b", a=4, g=PASSES, b=4)[:, :, g, :, :],
-                    scores[qt, g][:].rearrange("p (s a b) -> p a s b", a=4, b=4),
-                    ACT.Exp,
-                    bias=neg_top[qt],
-                )
-            share[qt] = tile([P, G], F32, "share%d" % qt)
-            share_sum[qt] = tile([P, 1], F32, "share_sum%d" % qt)
-            nc.scalar.activation(share[qt][:], best[qt], ACT.Exp, bias=neg_top[qt], accum_out=share_sum[qt][:])
-
-        def times_size(qt):
-            sized[qt] = tile([P, I], F32, "sized%d" % qt)
-            for half in range(2):
-                nc.vector.tensor_tensor(
-                    sized[qt][:].rearrange("p (a h s b) -> p a h s b", a=2, h=2, b=4)[:, :, half, :, :],
-                    probs[qt].rearrange("p (a h s b) -> p a h s b", a=2, h=2, b=4)[:, :, half, :, :],
-                    spread[half][:].rearrange("p b (s a) -> p a s b", a=2),
-                    ALU.mult,
-                )
-
-        def sums(qt):
-            total[qt] = tile([P, G], F32, "total%d" % qt)
-            partial = bank([P, PASSES, P], qt, "partial%d" % qt)
-            for g in range(PASSES):
-                for a in range(4):
-                    nc.tensor.matmul(
-                        out=partial[:, g, :],
-                        lhsT=probs[qt][:, (PASSES * a + g) * P : (PASSES * a + g + 1) * P],
-                        rhs=ident[:],
-                        start=(a == 0),
-                        stop=(a == 3),
-                        is_transpose=True,
-                    )
-            partial_sb = tile([P, PASSES, P], F32, "partial_sb%d" % qt)
-            nc.scalar.copy(partial_sb[:], partial[:])
-            back[qt] = bank([P, PASSES, P], qt, "back%d" % qt)
-            for g in range(PASSES):
-                nc.tensor.transpose(back[qt][:, g, :], partial_sb[:, g, :], ident[:])
-
-        def sums_end(qt):
-            nc.vector.tensor_reduce(
-                total[qt][:], back[qt][:].rearrange("p g (s b) -> p (g s) b", b=4), AXIS_X, ALU.add
-            )
-
-        def denominators(qt):
-            denom[qt] = tile([P, G], F32, "denom%d" % qt)
-            nc.vector.tensor_scalar(denom[qt][:], total[qt][:], TINY, share_sum[qt][:], ALU.max, ALU.mult)
-
-        def inverses(qt):
-            inverse[qt] = tile([P, G], F32, "inverse%d" % qt)
-            nc.vector.reciprocal(inverse[qt][:], denom[qt][:])
-
-        def factors(qt):
-            factor[qt] = tile([P, G], F32, "factor%d" % qt)
-            nc.vector.tensor_tensor(factor[qt][:], share[qt][:], inverse[qt][:], ALU.mult)
-
-        def weights(qt):
-            w_bf[qt] = tile([P, I // 2], F32, "w_bf%d" % qt)
+        def weights(g, first, last):
+            name = "%d_%d" % (g, first)
+            width = (last - first) * P
+            span = slice(first * P, last * P)
+            rounded = tile([P, width, PACK], BF16, "w_bf" + name)
             nc.vector.tensor_tensor(
-                w_bf[qt][:].bitcast(BF16).rearrange("p (s a b) -> p s a b", a=4, b=4),
-                sized[qt][:].rearrange("p (a s b) -> p s a b", a=4, b=4),
-                factor[qt][:].unsqueeze(2).unsqueeze(3).to_broadcast([P, G, 4, 4]),
+                rounded[:].rearrange("p (c i) t -> p c t i", i=2),
+                sized[g][:, :, span].rearrange("p t (c i) -> p c t i", i=2),
+                f_turned[:, g, span].rearrange("p (c i) -> p c i", i=2).unsqueeze(2).to_broadcast([P, width // 2, PACK, 2]),
                 ALU.mult,
             )
+            w_bf[g, first] = rounded
 
-        def turn_weights(qt):
-            turned = bank([P, PASSES, 2, P], 4 + qt, "w_turned%d" % qt)
-            for g in range(PASSES):
-                for u in range(2):
-                    nc.tensor.transpose(turned[:, g, u, :], w_bf[qt][:, g * PASS // 2 + u : (g + 1) * PASS // 2 : 2], ident[:])
-            wt_bf[qt] = tile([P, PASSES, P, 2], F32, "wt_bf%d" % qt)
-            nc.scalar.copy(wt_bf[qt][:], turned[:].rearrange("p g u q -> p g q u"))
-
-        def quantize_weights(qt):
-            w_codes[qt] = tile([P, PASSES * P], U32, "w_codes%d" % qt)
-            w_scales[qt] = tile([P, PASSES * P], U8, "w_scales%d" % qt)
+        def quantize_weights(g, first, last):
+            name = "%d_%d" % (g, first)
+            width = (last - first) * P
+            codes = tile([P, width], U32, "w_codes" + name)
+            scales = tile([P, width], U8, "w_scales" + name)
             nc.vector.quantize_mx(
-                out=w_codes[qt][:].bitcast(FP8X4),
-                scales=w_scales[qt][:],
-                in_=wt_bf[qt][:].rearrange("p g q u -> p (g q u)").bitcast(BF16),
+                out=codes[:].bitcast(FP8X4), scales=scales[:], in_=w_bf[g, first][:].rearrange("p q t -> p (q t)")
             )
+            for qt in range(first, last):
+                w_codes[g, qt] = codes[:, (qt - first) * P : (qt - first + 1) * P]
+                w_scales[g, qt] = scales[:, (qt - first) * P : (qt - first + 1) * P]
 
-        y = tile([P, PACK, Q], F32, "y")
-        y_bf = tile([P, Q, PACK], BF16, "y_bf")
-
-        def product(pair, qt):
-            acc[pair, qt] = bank([P, 2, P], 6 - 2 * pair + qt, "acc%d_%d" % (pair, qt))
+        def product(qt, pair, g):
+            if g == 0:
+                acc[qt, pair] = bank([P, 2, P], (4, 5, 0, 1)[2 * qt + pair], "acc%d_%d" % (qt, pair))
             for h in range(2):
-                for g in range(PASSES):
-                    nc.tensor.matmul_mx(
-                        out=acc[pair, qt][:, h, :],
-                        lhsT=v_codes[pair, g][:, h * P : (h + 1) * P].bitcast(FP8X4),
-                        lhsT_scale=v_scales[pair, g][:, h * P : (h + 1) * P],
-                        rhs=w_codes[qt][:, g * P : (g + 1) * P].bitcast(FP8X4),
-                        rhs_scale=w_scales[qt][:, g * P : (g + 1) * P],
-                        start=(g == 0),
-                        stop=(g == PASSES - 1),
-                    )
-
-        def copy_y(pair, qt):
-            rows = slice(2 * pair, 2 * pair + 2)
-            nc.scalar.copy(y[:, rows, qt * P : (qt + 1) * P], acc[pair, qt][:])
-
-        def store_y(pair):
-            rows = slice(2 * pair, 2 * pair + 2)
-            nc.sync.dma_start(out_rows[:, rows, :], y[:, rows, :])
-
-        def store_half(qt):
-            half = tile([P, PACK, P], F32, "y%d" % qt)
-            nc.scalar.copy(half[:], acc[qt][:])
-            nc.sync.dma_start(out_rows[:, :, qt * P : (qt + 1) * P], half[:])
-
-        def planes():
-            y_codes = tile([P, Q], U32, "y_codes")
-            y_scales = tile([P, Q], U8, "y_scales")
-            nc.vector.quantize_mx(
-                out=y_codes[:].bitcast(FP8X4), scales=y_scales[:], in_=y_bf[:].rearrange("p q t -> p (q t)")
-            )
-            nc.sync.dma_start(out_1[0].rearrange("p q t -> p (q t)").bitcast(I32), y_codes[:].bitcast(I32))
-            for quad in range(4):
-                queue = nc.scalar if quad % 2 == 0 else nc.sync
-                queue.dma_start(
-                    out_2[0, 4 * quad : 4 * quad + 4, :].bitcast(I32),
-                    y_scales[32 * quad : 32 * quad + 4, :].bitcast(I32),
+                nc.tensor.matmul_mx(
+                    out=acc[qt, pair][:, h, :],
+                    lhsT=v_codes[pair, g][:, h * P : (h + 1) * P].bitcast(FP8X4),
+                    lhsT_scale=v_scales[pair, g][:, h * P : (h + 1) * P],
+                    rhs=w_codes[g, qt].bitcast(FP8X4),
+                    rhs_scale=w_scales[g, qt],
+                    start=(g == 0 and h == 0),
+                    stop=(g == PASSES - 1 and h == 1),
                 )
 
-        nc.gpsimd.memset(scale_pool[:].bitcast(I32), 0)
+        def copy_y(qt, pair, on_vector):
+            if pair == 0:
+                y[qt] = tile([P, PACK, P], F32, "y%d" % qt)
+            rows = slice(2 * pair, 2 * pair + 2)
+            if on_vector:
+                nc.vector.tensor_copy(y[qt][:, rows, :], acc[qt, pair][:])
+            else:
+                nc.scalar.copy(y[qt][:, rows, :], acc[qt, pair][:])
+
+        def store_y(qt):
+            nc.sync.dma_start(out_rows[:, :, qt * P : (qt + 1) * P], y[qt][:])
+
+        def round_y(qt, on_vector):
+            y_bf[qt] = tile([P, P, PACK], BF16, "y_bf%d" % qt)
+            dst = y_bf[qt][:].rearrange("p (c i) t -> p c t i", i=4)
+            src = y[qt][:].rearrange("p t (c i) -> p c t i", i=4)
+            if on_vector:
+                nc.vector.tensor_copy(dst, src)
+            else:
+                nc.scalar.copy(dst, src)
+
+        def planes(qt):
+            y_codes = tile([P, P], U32, "y_codes%d" % qt)
+            nc.vector.quantize_mx(
+                out=y_codes[:].bitcast(FP8X4),
+                scales=y_scales[:, qt * P : (qt + 1) * P],
+                in_=y_bf[qt][:].rearrange("p q t -> p (q t)"),
+            )
+            words = out_1[0].rearrange("p q t -> p (q t)").bitcast(I32)
+            nc.sync.dma_start(words[:, qt * P : (qt + 1) * P], y_codes[:].bitcast(I32))
+
         nc.sync.dma_start(offsets[:], offs)
         make_identity(nc, ident[:])
-        load_size()
-        load_scales()
-        load_keys()
-        load_q()
-        load_vals(0, 0)
-        load_vals(0, 1)
-        load_vals(0, 2)
-        load_vals(0, 3)
-        load_vals(1, 0)
-        load_vals(1, 1)
-        load_vals(1, 2)
-        load_vals(1, 3)
-        spread_size()
-        gather_scales()
-        gather_words(0)
-        quantize_q()
-        gather_words(1)
-        score(0, 0)
-        score(1, 0)
-        score(0, 1)
-        score(1, 1)
-        cast(0, 0)
-        cast(0, 1)
-        cast(0, 2)
-        cast(0, 3)
-        maxima(0, 0)
-        maxima(1, 0)
-        maxima(0, 1)
-        maxima(1, 1)
-        tops()
-        exps(0)
-        exps(1)
-        sums(0)
-        sums(1)
-        sums_end(0)
-        denominators(0)
-        inverses(0)
-        factors(0)
-        sums_end(1)
-        denominators(1)
-        inverses(1)
-        factors(1)
-        gather_values(0, 0, 2)
-        gather_values(0, 1, 3)
-        times_size(0)
-        times_size(1)
-        weights(0)
-        weights(1)
-        cast(1, 0)
-        cast(1, 1)
-        cast(1, 2)
-        cast(1, 3)
+        for quad in range(4):
+            nc.sync.dma_start(
+                scale_pool[32 * quad : 32 * quad + 32, :].bitcast(I32),
+                keys_scales[0, 4 * quad : 4 * quad + 4, :].bitcast(I32).unsqueeze(0).to_broadcast([8, 4, T // 4]),
+            )
+        nc.sync.dma_start(key_pool[:].bitcast(I32), keys_words[0].bitcast(I32))
+        nc.sync.dma_start(q_raw[:], query.rearrange("(p j) q -> p j q", j=PACK))
+        for pair in range(PAIRS):
+            for c in range(CHUNKS):
+                load_vals(pair, c)
+            if pair == 0:
+                nc.sync.dma_start(size_cols[:], size.rearrange("o (g p t) -> (o p) g t", p=P, t=PACK))
+
+        key_scales = tile([P, I], U8, "key_scales")
+        nc.vector.tensor_copy(key_scales[:], scale_pool[:].indirect(offsets[:]))
+        gather_words(0, None)
+        q_bf = tile([P, Q, PACK], BF16, "q_bf")
+        q_codes = tile([P, Q], U32, "q_codes")
+        q_scales = tile([P, Q], U8, "q_scales")
+        nc.scalar.copy(q_bf[:].rearrange("p (c i) j -> p c j i", i=4), q_raw[:].rearrange("p j (c i) -> p c j i", i=4))
+        nc.vector.quantize_mx(out=q_codes[:].bitcast(FP8X4), scales=q_scales[:], in_=q_bf[:].rearrange("p q j -> p (q j)"))
+        gather_words(1, "q_bf")
+
+        best = tile([P, QTILES, G], F32, "best")
+        for g in range(PASSES):
+            for qt in range(QTILES):
+                score(qt, g)
+        for g in range(PASSES):
+            for qt in range(QTILES):
+                maxima(qt, g)
+            top(g)
+        neg_all = tile([P, QTILES], F32, "neg_all")
+        nc.vector.tensor_reduce(neg_all[:], best[:], AXIS_X, ALU.max, negate=True)
+
+        for pair in range(PAIRS):
+            windows[pair] = tile([P, T], F32, "window%d" % pair)
+        for c in range(CHUNKS):
+            cast(0, c, c == CHUNKS - 1)
+
+        partial = bank([P, QTILES, PASSES, P], 6, "partial")
+        for g in range(PASSES):
+            for qt in range(QTILES):
+                exps(qt, g)
+            for qt in range(QTILES):
+                quarter_sums(qt, g)
+            sized[g] = tile([P, PACK, Q], F32, "sized%d" % g)
+
+        share = tile([P, QTILES, G], F32, "share")
+        share_sum = tile([P, QTILES], F32, "share_sum")
+        for qt in range(QTILES):
+            nc.scalar.activation(
+                share[:, qt, :], best[:, qt, :], ACT.Exp, bias=neg_all[:, qt : qt + 1], accum_out=share_sum[:, qt : qt + 1]
+            )
+
+        partial_sb = tile([P, QTILES * PASSES, P], F32, "partial_sb")
+        nc.scalar.copy(partial_sb[:], partial[:].rearrange("p a g q -> p (a g) q"))
+        back = bank([P, QTILES * PASSES, P], 7, "back")
+        for n in range(QTILES * PASSES):
+            nc.tensor.transpose(back[:, n, :], partial_sb[:, n, :], ident[:])
+        for g in range(PASSES):
+            for half in range(2):
+                turn_probs(g, half)
+        times_size(0, 0)
+
+        gather_values(0, 0, None)
+        gather_values(0, 1, None)
+        turn_values(0, 0, 6)
+
+        total = tile([P, QTILES, G], F32, "total")
+        nc.vector.tensor_reduce(
+            total[:].rearrange("p a g -> p (a g)"), back[:].rearrange("p n (s c) -> p (n s) c", c=4), AXIS_X, ALU.add
+        )
+        turn_values(0, 1, 7)
+        denom = tile([P, QTILES, G], F32, "denom")
+        nc.vector.scalar_tensor_tensor(
+            denom[:], total[:], TINY, share_sum[:].unsqueeze(2).to_broadcast([P, QTILES, G]), ALU.max, ALU.mult
+        )
+        inverse = tile([P, QTILES * G], F32, "inverse")
+        nc.vector.reciprocal(inverse[:], denom[:].rearrange("p a g -> p (a g)"))
+        factor = tile([P, QTILES * G, 4], F32, "factor")
+        nc.vector.tensor_tensor(
+            factor[:],
+            share[:].rearrange("p a g -> p (a g)").unsqueeze(2).to_broadcast([P, QTILES * G, 4]),
+            inverse[:].unsqueeze(2).to_broadcast([P, QTILES * G, 4]),
+            ALU.mult,
+        )
+        f_turned = bank([P, PASSES, Q], 2, "f_turned")
+        flat = factor[:].rearrange("p n c -> p (n c)")
+        for g in range(PASSES):
+            for qt in range(QTILES):
+                n = PASSES * qt + g
+                nc.tensor.transpose(f_turned[:, g, qt * P : (qt + 1) * P], flat[:, n * P : (n + 1) * P], ident[:])
+
+        for c in range(CHUNKS):
+            cast(1, c, c == CHUNKS - 1)
+        gather_values(1, 0, "inverse")
+        gather_values(1, 1, None)
+        turn_values(1, 0, 3)
+        for t in range(1, PACK):
+            times_size(0, t)
         copy_values(0, 0)
+        turn_values(1, 1, 6)
         copy_values(0, 1)
-        turn_weights(0)
-        gather_values(1, 0, 2)
-        turn_weights(1)
-        gather_values(1, 1, 3)
+        for t in range(PACK):
+            times_size(1, t)
         copy_values(1, 0)
+        copy_values(1, 1)
+
+        weights(0, 0, QTILES)
         quantize_values(0, 0)
         quantize_values(0, 1)
-        quantize_weights(0)
-        quantize_weights(1)
-        copy_values(1, 1)
+        quantize_weights(0, 0, QTILES)
+        weights(1, 0, 1)
         quantize_values(1, 0)
+        quantize_weights(1, 0, 1)
         quantize_values(1, 1)
-        product(0, 0)
-        product(0, 1)
-        copy_y(0, 0)
-        copy_y(0, 1)
-        store_y(0)
-        product(1, 0)
-        product(1, 1)
-        copy_y(1, 0)
-        copy_y(1, 1)
-        store_y(1)
-        nc.vector.tensor_copy(y_bf[:, 0:P, :].rearrange("p (c i) t -> p c t i", i=4), y[:, :, 0:P].rearrange("p t (c i) -> p c t i", i=4))
-        nc.vector.tensor_copy(y_bf[:, P:Q, :].rearrange("p (c i) t -> p c t i", i=4), y[:, :, P:Q].rearrange("p t (c i) -> p c t i", i=4))
-        planes()
+        weights(1, 1, 2)
+        quantize_weights(1, 1, 2)
+        y_scales = tile([P, Q], U8, "y_scales")
+        for qt in range(QTILES):
+            for pair in range(PAIRS):
+                product(qt, pair, 0)
+        for qt in range(QTILES):
+            for pair in range(PAIRS):
+                product(qt, pair, 1)
+            copy_y(qt, 0, False)
+            copy_y(qt, 1, qt == 1)
+            store_y(qt)
+            round_y(qt, qt == 1)
+            planes(qt)
+        for quad in range(4):
+            queue = nc.scalar if quad % 2 == 0 else nc.sync
+            queue.dma_start(
+                out_2[0, 4 * quad : 4 * quad + 4, :].bitcast(I32),
+                y_scales[32 * quad : 32 * quad + 4, :].bitcast(I32),
+            )

@@ -108,7 +108,7 @@ def tile_attend_docmix_pl_kernel(tc, query, keys_words, keys_scales, size, vals,
         def quarter_sums(qt, g):
             for t in range(PACK):
                 nc.tensor.matmul(
-                    out=partial[:, qt, g, :],
+                    out=partial[g][:, qt, :],
                     lhsT=probs[qt, g][:, t, :],
                     rhs=ident[:],
                     start=(t == 0),
@@ -116,8 +116,8 @@ def tile_attend_docmix_pl_kernel(tc, query, keys_words, keys_scales, size, vals,
                     is_transpose=True,
                 )
 
-        def turn_probs(g, half):
-            p_turned[g, half] = bank([P, 2, Q], (4, 5, 0, 1)[2 * g + half], "p_turned%d_%d" % (g, half))
+        def turn_probs(g, half, number):
+            p_turned[g, half] = bank([P, 2, Q], number, "p_turned%d_%d" % (g, half))
             for qt in range(QTILES):
                 for u in range(2):
                     nc.tensor.transpose(p_turned[g, half][:, u, qt * P : (qt + 1) * P], probs[qt, g][:, 2 * half + u, :], ident[:])
@@ -177,7 +177,7 @@ def tile_attend_docmix_pl_kernel(tc, query, keys_words, keys_scales, size, vals,
 
         def product(qt, pair, g):
             if g == 0:
-                acc[qt, pair] = bank([P, 2, P], (4, 5, 0, 1)[2 * qt + pair], "acc%d_%d" % (qt, pair))
+                acc[qt, pair] = bank([P, 2, P], (2, 3, 7, 1)[2 * qt + pair], "acc%d_%d" % (qt, pair))
             for h in range(2):
                 nc.tensor.matmul_mx(
                     out=acc[qt, pair][:, h, :],
@@ -256,13 +256,13 @@ def tile_attend_docmix_pl_kernel(tc, query, keys_words, keys_scales, size, vals,
         neg_all = tile([P, QTILES], F32, "neg_all")
         nc.vector.tensor_reduce(neg_all[:], best[:], AXIS_X, ALU.max, negate=True)
 
-        for pair in range(PAIRS):
-            windows[pair] = tile([P, T], F32, "window%d" % pair)
+        windows[0] = tile([P, T], F32, "window0")
         for c in range(CHUNKS):
             cast(0, c, c == CHUNKS - 1)
 
-        partial = bank([P, QTILES, PASSES, P], 6, "partial")
+        partial = {}
         for g in range(PASSES):
+            partial[g] = bank([P, QTILES, P], 4 + g, "partial%d" % g)
             for qt in range(QTILES):
                 exps(qt, g)
             for qt in range(QTILES):
@@ -276,25 +276,23 @@ def tile_attend_docmix_pl_kernel(tc, query, keys_words, keys_scales, size, vals,
                 share[:, qt, :], best[:, qt, :], ACT.Exp, bias=neg_all[:, qt : qt + 1], accum_out=share_sum[:, qt : qt + 1]
             )
 
-        partial_sb = tile([P, QTILES * PASSES, P], F32, "partial_sb")
-        nc.scalar.copy(partial_sb[:], partial[:].rearrange("p a g q -> p (a g) q"))
-        back = bank([P, QTILES * PASSES, P], 7, "back")
-        for n in range(QTILES * PASSES):
-            nc.tensor.transpose(back[:, n, :], partial_sb[:, n, :], ident[:])
-        for g in range(PASSES):
-            for half in range(2):
-                turn_probs(g, half)
-        times_size(0, 0)
-
         gather_values(0, 0, None)
         gather_values(0, 1, None)
-        turn_values(0, 0, 6)
 
         total = tile([P, QTILES, G], F32, "total")
-        nc.vector.tensor_reduce(
-            total[:].rearrange("p a g -> p (a g)"), back[:].rearrange("p n (s c) -> p (n s) c", c=4), AXIS_X, ALU.add
-        )
-        turn_values(0, 1, 7)
+        for g in range(PASSES):
+            partial_sb = tile([P, QTILES, P], F32, "partial_sb%d" % g)
+            nc.scalar.copy(partial_sb[:], partial[g][:])
+            back = bank([P, QTILES, P], 2 + g, "back%d" % g)
+            for qt in range(QTILES):
+                nc.tensor.transpose(back[:, qt, :], partial_sb[:, qt, :], ident[:])
+            nc.vector.tensor_reduce(
+                total[:, :, g * per : (g + 1) * per], back[:].rearrange("p a (s c) -> p a s c", c=4), AXIS_X, ALU.add
+            )
+        turn_probs(0, 0, 2)
+        turn_probs(0, 1, 3)
+        turn_values(0, 0, 4)
+        turn_values(0, 1, 5)
         denom = tile([P, QTILES, G], F32, "denom")
         nc.vector.scalar_tensor_tensor(
             denom[:], total[:], TINY, share_sum[:].unsqueeze(2).to_broadcast([P, QTILES, G]), ALU.max, ALU.mult
@@ -308,23 +306,26 @@ def tile_attend_docmix_pl_kernel(tc, query, keys_words, keys_scales, size, vals,
             inverse[:].unsqueeze(2).to_broadcast([P, QTILES * G, 4]),
             ALU.mult,
         )
-        f_turned = bank([P, PASSES, Q], 2, "f_turned")
+        f_turned = bank([P, PASSES, Q], 0, "f_turned")
         flat = factor[:].rearrange("p n c -> p (n c)")
         for g in range(PASSES):
             for qt in range(QTILES):
                 n = PASSES * qt + g
                 nc.tensor.transpose(f_turned[:, g, qt * P : (qt + 1) * P], flat[:, n * P : (n + 1) * P], ident[:])
 
+        windows[1] = tile([P, T], F32, "window1", "neg_all")
         for c in range(CHUNKS):
             cast(1, c, c == CHUNKS - 1)
         gather_values(1, 0, "inverse")
         gather_values(1, 1, None)
-        turn_values(1, 0, 3)
-        for t in range(1, PACK):
+        for t in range(PACK):
             times_size(0, t)
         copy_values(0, 0)
-        turn_values(1, 1, 6)
         copy_values(0, 1)
+        turn_probs(1, 0, 4)
+        turn_probs(1, 1, 5)
+        turn_values(1, 0, 1)
+        turn_values(1, 1, 6)
         for t in range(PACK):
             times_size(1, t)
         copy_values(1, 0)

@@ -60,9 +60,9 @@ def tile_attend_docmix_pl_kernel(tc, query, keys_words, keys_scales, size, vals,
             v_raw[pair, c] = tile([P, 2, CHUNK], F32, "v_raw%d_%d" % (pair, c))
             nc.sync.dma_start(v_raw[pair, c][:], vals_rows[:, 2 * pair : 2 * pair + 2, c * CHUNK : (c + 1) * CHUNK])
 
-        def cast(pair, c, on_vector):
-            dst = windows[pair][:, c * CHUNK : (c + 1) * CHUNK].bitcast(BF16).rearrange("p (m h j) -> p m h j", h=2, j=PACK)
-            src = v_raw[pair, c][:].rearrange("p h (m j) -> p m h j", j=PACK)
+        def cast(pair, c, on_vector, first=0, last=CHUNK):
+            dst = windows[pair][:, c * CHUNK + first : c * CHUNK + last].bitcast(BF16).rearrange("p (m h j) -> p m h j", h=2, j=PACK)
+            src = v_raw[pair, c][:, :, first:last].rearrange("p h (m j) -> p m h j", j=PACK)
             if on_vector:
                 nc.vector.tensor_copy(dst, src)
             else:
@@ -92,9 +92,9 @@ def tile_attend_docmix_pl_kernel(tc, query, keys_words, keys_scales, size, vals,
                 ALU.max,
             )
 
-        def top(g):
-            neg_top[g] = tile([P, QTILES], F32, "neg_top%d" % g)
-            nc.vector.tensor_reduce(neg_top[g][:], best[:, :, g * per : (g + 1) * per], AXIS_X, ALU.max, negate=True)
+        def top(qt, g):
+            neg_top[qt, g] = tile([P, 1], F32, "neg_top%d_%d" % (qt, g))
+            nc.vector.tensor_reduce(neg_top[qt, g][:], best[:, qt, g * per : (g + 1) * per], AXIS_X, ALU.max, negate=True)
 
         def exps(qt, g):
             probs[qt, g] = tile([P, PACK, P], F32, "probs%d_%d" % (qt, g))
@@ -102,7 +102,7 @@ def tile_attend_docmix_pl_kernel(tc, query, keys_words, keys_scales, size, vals,
                 probs[qt, g][:],
                 scores[qt, g][:].rearrange("q (p t) -> q t p", t=PACK),
                 ACT.Exp,
-                bias=neg_top[g][:, qt : qt + 1],
+                bias=neg_top[qt, g][:],
             )
 
         def quarter_sums(qt, g):
@@ -156,9 +156,9 @@ def tile_attend_docmix_pl_kernel(tc, query, keys_words, keys_scales, size, vals,
             span = slice(first * P, last * P)
             rounded = tile([P, width, PACK], BF16, "w_bf" + name)
             nc.vector.tensor_tensor(
-                rounded[:].rearrange("p (c i) t -> p c t i", i=2),
-                sized[g][:, :, span].rearrange("p t (c i) -> p c t i", i=2),
-                f_turned[:, g, span].rearrange("p (c i) -> p c i", i=2).unsqueeze(2).to_broadcast([P, width // 2, PACK, 2]),
+                rounded[:],
+                sized[g][:, :, span].rearrange("p t q -> p q t"),
+                f_turned[:, g, span].unsqueeze(2).to_broadcast([P, width, PACK]),
                 ALU.mult,
             )
             w_bf[g, first] = rounded
@@ -177,7 +177,7 @@ def tile_attend_docmix_pl_kernel(tc, query, keys_words, keys_scales, size, vals,
 
         def product(qt, pair, g):
             if g == 0:
-                acc[qt, pair] = bank([P, 2, P], (2, 3, 7, 1)[2 * qt + pair], "acc%d_%d" % (qt, pair))
+                acc[qt, pair] = bank([P, 2, P], (3, 4, 5, 6)[2 * qt + pair], "acc%d_%d" % (qt, pair))
             for h in range(2):
                 nc.tensor.matmul_mx(
                     out=acc[qt, pair][:, h, :],
@@ -252,7 +252,7 @@ def tile_attend_docmix_pl_kernel(tc, query, keys_words, keys_scales, size, vals,
         for g in range(PASSES):
             for qt in range(QTILES):
                 maxima(qt, g)
-            top(g)
+                top(qt, g)
         neg_all = tile([P, QTILES], F32, "neg_all")
         nc.vector.tensor_reduce(neg_all[:], best[:], AXIS_X, ALU.max, negate=True)
 
@@ -279,53 +279,52 @@ def tile_attend_docmix_pl_kernel(tc, query, keys_words, keys_scales, size, vals,
         gather_values(0, 0, None)
         gather_values(0, 1, None)
 
-        total = tile([P, QTILES, G], F32, "total")
+        over_sum = tile([P, QTILES], F32, "over_sum")
+        nc.vector.reciprocal(over_sum[:], share_sum[:])
+        portion = tile([P, QTILES, G], F32, "portion")
+        nc.vector.tensor_tensor(portion[:], share[:], over_sum[:].unsqueeze(2).to_broadcast([P, QTILES, G]), ALU.mult)
+        f_turned = bank([P, PASSES, Q], 0, "f_turned")
         for g in range(PASSES):
             partial_sb = tile([P, QTILES, P], F32, "partial_sb%d" % g)
-            nc.scalar.copy(partial_sb[:], partial[g][:])
+            nc.scalar.activation(partial_sb[:], partial[g][:], ACT.Copy, bias=TINY)
             back = bank([P, QTILES, P], 2 + g, "back%d" % g)
             for qt in range(QTILES):
                 nc.tensor.transpose(back[:, qt, :], partial_sb[:, qt, :], ident[:])
-            nc.vector.tensor_reduce(
-                total[:, :, g * per : (g + 1) * per], back[:].rearrange("p a (s c) -> p a s c", c=4), AXIS_X, ALU.add
+            total = tile([P, QTILES * per], F32, "total%d" % g)
+            nc.vector.tensor_reduce(total[:], back[:].rearrange("p a (s c) -> p (a s) c", c=4), AXIS_X, ALU.add)
+            inverse = tile([P, QTILES, per], F32, "inverse%d" % g)
+            nc.vector.reciprocal(inverse[:].rearrange("p a s -> p (a s)"), total[:])
+            factor = tile([P, QTILES, per, 4], F32, "factor%d" % g)
+            nc.vector.tensor_tensor(
+                factor[:],
+                portion[:, :, g * per : (g + 1) * per].unsqueeze(3).to_broadcast([P, QTILES, per, 4]),
+                inverse[:].unsqueeze(3).to_broadcast([P, QTILES, per, 4]),
+                ALU.mult,
             )
+            for qt in range(QTILES):
+                nc.tensor.transpose(
+                    f_turned[:, g, qt * P : (qt + 1) * P], factor[:, qt].rearrange("p s c -> p (s c)"), ident[:]
+                )
         turn_probs(0, 0, 2)
         turn_probs(0, 1, 3)
+        turn_probs(1, 0, 6)
+        turn_probs(1, 1, 7)
         turn_values(0, 0, 4)
         turn_values(0, 1, 5)
-        denom = tile([P, QTILES, G], F32, "denom")
-        nc.vector.scalar_tensor_tensor(
-            denom[:], total[:], TINY, share_sum[:].unsqueeze(2).to_broadcast([P, QTILES, G]), ALU.max, ALU.mult
-        )
-        inverse = tile([P, QTILES * G], F32, "inverse")
-        nc.vector.reciprocal(inverse[:], denom[:].rearrange("p a g -> p (a g)"))
-        factor = tile([P, QTILES * G, 4], F32, "factor")
-        nc.vector.tensor_tensor(
-            factor[:],
-            share[:].rearrange("p a g -> p (a g)").unsqueeze(2).to_broadcast([P, QTILES * G, 4]),
-            inverse[:].unsqueeze(2).to_broadcast([P, QTILES * G, 4]),
-            ALU.mult,
-        )
-        f_turned = bank([P, PASSES, Q], 0, "f_turned")
-        flat = factor[:].rearrange("p n c -> p (n c)")
-        for g in range(PASSES):
-            for qt in range(QTILES):
-                n = PASSES * qt + g
-                nc.tensor.transpose(f_turned[:, g, qt * P : (qt + 1) * P], flat[:, n * P : (n + 1) * P], ident[:])
 
         windows[1] = tile([P, T], F32, "window1", "neg_all")
-        for c in range(CHUNKS):
-            cast(1, c, c == CHUNKS - 1)
-        gather_values(1, 0, "inverse")
+        cast(1, 0, True, 0, CHUNK // 2)
+        cast(1, 0, False, CHUNK // 2, CHUNK)
+        for c in range(1, CHUNKS):
+            cast(1, c, False)
+        gather_values(1, 0, None)
         gather_values(1, 1, None)
         for t in range(PACK):
             times_size(0, t)
         copy_values(0, 0)
         copy_values(0, 1)
-        turn_probs(1, 0, 4)
-        turn_probs(1, 1, 5)
         turn_values(1, 0, 1)
-        turn_values(1, 1, 6)
+        turn_values(1, 1, 2)
         for t in range(PACK):
             times_size(1, t)
         copy_values(1, 0)

@@ -27,6 +27,7 @@ QTILES = Q // P
 PAIRS = 2
 CHUNK = 512
 CHUNKS = T // CHUNK
+SPLIT = 320
 TINY = 1e-30
 
 
@@ -220,12 +221,13 @@ def tile_attend_docmix_pl_kernel(tc, query, keys_words, keys_scales, size, vals,
             words = out_1[0].rearrange("p q t -> p (q t)").bitcast(I32)
             nc.sync.dma_start(words[:, qt * P : (qt + 1) * P], y_codes[:].bitcast(I32))
 
+        nc.gpsimd.memset(scale_pool[:].bitcast(I32), 0)
         nc.sync.dma_start(offsets[:], offs)
         make_identity(nc, ident[:])
         for quad in range(4):
             nc.sync.dma_start(
-                scale_pool[32 * quad : 32 * quad + 32, :].bitcast(I32),
-                keys_scales[0, 4 * quad : 4 * quad + 4, :].bitcast(I32).unsqueeze(0).to_broadcast([8, 4, T // 4]),
+                scale_pool[32 * quad : 32 * quad + 4, :].bitcast(I32),
+                keys_scales[0, 4 * quad : 4 * quad + 4, :].bitcast(I32),
             )
         nc.sync.dma_start(key_pool[:].bitcast(I32), keys_words[0].bitcast(I32))
         nc.sync.dma_start(q_raw[:], query.rearrange("(p j) q -> p j q", j=PACK))
@@ -258,7 +260,7 @@ def tile_attend_docmix_pl_kernel(tc, query, keys_words, keys_scales, size, vals,
 
         windows[0] = tile([P, T], F32, "window0")
         for c in range(CHUNKS):
-            cast(0, c, c == CHUNKS - 1)
+            cast(0, c, False)
 
         partial = {}
         for g in range(PASSES):
@@ -313,8 +315,8 @@ def tile_attend_docmix_pl_kernel(tc, query, keys_words, keys_scales, size, vals,
         turn_values(0, 1, 5)
 
         windows[1] = tile([P, T], F32, "window1", "neg_all")
-        cast(1, 0, True, 0, CHUNK // 2)
-        cast(1, 0, False, CHUNK // 2, CHUNK)
+        cast(1, 0, True, 0, SPLIT)
+        cast(1, 0, False, SPLIT, CHUNK)
         for c in range(1, CHUNKS):
             cast(1, c, False)
         gather_values(1, 0, None)

@@ -27,7 +27,6 @@ QTILES = Q // P
 PAIRS = 2
 CHUNK = 512
 CHUNKS = T // CHUNK
-SPLIT = 320
 TINY = 1e-30
 
 
@@ -61,9 +60,9 @@ def tile_attend_docmix_pl_kernel(tc, query, keys_words, keys_scales, size, vals,
             v_raw[pair, c] = tile([P, 2, CHUNK], F32, "v_raw%d_%d" % (pair, c))
             nc.sync.dma_start(v_raw[pair, c][:], vals_rows[:, 2 * pair : 2 * pair + 2, c * CHUNK : (c + 1) * CHUNK])
 
-        def cast(pair, c, on_vector, first=0, last=CHUNK):
-            dst = windows[pair][:, c * CHUNK + first : c * CHUNK + last].bitcast(BF16).rearrange("p (m h j) -> p m h j", h=2, j=PACK)
-            src = v_raw[pair, c][:, :, first:last].rearrange("p h (m j) -> p m h j", j=PACK)
+        def cast(pair, c, on_vector):
+            dst = windows[pair][:, c * CHUNK : (c + 1) * CHUNK].bitcast(BF16).rearrange("p (m h j) -> p m h j", h=2, j=PACK)
+            src = v_raw[pair, c][:].rearrange("p h (m j) -> p m h j", j=PACK)
             if on_vector:
                 nc.vector.tensor_copy(dst, src)
             else:
@@ -109,7 +108,7 @@ def tile_attend_docmix_pl_kernel(tc, query, keys_words, keys_scales, size, vals,
         def quarter_sums(qt, g):
             for t in range(PACK):
                 nc.tensor.matmul(
-                    out=partial[g][:, qt, :],
+                    out=partial[qt][:, g, :],
                     lhsT=probs[qt, g][:, t, :],
                     rhs=ident[:],
                     start=(t == 0),
@@ -202,24 +201,24 @@ def tile_attend_docmix_pl_kernel(tc, query, keys_words, keys_scales, size, vals,
         def store_y(qt):
             nc.sync.dma_start(out_rows[:, :, qt * P : (qt + 1) * P], y[qt][:])
 
-        def round_y(qt, on_vector):
-            y_bf[qt] = tile([P, P, PACK], BF16, "y_bf%d" % qt)
-            dst = y_bf[qt][:].rearrange("p (c i) t -> p c t i", i=4)
-            src = y[qt][:].rearrange("p t (c i) -> p c t i", i=4)
+        def round_y(qt, first, last, on_vector):
+            dst = y_bf[qt][:, first:last, :].rearrange("p (c i) t -> p c t i", i=4)
+            src = y[qt][:, :, first:last].rearrange("p t (c i) -> p c t i", i=4)
             if on_vector:
                 nc.vector.tensor_copy(dst, src)
             else:
                 nc.scalar.copy(dst, src)
 
-        def planes(qt):
-            y_codes = tile([P, P], U32, "y_codes%d" % qt)
+        def quantize_y(qt, first, last):
             nc.vector.quantize_mx(
-                out=y_codes[:].bitcast(FP8X4),
-                scales=y_scales[:, qt * P : (qt + 1) * P],
-                in_=y_bf[qt][:].rearrange("p q t -> p (q t)"),
+                out=y_codes[qt][:, first:last].bitcast(FP8X4),
+                scales=y_scales[:, qt * P + first : qt * P + last],
+                in_=y_bf[qt][:, first:last, :].rearrange("p q t -> p (q t)"),
             )
+
+        def store_codes(qt, queue):
             words = out_1[0].rearrange("p q t -> p (q t)").bitcast(I32)
-            nc.sync.dma_start(words[:, qt * P : (qt + 1) * P], y_codes[:].bitcast(I32))
+            queue.dma_start(words[:, qt * P : (qt + 1) * P], y_codes[qt][:].bitcast(I32))
 
         nc.gpsimd.memset(scale_pool[:].bitcast(I32), 0)
         nc.sync.dma_start(offsets[:], offs)
@@ -262,50 +261,50 @@ def tile_attend_docmix_pl_kernel(tc, query, keys_words, keys_scales, size, vals,
         for c in range(CHUNKS):
             cast(0, c, False)
 
-        partial = {}
+        partial, share, sums = {}, {}, {}
+        for qt in range(QTILES):
+            partial[qt] = bank([P, PASSES, P], 4 + qt, "partial%d" % qt)
         for g in range(PASSES):
-            partial[g] = bank([P, QTILES, P], 4 + g, "partial%d" % g)
             for qt in range(QTILES):
                 exps(qt, g)
-            for qt in range(QTILES):
                 quarter_sums(qt, g)
-            sized[g] = tile([P, PACK, Q], F32, "sized%d" % g)
-
-        share = tile([P, QTILES, G], F32, "share")
-        share_sum = tile([P, QTILES], F32, "share_sum")
         for qt in range(QTILES):
-            nc.scalar.activation(
-                share[:, qt, :], best[:, qt, :], ACT.Exp, bias=neg_all[:, qt : qt + 1], accum_out=share_sum[:, qt : qt + 1]
-            )
+            share[qt] = tile([P, G], F32, "share%d" % qt)
+            sums[qt] = tile([P, G + 1], F32, "sums%d" % qt)
+            nc.scalar.activation(share[qt][:], best[:, qt, :], ACT.Exp, bias=neg_all[:, qt : qt + 1], accum_out=sums[qt][:, G : G + 1])
+        for g in range(PASSES):
+            sized[g] = tile([P, PACK, Q], F32, "sized%d" % g)
 
         gather_values(0, 0, None)
         gather_values(0, 1, None)
 
-        over_sum = tile([P, QTILES], F32, "over_sum")
-        nc.vector.reciprocal(over_sum[:], share_sum[:])
-        portion = tile([P, QTILES, G], F32, "portion")
-        nc.vector.tensor_tensor(portion[:], share[:], over_sum[:].unsqueeze(2).to_broadcast([P, QTILES, G]), ALU.mult)
         f_turned = bank([P, PASSES, Q], 0, "f_turned")
-        for g in range(PASSES):
-            partial_sb = tile([P, QTILES, P], F32, "partial_sb%d" % g)
-            nc.scalar.activation(partial_sb[:], partial[g][:], ACT.Copy, bias=TINY)
-            back = bank([P, QTILES, P], 2 + g, "back%d" % g)
-            for qt in range(QTILES):
-                nc.tensor.transpose(back[:, qt, :], partial_sb[:, qt, :], ident[:])
-            total = tile([P, QTILES * per], F32, "total%d" % g)
-            nc.vector.tensor_reduce(total[:], back[:].rearrange("p a (s c) -> p (a s) c", c=4), AXIS_X, ALU.add)
-            inverse = tile([P, QTILES, per], F32, "inverse%d" % g)
-            nc.vector.reciprocal(inverse[:].rearrange("p a s -> p (a s)"), total[:])
-            factor = tile([P, QTILES, per, 4], F32, "factor%d" % g)
-            nc.vector.tensor_tensor(
+        inverse = {}
+        for qt in range(QTILES):
+            partial_sb = tile([P, PASSES, P], F32, "partial_sb%d" % qt)
+            nc.scalar.activation(partial_sb[:], partial[qt][:], ACT.Copy, bias=TINY)
+            back = bank([P, PASSES, P], 2 + qt, "back%d" % qt)
+            for g in range(PASSES):
+                nc.tensor.transpose(back[:, g, :], partial_sb[:, g, :], ident[:])
+            nc.vector.tensor_reduce(sums[qt][:, 0:G], back[:].rearrange("p g (s c) -> p (g s) c", c=4), AXIS_X, ALU.add)
+        for qt in range(QTILES):
+            inverse[qt] = tile([P, G + 1], F32, "inverse%d" % qt)
+            nc.vector.reciprocal(inverse[qt][:], sums[qt][:])
+        for qt in range(QTILES):
+            factor = tile([P, G, 4], F32, "factor%d" % qt)
+            nc.vector.scalar_tensor_tensor(
                 factor[:],
-                portion[:, :, g * per : (g + 1) * per].unsqueeze(3).to_broadcast([P, QTILES, per, 4]),
-                inverse[:].unsqueeze(3).to_broadcast([P, QTILES, per, 4]),
+                inverse[qt][:, 0:G].unsqueeze(2).to_broadcast([P, G, 4]),
+                inverse[qt][:, G : G + 1],
+                share[qt][:].unsqueeze(2).to_broadcast([P, G, 4]),
+                ALU.mult,
                 ALU.mult,
             )
-            for qt in range(QTILES):
+            for g in range(PASSES):
                 nc.tensor.transpose(
-                    f_turned[:, g, qt * P : (qt + 1) * P], factor[:, qt].rearrange("p s c -> p (s c)"), ident[:]
+                    f_turned[:, g, qt * P : (qt + 1) * P],
+                    factor[:, g * per : (g + 1) * per, :].rearrange("p s c -> p (s c)"),
+                    ident[:],
                 )
         turn_probs(0, 0, 2)
         turn_probs(0, 1, 3)
@@ -315,8 +314,7 @@ def tile_attend_docmix_pl_kernel(tc, query, keys_words, keys_scales, size, vals,
         turn_values(0, 1, 5)
 
         windows[1] = tile([P, T], F32, "window1", "neg_all")
-        cast(1, 0, True, 0, SPLIT)
-        cast(1, 0, False, SPLIT, CHUNK)
+        cast(1, 0, True)
         for c in range(1, CHUNKS):
             cast(1, c, False)
         gather_values(1, 0, None)
@@ -346,14 +344,26 @@ def tile_attend_docmix_pl_kernel(tc, query, keys_words, keys_scales, size, vals,
         for qt in range(QTILES):
             for pair in range(PAIRS):
                 product(qt, pair, 0)
+        y_codes = {}
         for qt in range(QTILES):
+            y_bf[qt] = tile([P, P, PACK], BF16, "y_bf%d" % qt)
+            y_codes[qt] = tile([P, P], U32, "y_codes%d" % qt)
             for pair in range(PAIRS):
                 product(qt, pair, 1)
-            copy_y(qt, 0, False)
-            copy_y(qt, 1, qt == 1)
-            store_y(qt)
-            round_y(qt, qt == 1)
-            planes(qt)
+        copy_y(0, 0, False)
+        copy_y(0, 1, False)
+        store_y(0)
+        round_y(0, 0, P, True)
+        copy_y(1, 0, False)
+        copy_y(1, 1, True)
+        store_y(1)
+        quantize_y(0, 0, P)
+        store_codes(0, nc.sync)
+        for half in range(2):
+            round_y(1, half * P // 2, (half + 1) * P // 2, True)
+        for half in range(2):
+            quantize_y(1, half * P // 2, (half + 1) * P // 2)
+        store_codes(1, nc.sync)
         for quad in range(4):
             queue = nc.scalar if quad % 2 == 0 else nc.sync
             queue.dma_start(

@@ -27,6 +27,7 @@ QTILES = Q // P
 PAIRS = 2
 CHUNK = 512
 CHUNKS = T // CHUNK
+FILL = 192
 TINY = 1e-30
 
 
@@ -60,9 +61,9 @@ def tile_attend_docmix_pl_kernel(tc, query, keys_words, keys_scales, size, vals,
             v_raw[pair, c] = tile([P, 2, CHUNK], F32, "v_raw%d_%d" % (pair, c))
             nc.sync.dma_start(v_raw[pair, c][:], vals_rows[:, 2 * pair : 2 * pair + 2, c * CHUNK : (c + 1) * CHUNK])
 
-        def cast(pair, c, on_vector):
-            dst = windows[pair][:, c * CHUNK : (c + 1) * CHUNK].bitcast(BF16).rearrange("p (m h j) -> p m h j", h=2, j=PACK)
-            src = v_raw[pair, c][:].rearrange("p h (m j) -> p m h j", j=PACK)
+        def cast(pair, c, on_vector, first=0, last=CHUNK):
+            dst = windows[pair][:, c * CHUNK + first : c * CHUNK + last].bitcast(BF16).rearrange("p (m h j) -> p m h j", h=2, j=PACK)
+            src = v_raw[pair, c][:, :, first:last].rearrange("p h (m j) -> p m h j", j=PACK)
             if on_vector:
                 nc.vector.tensor_copy(dst, src)
             else:
@@ -137,18 +138,22 @@ def tile_attend_docmix_pl_kernel(tc, query, keys_words, keys_scales, size, vals,
                 nc.tensor.transpose(v_turned[pair, g][:, c, :], picked[pair, g][:, c:PASS:4], ident[:])
 
         def copy_values(pair, g):
-            v_bf[pair, g] = tile([P, PASS], F32, "v_bf%d_%d" % (pair, g))
+            if g == 0:
+                v_bf[pair] = tile([P, I], F32, "v_bf%d" % pair)
             nc.scalar.copy(
-                v_bf[pair, g][:].rearrange("p (h e u) -> p h e u", h=2, u=2),
+                v_bf[pair][:, g * PASS : (g + 1) * PASS].rearrange("p (h e u) -> p h e u", h=2, u=2),
                 v_turned[pair, g][:].rearrange("p (h u) e -> p h e u", u=2),
             )
 
-        def quantize_values(pair, g):
-            v_codes[pair, g] = tile([P, 2 * P], U32, "v_codes%d_%d" % (pair, g))
-            v_scales[pair, g] = tile([P, 2 * P], U8, "v_scales%d_%d" % (pair, g))
+        def quantize_values(pair, first, last):
+            codes = tile([P, (last - first) * 2 * P], U32, "v_codes%d_%d" % (pair, first))
+            scales = tile([P, (last - first) * 2 * P], U8, "v_scales%d_%d" % (pair, first))
             nc.vector.quantize_mx(
-                out=v_codes[pair, g][:].bitcast(FP8X4), scales=v_scales[pair, g][:], in_=v_bf[pair, g][:].bitcast(BF16)
+                out=codes[:].bitcast(FP8X4), scales=scales[:], in_=v_bf[pair][:, first * PASS : last * PASS].bitcast(BF16)
             )
+            for g in range(first, last):
+                v_codes[pair, g] = codes[:, (g - first) * 2 * P : (g - first + 1) * 2 * P]
+                v_scales[pair, g] = scales[:, (g - first) * 2 * P : (g - first + 1) * 2 * P]
 
         def weights(g, first, last):
             name = "%d_%d" % (g, first)
@@ -242,9 +247,9 @@ def tile_attend_docmix_pl_kernel(tc, query, keys_words, keys_scales, size, vals,
         q_bf = tile([P, Q, PACK], BF16, "q_bf")
         q_codes = tile([P, Q], U32, "q_codes")
         q_scales = tile([P, Q], U8, "q_scales")
-        nc.scalar.copy(q_bf[:].rearrange("p (c i) j -> p c j i", i=4), q_raw[:].rearrange("p j (c i) -> p c j i", i=4))
+        nc.scalar.copy(q_bf[:], q_raw[:].rearrange("p j q -> p q j"))
         nc.vector.quantize_mx(out=q_codes[:].bitcast(FP8X4), scales=q_scales[:], in_=q_bf[:].rearrange("p q j -> p (q j)"))
-        gather_words(1, "q_bf")
+        gather_words(1, "q_raw")
 
         best = tile([P, QTILES, G], F32, "best")
         for g in range(PASSES):
@@ -258,8 +263,10 @@ def tile_attend_docmix_pl_kernel(tc, query, keys_words, keys_scales, size, vals,
         nc.vector.tensor_reduce(neg_all[:], best[:], AXIS_X, ALU.max, negate=True)
 
         windows[0] = tile([P, T], F32, "window0")
-        for c in range(CHUNKS):
+        for c in range(CHUNKS - 1):
             cast(0, c, False)
+        cast(0, CHUNKS - 1, False, 0, CHUNK - FILL)
+        cast(0, CHUNKS - 1, True, CHUNK - FILL, CHUNK)
 
         partial, share, sums = {}, {}, {}
         for qt in range(QTILES):
@@ -331,14 +338,13 @@ def tile_attend_docmix_pl_kernel(tc, query, keys_words, keys_scales, size, vals,
         copy_values(1, 1)
 
         weights(0, 0, QTILES)
-        quantize_values(0, 0)
-        quantize_values(0, 1)
+        quantize_values(0, 0, PASSES)
         quantize_weights(0, 0, QTILES)
         weights(1, 0, 1)
-        quantize_values(1, 0)
+        quantize_values(1, 0, 1)
         quantize_weights(1, 0, 1)
-        quantize_values(1, 1)
         weights(1, 1, 2)
+        quantize_values(1, 1, 2)
         quantize_weights(1, 1, 2)
         y_scales = tile([P, Q], U8, "y_scales")
         for qt in range(QTILES):

@@ -334,6 +334,17 @@ def tile_attend_docmix_pl_kernel(tc, query, keys_words, keys_scales, size, vals,
         turn_values(1, 1, 2)
         for t in range(PACK):
             times_size(1, t)
+        idle = bank([P, PASS], 7, "idle")
+        for qt in range(QTILES):
+            nc.tensor.matmul_mx(
+                out=idle[:],
+                lhsT=q_codes[:, qt * P : (qt + 1) * P].bitcast(FP8X4),
+                lhsT_scale=q_scales[:, qt * P : (qt + 1) * P],
+                rhs=key_words[0][:].bitcast(FP4X4),
+                rhs_scale=key_scales[:, 0:PASS],
+                start=True,
+                stop=True,
+            )
         copy_values(1, 0)
         copy_values(1, 1)
 

@@ -25,9 +25,6 @@ RUN = I // G
 PASSES = I // PASS
 QTILES = Q // P
 PAIRS = 2
-CHUNK = 512
-CHUNKS = T // CHUNK
-FILL = 192
 TINY = 1e-30
 
 
@@ -53,21 +50,13 @@ def tile_attend_docmix_pl_kernel(tc, query, keys_words, keys_scales, size, vals,
         ident = tile([P, P], F32, "ident")
         vals_rows = vals.rearrange("(p t) n -> p t n", t=PACK)
         out_rows = out_0.rearrange("(p t) q -> p t q", t=PACK)
-        v_raw, windows, key_words, scores, neg_top, probs = {}, {}, {}, {}, {}, {}
+        windows, key_words, scores, neg_top, probs = {}, {}, {}, {}, {}
         picked, v_turned, v_bf, v_codes, v_scales = {}, {}, {}, {}, {}
         p_turned, sized, w_bf, w_codes, w_scales, acc, y, y_bf = {}, {}, {}, {}, {}, {}, {}, {}
 
-        def load_vals(pair, c):
-            v_raw[pair, c] = tile([P, 2, CHUNK], F32, "v_raw%d_%d" % (pair, c))
-            nc.sync.dma_start(v_raw[pair, c][:], vals_rows[:, 2 * pair : 2 * pair + 2, c * CHUNK : (c + 1) * CHUNK])
-
-        def cast(pair, c, on_vector, first=0, last=CHUNK):
-            dst = windows[pair][:, c * CHUNK + first : c * CHUNK + last].bitcast(BF16).rearrange("p (m h j) -> p m h j", h=2, j=PACK)
-            src = v_raw[pair, c][:, :, first:last].rearrange("p h (m j) -> p m h j", j=PACK)
-            if on_vector:
-                nc.vector.tensor_copy(dst, src)
-            else:
-                nc.scalar.activation(dst, src, ACT.Copy)
+        def load_vals(t):
+            windows[t] = tile([P, T], F32, "window%d" % t)
+            nc.sync.dma_start(windows[t][:], vals_rows[:, t, :])
 
         def gather_words(g, tag):
             key_words[g] = tile([P, PASS], U16, "key_words%d" % g, tag)
@@ -128,32 +117,30 @@ def tile_attend_docmix_pl_kernel(tc, query, keys_words, keys_scales, size, vals,
                 sized[g][:, t, :], p_turned[g, t // 2][:, t % 2, :], ACT.Copy, scale=size_cols[:, g, t : t + 1]
             )
 
-        def gather_values(pair, g, tag):
-            picked[pair, g] = tile([P, PASS], F32, "picked%d_%d" % (pair, g), tag)
-            nc.vector.tensor_copy(picked[pair, g][:], windows[pair][:].indirect(offsets[:, g * cols : (g + 1) * cols]))
+        def gather_values(t):
+            picked[t] = tile([P, I], BF16, "picked%d" % t)
+            nc.vector.tensor_copy(picked[t][:], windows[t][:].indirect(offsets[:]))
 
-        def turn_values(pair, g, number):
-            v_turned[pair, g] = bank([P, 4, P], number, "v_turned%d_%d" % (pair, g))
-            for c in range(4):
-                nc.tensor.transpose(v_turned[pair, g][:, c, :], picked[pair, g][:, c:PASS:4], ident[:])
+        def turn_values(t, number):
+            v_turned[t] = bank([P, PASSES, 2, P], number, "v_turned%d" % t)
+            words = picked[t][:].bitcast(F32)
+            for g in range(PASSES):
+                for u in range(2):
+                    nc.tensor.transpose(v_turned[t][:, g, u, :], words[:, 2 * P * g + u : 2 * P * (g + 1) : 2], ident[:])
 
-        def copy_values(pair, g):
-            if g == 0:
-                v_bf[pair] = tile([P, I], F32, "v_bf%d" % pair)
-            nc.scalar.copy(
-                v_bf[pair][:, g * PASS : (g + 1) * PASS].rearrange("p (h e u) -> p h e u", h=2, u=2),
-                v_turned[pair, g][:].rearrange("p (h u) e -> p h e u", u=2),
-            )
+        def copy_values(t):
+            v_bf[t] = tile([P, PASSES, P, 2], F32, "v_bf%d" % t)
+            nc.scalar.copy(v_bf[t][:], v_turned[t][:].rearrange("p g u e -> p g e u"))
 
-        def quantize_values(pair, first, last):
-            codes = tile([P, (last - first) * 2 * P], U32, "v_codes%d_%d" % (pair, first))
-            scales = tile([P, (last - first) * 2 * P], U8, "v_scales%d_%d" % (pair, first))
+        def quantize_values(t):
+            codes = tile([P, PASSES * P], U32, "v_codes%d" % t)
+            scales = tile([P, PASSES * P], U8, "v_scales%d" % t)
             nc.vector.quantize_mx(
-                out=codes[:].bitcast(FP8X4), scales=scales[:], in_=v_bf[pair][:, first * PASS : last * PASS].bitcast(BF16)
+                out=codes[:].bitcast(FP8X4), scales=scales[:], in_=v_bf[t][:].rearrange("p g e u -> p (g e u)").bitcast(BF16)
             )
-            for g in range(first, last):
-                v_codes[pair, g] = codes[:, (g - first) * 2 * P : (g - first + 1) * 2 * P]
-                v_scales[pair, g] = scales[:, (g - first) * 2 * P : (g - first + 1) * 2 * P]
+            for g in range(PASSES):
+                v_codes[t, g] = codes[:, g * P : (g + 1) * P]
+                v_scales[t, g] = scales[:, g * P : (g + 1) * P]
 
         def weights(g, first, last):
             name = "%d_%d" % (g, first)
@@ -182,12 +169,12 @@ def tile_attend_docmix_pl_kernel(tc, query, keys_words, keys_scales, size, vals,
 
         def product(qt, pair, g):
             if g == 0:
-                acc[qt, pair] = bank([P, 2, P], (3, 4, 5, 6)[2 * qt + pair], "acc%d_%d" % (qt, pair))
+                acc[qt, pair] = bank([P, 2, P], (2, 3, 1, 5)[2 * qt + pair], "acc%d_%d" % (qt, pair))
             for h in range(2):
                 nc.tensor.matmul_mx(
                     out=acc[qt, pair][:, h, :],
-                    lhsT=v_codes[pair, g][:, h * P : (h + 1) * P].bitcast(FP8X4),
-                    lhsT_scale=v_scales[pair, g][:, h * P : (h + 1) * P],
+                    lhsT=v_codes[2 * pair + h, g].bitcast(FP8X4),
+                    lhsT_scale=v_scales[2 * pair + h, g],
                     rhs=w_codes[g, qt].bitcast(FP8X4),
                     rhs_scale=w_scales[g, qt],
                     start=(g == 0 and h == 0),
@@ -235,11 +222,9 @@ def tile_attend_docmix_pl_kernel(tc, query, keys_words, keys_scales, size, vals,
             )
         nc.sync.dma_start(key_pool[:].bitcast(I32), keys_words[0].bitcast(I32))
         nc.sync.dma_start(q_raw[:], query.rearrange("(p j) q -> p j q", j=PACK))
-        for pair in range(PAIRS):
-            for c in range(CHUNKS):
-                load_vals(pair, c)
-            if pair == 0:
-                nc.sync.dma_start(size_cols[:], size.rearrange("o (g p t) -> (o p) g t", p=P, t=PACK))
+        nc.sync.dma_start(size_cols[:], size.rearrange("o (g p t) -> (o p) g t", p=P, t=PACK))
+        for t in range(PACK):
+            load_vals(t)
 
         key_scales = tile([P, I], U8, "key_scales")
         nc.vector.tensor_copy(key_scales[:], scale_pool[:].indirect(offsets[:]))
@@ -262,12 +247,6 @@ def tile_attend_docmix_pl_kernel(tc, query, keys_words, keys_scales, size, vals,
         neg_all = tile([P, QTILES], F32, "neg_all")
         nc.vector.tensor_reduce(neg_all[:], best[:], AXIS_X, ALU.max, negate=True)
 
-        windows[0] = tile([P, T], F32, "window0")
-        for c in range(CHUNKS - 1):
-            cast(0, c, False)
-        cast(0, CHUNKS - 1, False, 0, CHUNK - FILL)
-        cast(0, CHUNKS - 1, True, CHUNK - FILL, CHUNK)
-
         partial, share, sums = {}, {}, {}
         for qt in range(QTILES):
             partial[qt] = bank([P, PASSES, P], 4 + qt, "partial%d" % qt)
@@ -282,8 +261,10 @@ def tile_attend_docmix_pl_kernel(tc, query, keys_words, keys_scales, size, vals,
         for g in range(PASSES):
             sized[g] = tile([P, PACK, Q], F32, "sized%d" % g)
 
-        gather_values(0, 0, None)
-        gather_values(0, 1, None)
+        for t in range(2):
+            gather_values(t)
+            turn_values(t, 6 + t)
+            copy_values(t)
 
         f_turned = bank([P, PASSES, Q], 0, "f_turned")
         inverse = {}
@@ -315,23 +296,15 @@ def tile_attend_docmix_pl_kernel(tc, query, keys_words, keys_scales, size, vals,
                 )
         turn_probs(0, 0, 2)
         turn_probs(0, 1, 3)
-        turn_probs(1, 0, 6)
-        turn_probs(1, 1, 7)
-        turn_values(0, 0, 4)
-        turn_values(0, 1, 5)
-
-        windows[1] = tile([P, T], F32, "window1", "neg_all")
-        cast(1, 0, True)
-        for c in range(1, CHUNKS):
-            cast(1, c, False)
-        gather_values(1, 0, None)
-        gather_values(1, 1, None)
+        turn_probs(1, 0, 5)
+        turn_probs(1, 1, 6)
+        gather_values(2)
+        gather_values(3)
         for t in range(PACK):
             times_size(0, t)
-        copy_values(0, 0)
-        copy_values(0, 1)
-        turn_values(1, 0, 1)
-        turn_values(1, 1, 2)
+        turn_values(2, 1)
+        turn_values(3, 4)
+        copy_values(2)
         for t in range(PACK):
             times_size(1, t)
         idle = bank([P, PASS], 7, "idle")
@@ -345,17 +318,17 @@ def tile_attend_docmix_pl_kernel(tc, query, keys_words, keys_scales, size, vals,
                 start=True,
                 stop=True,
             )
-        copy_values(1, 0)
-        copy_values(1, 1)
+        copy_values(3)
 
+        quantize_values(0)
+        quantize_values(1)
         weights(0, 0, QTILES)
-        quantize_values(0, 0, PASSES)
+        quantize_values(2)
         quantize_weights(0, 0, QTILES)
         weights(1, 0, 1)
-        quantize_values(1, 0, 1)
+        quantize_values(3)
         quantize_weights(1, 0, 1)
         weights(1, 1, 2)
-        quantize_values(1, 1, 2)
         quantize_weights(1, 1, 2)
         y_scales = tile([P, Q], U8, "y_scales")
         for qt in range(QTILES):

@@ -25,6 +25,7 @@ RUN = I // G
 PASSES = I // PASS
 QTILES = Q // P
 PAIRS = 2
+HALF = T // 2
 TINY = 1e-30
 
 
@@ -45,46 +46,63 @@ def tile_attend_docmix_pl_kernel(tc, query, keys_words, keys_scales, size, vals,
         offsets = sb.tile([P, I // 16], U16, name="offsets")
         key_pool = tile([P, T], U16, "key_pool")
         scale_pool = tile([P, T], U8, "scale_pool")
-        size_cols = tile([P, PASSES, PACK], F32, "size_cols")
         q_raw = tile([P, PACK, Q], F32, "q_raw")
         ident = tile([P, P], F32, "ident")
         vals_rows = vals.rearrange("(p t) n -> p t n", t=PACK)
         out_rows = out_0.rearrange("(p t) q -> p t q", t=PACK)
-        windows, key_words, scores, neg_top, probs = {}, {}, {}, {}, {}
+        v_raw, windows, key_words, key_scales, scores, neg_top, probs = {}, {}, {}, {}, {}, {}, {}
+        q_bf, q_codes, q_scales, best, partial, share, sums, inverse, f_turned = {}, {}, {}, {}, {}, {}, {}, {}, {}
         picked, v_turned, v_bf, v_codes, v_scales = {}, {}, {}, {}, {}
-        p_turned, sized, w_bf, w_codes, w_scales, acc, y, y_bf = {}, {}, {}, {}, {}, {}, {}, {}
+        p_turned, sized, w_bf, w_codes, w_scales, acc, y, y_bf, y_codes = {}, {}, {}, {}, {}, {}, {}, {}, {}
 
-        def load_vals(t):
-            windows[t] = tile([P, T], F32, "window%d" % t)
+        def load_window(t, tag):
+            windows[t] = tile([P, T], F32, "window%d" % t, tag)
             nc.sync.dma_start(windows[t][:], vals_rows[:, t, :])
 
-        def gather_words(g, tag):
-            key_words[g] = tile([P, PASS], U16, "key_words%d" % g, tag)
+        def gather_words(g):
+            key_words[g] = tile([P, PASS], U16, "key_words%d" % g)
             nc.vector.tensor_copy(key_words[g][:], key_pool[:].indirect(offsets[:, g * cols : (g + 1) * cols]))
 
+        def gather_scales(g):
+            key_scales[g] = tile([P, PASS], U8, "key_scales%d" % g)
+            nc.vector.tensor_copy(key_scales[g][:], scale_pool[:].indirect(offsets[:, g * cols : (g + 1) * cols]))
+
+        def round_queries(qt):
+            q_bf[qt] = tile([P, P, PACK], BF16, "q_bf%d" % qt)
+            nc.scalar.copy(q_bf[qt][:], q_raw[:, :, qt * P : (qt + 1) * P].rearrange("p j q -> p q j"))
+
+        def quantize_queries(qt):
+            q_codes[qt] = tile([P, P], U32, "q_codes%d" % qt)
+            q_scales[qt] = tile([P, P], U8, "q_scales%d" % qt)
+            nc.vector.quantize_mx(
+                out=q_codes[qt][:].bitcast(FP8X4), scales=q_scales[qt][:], in_=q_bf[qt][:].rearrange("p q j -> p (q j)")
+            )
+
         def score(qt, g):
-            scores[qt, g] = bank([P, PASS], 2 * g + qt, "scores%d_%d" % (qt, g))
+            scores[qt, g] = bank([P, PASS], 2 * qt + g, "scores%d_%d" % (qt, g))
             nc.tensor.matmul_mx(
                 out=scores[qt, g][:],
-                lhsT=q_codes[:, qt * P : (qt + 1) * P].bitcast(FP8X4),
-                lhsT_scale=q_scales[:, qt * P : (qt + 1) * P],
+                lhsT=q_codes[qt][:].bitcast(FP8X4),
+                lhsT_scale=q_scales[qt][:],
                 rhs=key_words[g][:].bitcast(FP4X4),
-                rhs_scale=key_scales[:, g * PASS : (g + 1) * PASS],
+                rhs_scale=key_scales[g][:],
                 start=True,
                 stop=True,
             )
 
         def maxima(qt, g):
+            if g == 0:
+                best[qt] = tile([P, G], F32, "best%d" % qt)
             nc.vector.tensor_reduce(
-                best[:, qt, g * per : (g + 1) * per],
+                best[qt][:, g * per : (g + 1) * per],
                 scores[qt, g][:].rearrange("p (s i) -> p s i", i=RUN),
                 AXIS_X,
                 ALU.max,
             )
 
-        def top(qt, g):
-            neg_top[qt, g] = tile([P, 1], F32, "neg_top%d_%d" % (qt, g))
-            nc.vector.tensor_reduce(neg_top[qt, g][:], best[:, qt, g * per : (g + 1) * per], AXIS_X, ALU.max, negate=True)
+        def top(qt):
+            neg_top[qt] = tile([P, 1], F32, "neg_top%d" % qt)
+            nc.vector.tensor_reduce(neg_top[qt][:], best[qt][:], AXIS_X, ALU.max, negate=True)
 
         def exps(qt, g):
             probs[qt, g] = tile([P, PACK, P], F32, "probs%d_%d" % (qt, g))
@@ -92,10 +110,12 @@ def tile_attend_docmix_pl_kernel(tc, query, keys_words, keys_scales, size, vals,
                 probs[qt, g][:],
                 scores[qt, g][:].rearrange("q (p t) -> q t p", t=PACK),
                 ACT.Exp,
-                bias=neg_top[qt, g][:],
+                bias=neg_top[qt][:],
             )
 
         def quarter_sums(qt, g):
+            if g == 0:
+                partial[qt] = bank([P, PASSES, P], 4 + qt, "partial%d" % qt)
             for t in range(PACK):
                 nc.tensor.matmul(
                     out=partial[qt][:, g, :],
@@ -106,6 +126,39 @@ def tile_attend_docmix_pl_kernel(tc, query, keys_words, keys_scales, size, vals,
                     is_transpose=True,
                 )
 
+        def shares(qt):
+            share[qt] = tile([P, G], F32, "share%d" % qt)
+            sums[qt] = tile([P, G + 1], F32, "sums%d" % qt)
+            nc.scalar.activation(share[qt][:], best[qt][:], ACT.Exp, bias=neg_top[qt][:], accum_out=sums[qt][:, G : G + 1])
+
+        def passage_sums(qt):
+            partial_sb = tile([P, PASSES, P], F32, "partial_sb%d" % qt)
+            nc.scalar.activation(partial_sb[:], partial[qt][:], ACT.Copy, bias=TINY)
+            back = bank([P, PASSES, P], 2 * qt, "back%d" % qt)
+            for g in range(PASSES):
+                nc.tensor.transpose(back[:, g, :], partial_sb[:, g, :], ident[:])
+            nc.vector.tensor_reduce(sums[qt][:, 0:G], back[:].rearrange("p g (s c) -> p (g s) c", c=4), AXIS_X, ALU.add)
+
+        def invert(qt):
+            inverse[qt] = tile([P, G + 1], F32, "inverse%d" % qt)
+            nc.vector.reciprocal(inverse[qt][:], sums[qt][:])
+
+        def factors(qt):
+            factor = tile([P, G, 4], F32, "factor%d" % qt)
+            nc.vector.scalar_tensor_tensor(
+                factor[:],
+                inverse[qt][:, 0:G].unsqueeze(2).to_broadcast([P, G, 4]),
+                inverse[qt][:, G : G + 1],
+                share[qt][:].unsqueeze(2).to_broadcast([P, G, 4]),
+                ALU.mult,
+                ALU.mult,
+            )
+            f_turned[qt] = bank([P, PASSES, P], 2 * qt + 1, "f_turned%d" % qt)
+            for g in range(PASSES):
+                nc.tensor.transpose(
+                    f_turned[qt][:, g, :], factor[:, g * per : (g + 1) * per, :].rearrange("p s c -> p (s c)"), ident[:]
+                )
+
         def turn_probs(g, half, number):
             p_turned[g, half] = bank([P, 2, Q], number, "p_turned%d_%d" % (g, half))
             for qt in range(QTILES):
@@ -113,13 +166,18 @@ def tile_attend_docmix_pl_kernel(tc, query, keys_words, keys_scales, size, vals,
                     nc.tensor.transpose(p_turned[g, half][:, u, qt * P : (qt + 1) * P], probs[qt, g][:, 2 * half + u, :], ident[:])
 
         def times_size(g, t):
+            if t == 0:
+                sized[g] = tile([P, PACK, Q], F32, "sized%d" % g)
             nc.scalar.activation(
                 sized[g][:, t, :], p_turned[g, t // 2][:, t % 2, :], ACT.Copy, scale=size_cols[:, g, t : t + 1]
             )
 
-        def gather_values(t):
-            picked[t] = tile([P, I], BF16, "picked%d" % t)
-            nc.vector.tensor_copy(picked[t][:], windows[t][:].indirect(offsets[:]))
+        def gather_values(t, tag=None):
+            picked[t] = tile([P, I], BF16, "picked%d" % t, tag)
+            if t == 0:
+                nc.scalar.activation(picked[t][:], windows[t][:].indirect(offsets[:]), ACT.Copy)
+            else:
+                nc.vector.tensor_copy(picked[t][:], windows[t][:].indirect(offsets[:]))
 
         def turn_values(t, number):
             v_turned[t] = bank([P, PASSES, 2, P], number, "v_turned%d" % t)
@@ -142,41 +200,32 @@ def tile_attend_docmix_pl_kernel(tc, query, keys_words, keys_scales, size, vals,
                 v_codes[t, g] = codes[:, g * P : (g + 1) * P]
                 v_scales[t, g] = scales[:, g * P : (g + 1) * P]
 
-        def weights(g, first, last):
-            name = "%d_%d" % (g, first)
-            width = (last - first) * P
-            span = slice(first * P, last * P)
-            rounded = tile([P, width, PACK], BF16, "w_bf" + name)
+        def weights(qt, g, tag=None):
+            w_bf[qt, g] = tile([P, P, PACK], BF16, "w_bf%d_%d" % (qt, g), tag)
             nc.vector.tensor_tensor(
-                rounded[:],
-                sized[g][:, :, span].rearrange("p t q -> p q t"),
-                f_turned[:, g, span].unsqueeze(2).to_broadcast([P, width, PACK]),
+                w_bf[qt, g][:],
+                sized[g][:, :, qt * P : (qt + 1) * P].rearrange("p t q -> p q t"),
+                f_turned[qt][:, g, :].unsqueeze(2).to_broadcast([P, P, PACK]),
                 ALU.mult,
             )
-            w_bf[g, first] = rounded
 
-        def quantize_weights(g, first, last):
-            name = "%d_%d" % (g, first)
-            width = (last - first) * P
-            codes = tile([P, width], U32, "w_codes" + name)
-            scales = tile([P, width], U8, "w_scales" + name)
+        def quantize_weights(qt, g):
+            w_codes[qt, g] = tile([P, P], U32, "w_codes%d_%d" % (qt, g))
+            w_scales[qt, g] = tile([P, P], U8, "w_scales%d_%d" % (qt, g))
             nc.vector.quantize_mx(
-                out=codes[:].bitcast(FP8X4), scales=scales[:], in_=w_bf[g, first][:].rearrange("p q t -> p (q t)")
+                out=w_codes[qt, g][:].bitcast(FP8X4), scales=w_scales[qt, g][:], in_=w_bf[qt, g][:].rearrange("p q t -> p (q t)")
             )
-            for qt in range(first, last):
-                w_codes[g, qt] = codes[:, (qt - first) * P : (qt - first + 1) * P]
-                w_scales[g, qt] = scales[:, (qt - first) * P : (qt - first + 1) * P]
 
         def product(qt, pair, g):
             if g == 0:
-                acc[qt, pair] = bank([P, 2, P], (2, 3, 1, 5)[2 * qt + pair], "acc%d_%d" % (qt, pair))
+                acc[qt, pair] = bank([P, 2, P], (4, 6, 5, 0)[2 * qt + pair], "acc%d_%d" % (qt, pair))
             for h in range(2):
                 nc.tensor.matmul_mx(
                     out=acc[qt, pair][:, h, :],
                     lhsT=v_codes[2 * pair + h, g].bitcast(FP8X4),
                     lhsT_scale=v_scales[2 * pair + h, g],
-                    rhs=w_codes[g, qt].bitcast(FP8X4),
-                    rhs_scale=w_scales[g, qt],
+                    rhs=w_codes[qt, g][:].bitcast(FP8X4),
+                    rhs_scale=w_scales[qt, g][:],
                     start=(g == 0 and h == 0),
                     stop=(g == PASSES - 1 and h == 1),
                 )
@@ -193,13 +242,10 @@ def tile_attend_docmix_pl_kernel(tc, query, keys_words, keys_scales, size, vals,
         def store_y(qt):
             nc.sync.dma_start(out_rows[:, :, qt * P : (qt + 1) * P], y[qt][:])
 
-        def round_y(qt, first, last, on_vector):
+        def round_y(qt, first, last):
             dst = y_bf[qt][:, first:last, :].rearrange("p (c i) t -> p c t i", i=4)
             src = y[qt][:, :, first:last].rearrange("p t (c i) -> p c t i", i=4)
-            if on_vector:
-                nc.vector.tensor_copy(dst, src)
-            else:
-                nc.scalar.copy(dst, src)
+            nc.vector.tensor_copy(dst, src)
 
         def quantize_y(qt, first, last):
             nc.vector.quantize_mx(
@@ -208,152 +254,111 @@ def tile_attend_docmix_pl_kernel(tc, query, keys_words, keys_scales, size, vals,
                 in_=y_bf[qt][:, first:last, :].rearrange("p q t -> p (q t)"),
             )
 
-        def store_codes(qt, queue):
+        def store_codes(qt):
             words = out_1[0].rearrange("p q t -> p (q t)").bitcast(I32)
-            queue.dma_start(words[:, qt * P : (qt + 1) * P], y_codes[qt][:].bitcast(I32))
+            nc.sync.dma_start(words[:, qt * P : (qt + 1) * P], y_codes[qt][:].bitcast(I32))
 
         nc.gpsimd.memset(scale_pool[:].bitcast(I32), 0)
         nc.sync.dma_start(offsets[:], offs)
-        make_identity(nc, ident[:])
+        nc.sync.dma_start(key_pool[:].bitcast(I32), keys_words[0].bitcast(I32))
         for quad in range(4):
-            nc.sync.dma_start(
+            nc.scalar.dma_start(
                 scale_pool[32 * quad : 32 * quad + 4, :].bitcast(I32),
                 keys_scales[0, 4 * quad : 4 * quad + 4, :].bitcast(I32),
             )
-        nc.sync.dma_start(key_pool[:].bitcast(I32), keys_words[0].bitcast(I32))
         nc.sync.dma_start(q_raw[:], query.rearrange("(p j) q -> p j q", j=PACK))
-        nc.sync.dma_start(size_cols[:], size.rearrange("o (g p t) -> (o p) g t", p=P, t=PACK))
-        for t in range(PACK):
-            load_vals(t)
+        for c in range(2):
+            v_raw[c] = tile([P, HALF], F32, "v_raw%d" % c)
+            nc.sync.dma_start(v_raw[c][:], vals_rows[:, 0, c * HALF : (c + 1) * HALF])
+        make_identity(nc, ident[:])
 
-        key_scales = tile([P, I], U8, "key_scales")
-        nc.vector.tensor_copy(key_scales[:], scale_pool[:].indirect(offsets[:]))
-        gather_words(0, None)
-        q_bf = tile([P, Q, PACK], BF16, "q_bf")
-        q_codes = tile([P, Q], U32, "q_codes")
-        q_scales = tile([P, Q], U8, "q_scales")
-        nc.scalar.copy(q_bf[:], q_raw[:].rearrange("p j q -> p q j"))
-        nc.vector.quantize_mx(out=q_codes[:].bitcast(FP8X4), scales=q_scales[:], in_=q_bf[:].rearrange("p q j -> p (q j)"))
-        gather_words(1, "q_raw")
-
-        best = tile([P, QTILES, G], F32, "best")
-        for g in range(PASSES):
-            for qt in range(QTILES):
-                score(qt, g)
-        for g in range(PASSES):
-            for qt in range(QTILES):
-                maxima(qt, g)
-                top(qt, g)
-        neg_all = tile([P, QTILES], F32, "neg_all")
-        nc.vector.tensor_reduce(neg_all[:], best[:], AXIS_X, ALU.max, negate=True)
-
-        partial, share, sums = {}, {}, {}
+        gather_words(0)
+        gather_words(1)
+        load_window(1, "key_pool")
         for qt in range(QTILES):
-            partial[qt] = bank([P, PASSES, P], 4 + qt, "partial%d" % qt)
-        for g in range(PASSES):
-            for qt in range(QTILES):
+            round_queries(qt)
+        load_window(2, "q_raw")
+        for half in range(2):
+            gather_scales(half)
+            quantize_queries(half)
+        load_window(3, "scale_pool")
+        size_cols = tile([P, PASSES, PACK], F32, "size_cols", "q_bf0")
+        nc.sync.dma_start(size_cols[:], size.rearrange("o (g p t) -> (o p) g t", p=P, t=PACK))
+
+        windows[0] = tile([P, T], BF16, "window0")
+        for c in range(2):
+            nc.scalar.activation(windows[0][:, c * HALF : (c + 1) * HALF], v_raw[c][:], ACT.Copy)
+
+        for qt in range(QTILES):
+            for g in range(PASSES):
+                score(qt, g)
+        for qt in range(QTILES):
+            for g in range(PASSES):
+                maxima(qt, g)
+            top(qt)
+        for qt in range(QTILES):
+            for g in range(PASSES):
                 exps(qt, g)
                 quarter_sums(qt, g)
+            shares(qt)
+        gather_values(1)
         for qt in range(QTILES):
-            share[qt] = tile([P, G], F32, "share%d" % qt)
-            sums[qt] = tile([P, G + 1], F32, "sums%d" % qt)
-            nc.scalar.activation(share[qt][:], best[:, qt, :], ACT.Exp, bias=neg_all[:, qt : qt + 1], accum_out=sums[qt][:, G : G + 1])
-        for g in range(PASSES):
-            sized[g] = tile([P, PACK, Q], F32, "sized%d" % g)
-
-        for t in range(2):
-            gather_values(t)
-            turn_values(t, 6 + t)
-            copy_values(t)
-
-        f_turned = bank([P, PASSES, Q], 0, "f_turned")
-        inverse = {}
+            passage_sums(qt)
+        gather_values(0, "neg_top1")
         for qt in range(QTILES):
-            partial_sb = tile([P, PASSES, P], F32, "partial_sb%d" % qt)
-            nc.scalar.activation(partial_sb[:], partial[qt][:], ACT.Copy, bias=TINY)
-            back = bank([P, PASSES, P], 2 + qt, "back%d" % qt)
-            for g in range(PASSES):
-                nc.tensor.transpose(back[:, g, :], partial_sb[:, g, :], ident[:])
-            nc.vector.tensor_reduce(sums[qt][:, 0:G], back[:].rearrange("p g (s c) -> p (g s) c", c=4), AXIS_X, ALU.add)
-        for qt in range(QTILES):
-            inverse[qt] = tile([P, G + 1], F32, "inverse%d" % qt)
-            nc.vector.reciprocal(inverse[qt][:], sums[qt][:])
-        for qt in range(QTILES):
-            factor = tile([P, G, 4], F32, "factor%d" % qt)
-            nc.vector.scalar_tensor_tensor(
-                factor[:],
-                inverse[qt][:, 0:G].unsqueeze(2).to_broadcast([P, G, 4]),
-                inverse[qt][:, G : G + 1],
-                share[qt][:].unsqueeze(2).to_broadcast([P, G, 4]),
-                ALU.mult,
-                ALU.mult,
-            )
-            for g in range(PASSES):
-                nc.tensor.transpose(
-                    f_turned[:, g, qt * P : (qt + 1) * P],
-                    factor[:, g * per : (g + 1) * per, :].rearrange("p s c -> p (s c)"),
-                    ident[:],
-                )
-        turn_probs(0, 0, 2)
-        turn_probs(0, 1, 3)
-        turn_probs(1, 0, 5)
-        turn_probs(1, 1, 6)
+            invert(qt)
+            factors(qt)
         gather_values(2)
-        gather_values(3)
+        turn_probs(0, 0, 6)
+        turn_probs(0, 1, 7)
+        turn_probs(1, 0, 4)
+        turn_probs(1, 1, 5)
+        turn_values(1, 0)
         for t in range(PACK):
             times_size(0, t)
-        turn_values(2, 1)
-        turn_values(3, 4)
-        copy_values(2)
+        copy_values(1)
+        turn_values(0, 2)
+        turn_values(2, 6)
         for t in range(PACK):
             times_size(1, t)
-        idle = bank([P, PASS], 7, "idle")
-        for qt in range(QTILES):
-            nc.tensor.matmul_mx(
-                out=idle[:],
-                lhsT=q_codes[:, qt * P : (qt + 1) * P].bitcast(FP8X4),
-                lhsT_scale=q_scales[:, qt * P : (qt + 1) * P],
-                rhs=key_words[0][:].bitcast(FP4X4),
-                rhs_scale=key_scales[:, 0:PASS],
-                start=True,
-                stop=True,
-            )
-        copy_values(3)
+        gather_values(3)
+        turn_values(3, 7)
+        for t in (0, 2, 3):
+            copy_values(t)
 
-        quantize_values(0)
+        weights(0, 0)
+        weights(0, 1)
         quantize_values(1)
-        weights(0, 0, QTILES)
+        quantize_weights(0, 0)
+        quantize_weights(0, 1)
+        weights(1, 0, "scale_pool")
+        quantize_values(0)
         quantize_values(2)
-        quantize_weights(0, 0, QTILES)
-        weights(1, 0, 1)
+        quantize_weights(1, 0)
+        weights(1, 1)
         quantize_values(3)
-        quantize_weights(1, 0, 1)
-        weights(1, 1, 2)
-        quantize_weights(1, 1, 2)
+        quantize_weights(1, 1)
         y_scales = tile([P, Q], U8, "y_scales")
-        for qt in range(QTILES):
-            for pair in range(PAIRS):
-                product(qt, pair, 0)
-        y_codes = {}
         for qt in range(QTILES):
             y_bf[qt] = tile([P, P, PACK], BF16, "y_bf%d" % qt)
             y_codes[qt] = tile([P, P], U32, "y_codes%d" % qt)
-            for pair in range(PAIRS):
-                product(qt, pair, 1)
+            for g in range(PASSES):
+                for pair in range(PAIRS):
+                    product(qt, pair, g)
         copy_y(0, 0, False)
         copy_y(0, 1, False)
         store_y(0)
-        round_y(0, 0, P, True)
+        round_y(0, 0, P)
         copy_y(1, 0, False)
         copy_y(1, 1, True)
         store_y(1)
         quantize_y(0, 0, P)
-        store_codes(0, nc.sync)
+        store_codes(0)
         for half in range(2):
-            round_y(1, half * P // 2, (half + 1) * P // 2, True)
+            round_y(1, half * P // 2, (half + 1) * P // 2)
         for half in range(2):
             quantize_y(1, half * P // 2, (half + 1) * P // 2)
-        store_codes(1, nc.sync)
+        store_codes(1)
         for quad in range(4):
             queue = nc.scalar if quad % 2 == 0 else nc.sync
             queue.dma_start(

@@ -25,7 +25,6 @@ RUN = I // G
 PASSES = I // PASS
 QTILES = Q // P
 PAIRS = 2
-HALF = T // 2
 TINY = 1e-30
 
 
@@ -50,12 +49,12 @@ def tile_attend_docmix_pl_kernel(tc, query, keys_words, keys_scales, size, vals,
         ident = tile([P, P], F32, "ident")
         vals_rows = vals.rearrange("(p t) n -> p t n", t=PACK)
         out_rows = out_0.rearrange("(p t) q -> p t q", t=PACK)
-        v_raw, windows, key_words, key_scales, scores, neg_top, probs = {}, {}, {}, {}, {}, {}, {}
+        windows, key_words, key_scales, scores, neg_top, probs = {}, {}, {}, {}, {}, {}
         q_bf, q_codes, q_scales, best, partial, share, sums, inverse, f_turned = {}, {}, {}, {}, {}, {}, {}, {}, {}
         picked, v_turned, v_bf, v_codes, v_scales = {}, {}, {}, {}, {}
         p_turned, sized, w_bf, w_codes, w_scales, acc, y, y_bf, y_codes = {}, {}, {}, {}, {}, {}, {}, {}, {}
 
-        def load_window(t, tag):
+        def load_window(t, tag=None):
             windows[t] = tile([P, T], F32, "window%d" % t, tag)
             nc.sync.dma_start(windows[t][:], vals_rows[:, t, :])
 
@@ -63,8 +62,8 @@ def tile_attend_docmix_pl_kernel(tc, query, keys_words, keys_scales, size, vals,
             key_words[g] = tile([P, PASS], U16, "key_words%d" % g)
             nc.vector.tensor_copy(key_words[g][:], key_pool[:].indirect(offsets[:, g * cols : (g + 1) * cols]))
 
-        def gather_scales(g):
-            key_scales[g] = tile([P, PASS], U8, "key_scales%d" % g)
+        def gather_scales(g, tag=None):
+            key_scales[g] = tile([P, PASS], U8, "key_scales%d" % g, tag)
             nc.vector.tensor_copy(key_scales[g][:], scale_pool[:].indirect(offsets[:, g * cols : (g + 1) * cols]))
 
         def round_queries(qt):
@@ -100,9 +99,9 @@ def tile_attend_docmix_pl_kernel(tc, query, keys_words, keys_scales, size, vals,
                 ALU.max,
             )
 
-        def top(qt):
-            neg_top[qt] = tile([P, 1], F32, "neg_top%d" % qt)
-            nc.vector.tensor_reduce(neg_top[qt][:], best[qt][:], AXIS_X, ALU.max, negate=True)
+        def top(qt, g):
+            neg_top[qt, g] = tile([P, 1], F32, "neg_top%d_%d" % (qt, g))
+            nc.vector.tensor_reduce(neg_top[qt, g][:], best[qt][:, 0 : (g + 1) * per], AXIS_X, ALU.max, negate=True)
 
         def exps(qt, g):
             probs[qt, g] = tile([P, PACK, P], F32, "probs%d_%d" % (qt, g))
@@ -110,7 +109,7 @@ def tile_attend_docmix_pl_kernel(tc, query, keys_words, keys_scales, size, vals,
                 probs[qt, g][:],
                 scores[qt, g][:].rearrange("q (p t) -> q t p", t=PACK),
                 ACT.Exp,
-                bias=neg_top[qt][:],
+                bias=neg_top[qt, g][:],
             )
 
         def quarter_sums(qt, g):
@@ -129,7 +128,7 @@ def tile_attend_docmix_pl_kernel(tc, query, keys_words, keys_scales, size, vals,
         def shares(qt):
             share[qt] = tile([P, G], F32, "share%d" % qt)
             sums[qt] = tile([P, G + 1], F32, "sums%d" % qt)
-            nc.scalar.activation(share[qt][:], best[qt][:], ACT.Exp, bias=neg_top[qt][:], accum_out=sums[qt][:, G : G + 1])
+            nc.scalar.activation(share[qt][:], best[qt][:], ACT.Exp, bias=neg_top[qt, PASSES - 1][:], accum_out=sums[qt][:, G : G + 1])
 
         def passage_sums(qt):
             partial_sb = tile([P, PASSES, P], F32, "partial_sb%d" % qt)
@@ -144,14 +143,11 @@ def tile_attend_docmix_pl_kernel(tc, query, keys_words, keys_scales, size, vals,
             nc.vector.reciprocal(inverse[qt][:], sums[qt][:])
 
         def factors(qt):
+            ratio = tile([P, G], F32, "ratio%d" % qt)
+            nc.vector.tensor_tensor(ratio[:], inverse[qt][:, 0:G], share[qt][:], ALU.mult)
             factor = tile([P, G, 4], F32, "factor%d" % qt)
-            nc.vector.scalar_tensor_tensor(
-                factor[:],
-                inverse[qt][:, 0:G].unsqueeze(2).to_broadcast([P, G, 4]),
-                inverse[qt][:, G : G + 1],
-                share[qt][:].unsqueeze(2).to_broadcast([P, G, 4]),
-                ALU.mult,
-                ALU.mult,
+            nc.scalar.activation(
+                factor[:], ratio[:].unsqueeze(2).to_broadcast([P, G, 4]), ACT.Copy, scale=inverse[qt][:, G : G + 1]
             )
             f_turned[qt] = bank([P, PASSES, P], 2 * qt + 1, "f_turned%d" % qt)
             for g in range(PASSES):
@@ -174,10 +170,7 @@ def tile_attend_docmix_pl_kernel(tc, query, keys_words, keys_scales, size, vals,
 
         def gather_values(t, tag=None):
             picked[t] = tile([P, I], BF16, "picked%d" % t, tag)
-            if t == 0:
-                nc.scalar.activation(picked[t][:], windows[t][:].indirect(offsets[:]), ACT.Copy)
-            else:
-                nc.vector.tensor_copy(picked[t][:], windows[t][:].indirect(offsets[:]))
+            nc.vector.tensor_copy(picked[t][:], windows[t][:].indirect(offsets[:]))
 
         def turn_values(t, number):
             v_turned[t] = bank([P, PASSES, 2, P], number, "v_turned%d" % t)
@@ -262,81 +255,71 @@ def tile_attend_docmix_pl_kernel(tc, query, keys_words, keys_scales, size, vals,
         nc.sync.dma_start(offsets[:], offs)
         nc.sync.dma_start(key_pool[:].bitcast(I32), keys_words[0].bitcast(I32))
         for quad in range(4):
-            nc.scalar.dma_start(
+            nc.sync.dma_start(
                 scale_pool[32 * quad : 32 * quad + 4, :].bitcast(I32),
                 keys_scales[0, 4 * quad : 4 * quad + 4, :].bitcast(I32),
             )
         nc.sync.dma_start(q_raw[:], query.rearrange("(p j) q -> p j q", j=PACK))
-        for c in range(2):
-            v_raw[c] = tile([P, HALF], F32, "v_raw%d" % c)
-            nc.sync.dma_start(v_raw[c][:], vals_rows[:, 0, c * HALF : (c + 1) * HALF])
+        size_cols = tile([P, PASSES, PACK], F32, "size_cols")
+        nc.sync.dma_start(size_cols[:], size.rearrange("o (g p t) -> (o p) g t", p=P, t=PACK))
+        for t in range(PACK):
+            load_window(t)
         make_identity(nc, ident[:])
 
         gather_words(0)
         gather_words(1)
-        load_window(1, "key_pool")
         for qt in range(QTILES):
             round_queries(qt)
-        load_window(2, "q_raw")
         for half in range(2):
             gather_scales(half)
-            quantize_queries(half)
-        load_window(3, "scale_pool")
-        size_cols = tile([P, PASSES, PACK], F32, "size_cols", "q_bf0")
-        nc.sync.dma_start(size_cols[:], size.rearrange("o (g p t) -> (o p) g t", p=P, t=PACK))
-
-        windows[0] = tile([P, T], BF16, "window0")
-        for c in range(2):
-            nc.scalar.activation(windows[0][:, c * HALF : (c + 1) * HALF], v_raw[c][:], ACT.Copy)
-
+        for qt in range(QTILES):
+            quantize_queries(qt)
         for qt in range(QTILES):
             for g in range(PASSES):
                 score(qt, g)
         for qt in range(QTILES):
             for g in range(PASSES):
                 maxima(qt, g)
-            top(qt)
+                top(qt, g)
         for qt in range(QTILES):
             for g in range(PASSES):
                 exps(qt, g)
                 quarter_sums(qt, g)
             shares(qt)
-        gather_values(1)
+        gather_values(0, "q_codes1")
         for qt in range(QTILES):
             passage_sums(qt)
-        gather_values(0, "neg_top1")
         for qt in range(QTILES):
             invert(qt)
             factors(qt)
+        gather_values(1)
         gather_values(2)
         turn_probs(0, 0, 6)
         turn_probs(0, 1, 7)
-        turn_probs(1, 0, 4)
-        turn_probs(1, 1, 5)
-        turn_values(1, 0)
         for t in range(PACK):
             times_size(0, t)
-        copy_values(1)
-        turn_values(0, 2)
-        turn_values(2, 6)
+        turn_probs(1, 0, 4)
+        turn_probs(1, 1, 5)
         for t in range(PACK):
             times_size(1, t)
         gather_values(3)
+        turn_values(0, 0)
+        turn_values(1, 2)
+        turn_values(2, 6)
         turn_values(3, 7)
-        for t in (0, 2, 3):
+        for t in range(PACK):
             copy_values(t)
 
         weights(0, 0)
         weights(0, 1)
-        quantize_values(1)
+        for t in range(PACK - 1):
+            quantize_values(t)
         quantize_weights(0, 0)
         quantize_weights(0, 1)
-        weights(1, 0, "scale_pool")
-        quantize_values(0)
-        quantize_values(2)
+        weights(1, 0, "window3")
+        quantize_values(PACK - 1)
         quantize_weights(1, 0)
-        weights(1, 1)
-        quantize_values(3)
+        weights(1, 1, "v_bf3")
         quantize_weights(1, 1)
         y_scales = tile([P, Q], U8, "y_scales")
         for qt in range(QTILES):

@@ -68,7 +68,10 @@ def tile_attend_docmix_pl_kernel(tc, query, keys_words, keys_scales, size, vals,
 
         def round_queries(qt):
             q_bf[qt] = tile([P, P, PACK], BF16, "q_bf%d" % qt)
-            nc.scalar.copy(q_bf[qt][:], q_raw[:, :, qt * P : (qt + 1) * P].rearrange("p j q -> p q j"))
+            nc.scalar.copy(
+                q_bf[qt][:].rearrange("p (c i) j -> p c j i", i=4),
+                q_raw[:, :, qt * P : (qt + 1) * P].rearrange("p j (c i) -> p c j i", i=4),
+            )
 
         def quantize_queries(qt):
             q_codes[qt] = tile([P, P], U32, "q_codes%d" % qt)
@@ -196,9 +199,9 @@ def tile_attend_docmix_pl_kernel(tc, query, keys_words, keys_scales, size, vals,
         def weights(qt, g, tag=None):
             w_bf[qt, g] = tile([P, P, PACK], BF16, "w_bf%d_%d" % (qt, g), tag)
             nc.vector.tensor_tensor(
-                w_bf[qt, g][:],
-                sized[g][:, :, qt * P : (qt + 1) * P].rearrange("p t q -> p q t"),
-                f_turned[qt][:, g, :].unsqueeze(2).to_broadcast([P, P, PACK]),
+                w_bf[qt, g][:].rearrange("p (c i) t -> p c t i", i=4),
+                sized[g][:, :, qt * P : (qt + 1) * P].rearrange("p t (c i) -> p c t i", i=4),
+                f_turned[qt][:, g, :].rearrange("p (c i) -> p c i", i=4).unsqueeze(2).to_broadcast([P, P // 4, PACK, 4]),
                 ALU.mult,
             )
 

@@ -25,6 +25,7 @@ RUN = I // G
 PASSES = I // PASS
 QTILES = Q // P
 PAIRS = 2
+LINE = 4
 TINY = 1e-30
 
 
@@ -47,30 +48,34 @@ def tile_attend_docmix_pl_kernel(tc, query, keys_words, keys_scales, size, vals,
         scale_pool = tile([P, T], U8, "scale_pool")
         q_raw = tile([P, PACK, Q], F32, "q_raw")
         ident = tile([P, P], F32, "ident")
+        ident_sums = tile([P, P], F32, "ident_sums")
+        size_cols = tile([P, PASSES, PACK], F32, "size_cols")
+        y_scales = tile([P, Q], U8, "y_scales")
         vals_rows = vals.rearrange("(p t) n -> p t n", t=PACK)
         out_rows = out_0.rearrange("(p t) q -> p t q", t=PACK)
         windows, key_words, key_scales, scores, neg_top, probs = {}, {}, {}, {}, {}, {}
-        q_bf, q_codes, q_scales, best, partial, share, sums, inverse, f_turned = {}, {}, {}, {}, {}, {}, {}, {}, {}
+        q_bf, q_codes, q_scales, best, share, sums, inverse, ratio, f_turned = {}, {}, {}, {}, {}, {}, {}, {}, {}
+        partial, back = {}, {}
         picked, v_turned, v_bf, v_codes, v_scales = {}, {}, {}, {}, {}
         p_turned, sized, w_bf, w_codes, w_scales, acc, y, y_bf, y_codes = {}, {}, {}, {}, {}, {}, {}, {}, {}
 
-        def load_window(t, tag=None):
-            windows[t] = tile([P, T], F32, "window%d" % t, tag)
+        def load_window(t):
+            windows[t] = tile([P, T], F32, "window%d" % t)
             nc.sync.dma_start(windows[t][:], vals_rows[:, t, :])
 
         def gather_words(g):
             key_words[g] = tile([P, PASS], U16, "key_words%d" % g)
             nc.vector.tensor_copy(key_words[g][:], key_pool[:].indirect(offsets[:, g * cols : (g + 1) * cols]))
 
-        def gather_scales(g, tag=None):
-            key_scales[g] = tile([P, PASS], U8, "key_scales%d" % g, tag)
+        def gather_scales(g):
+            key_scales[g] = tile([P, PASS], U8, "key_scales%d" % g)
             nc.vector.tensor_copy(key_scales[g][:], scale_pool[:].indirect(offsets[:, g * cols : (g + 1) * cols]))
 
         def round_queries(qt):
             q_bf[qt] = tile([P, P, PACK], BF16, "q_bf%d" % qt)
             nc.scalar.copy(
-                q_bf[qt][:].rearrange("p (c i) j -> p c j i", i=4),
-                q_raw[:, :, qt * P : (qt + 1) * P].rearrange("p j (c i) -> p c j i", i=4),
+                q_bf[qt][:].rearrange("p (c i) j -> p c j i", i=LINE),
+                q_raw[:, :, qt * P : (qt + 1) * P].rearrange("p j (c i) -> p c j i", i=LINE),
             )
 
         def quantize_queries(qt):
@@ -115,6 +120,11 @@ def tile_attend_docmix_pl_kernel(tc, query, keys_words, keys_scales, size, vals,
                 bias=neg_top[qt, g][:],
             )
 
+        def shares(qt):
+            share[qt] = tile([P, G], F32, "share%d" % qt)
+            sums[qt] = tile([P, G + 1], F32, "sums%d" % qt)
+            nc.scalar.activation(share[qt][:], best[qt][:], ACT.Exp, bias=neg_top[qt, PASSES - 1][:], accum_out=sums[qt][:, G : G + 1])
+
         def quarter_sums(qt, g):
             if g == 0:
                 partial[qt] = bank([P, PASSES, P], 4 + qt, "partial%d" % qt)
@@ -122,37 +132,39 @@ def tile_attend_docmix_pl_kernel(tc, query, keys_words, keys_scales, size, vals,
                 nc.tensor.matmul(
                     out=partial[qt][:, g, :],
                     lhsT=probs[qt, g][:, t, :],
-                    rhs=ident[:],
+                    rhs=ident_sums[:],
                     start=(t == 0),
                     stop=(t == PACK - 1),
                     is_transpose=True,
                 )
 
-        def shares(qt):
-            share[qt] = tile([P, G], F32, "share%d" % qt)
-            sums[qt] = tile([P, G + 1], F32, "sums%d" % qt)
-            nc.scalar.activation(share[qt][:], best[qt][:], ACT.Exp, bias=neg_top[qt, PASSES - 1][:], accum_out=sums[qt][:, G : G + 1])
-
-        def passage_sums(qt):
+        def turn_sums_back(qt):
             partial_sb = tile([P, PASSES, P], F32, "partial_sb%d" % qt)
             nc.scalar.activation(partial_sb[:], partial[qt][:], ACT.Copy, bias=TINY)
-            back = bank([P, PASSES, P], 2 * qt, "back%d" % qt)
+            back[qt] = bank([P, PASSES, P], 2 * qt, "back%d" % qt)
             for g in range(PASSES):
-                nc.tensor.transpose(back[:, g, :], partial_sb[:, g, :], ident[:])
-            nc.vector.tensor_reduce(sums[qt][:, 0:G], back[:].rearrange("p g (s c) -> p (g s) c", c=4), AXIS_X, ALU.add)
+                nc.tensor.transpose(back[qt][:, g, :], partial_sb[:, g, :], ident[:])
 
-        def invert(qt):
-            inverse[qt] = tile([P, G + 1], F32, "inverse%d" % qt)
+        def passage_sums(qt):
+            nc.vector.tensor_reduce(
+                sums[qt][:, 0:G], back[qt][:].rearrange("p g (s c) -> p (g s) c", c=RUN // PACK), AXIS_X, ALU.add
+            )
+
+        def invert(qt, tag=None):
+            inverse[qt] = tile([P, G + 1], F32, "inverse%d" % qt, tag)
             nc.vector.reciprocal(inverse[qt][:], sums[qt][:])
 
-        def factors(qt):
-            ratio = tile([P, G], F32, "ratio%d" % qt)
-            nc.vector.tensor_tensor(ratio[:], inverse[qt][:, 0:G], share[qt][:], ALU.mult)
-            factor = tile([P, G, 4], F32, "factor%d" % qt)
+        def ratios(qt):
+            ratio[qt] = tile([P, G], F32, "ratio%d" % qt)
+            nc.vector.tensor_tensor(ratio[qt][:], inverse[qt][:, 0:G], share[qt][:], ALU.mult)
+
+        def factors(qt, number):
+            spread = RUN // PACK
+            factor = tile([P, G, spread], F32, "factor%d" % qt)
             nc.scalar.activation(
-                factor[:], ratio[:].unsqueeze(2).to_broadcast([P, G, 4]), ACT.Copy, scale=inverse[qt][:, G : G + 1]
+                factor[:], ratio[qt][:].unsqueeze(2).to_broadcast([P, G, spread]), ACT.Copy, scale=inverse[qt][:, G : G + 1]
             )
-            f_turned[qt] = bank([P, PASSES, P], 2 * qt + 1, "f_turned%d" % qt)
+            f_turned[qt] = bank([P, PASSES, P], number, "f_turned%d" % qt)
             for g in range(PASSES):
                 nc.tensor.transpose(
                     f_turned[qt][:, g, :], factor[:, g * per : (g + 1) * per, :].rearrange("p s c -> p (s c)"), ident[:]
@@ -164,23 +176,27 @@ def tile_attend_docmix_pl_kernel(tc, query, keys_words, keys_scales, size, vals,
                 for u in range(2):
                     nc.tensor.transpose(p_turned[g, half][:, u, qt * P : (qt + 1) * P], probs[qt, g][:, 2 * half + u, :], ident[:])
 
-        def times_size(g, t):
-            if t == 0:
-                sized[g] = tile([P, PACK, Q], F32, "sized%d" % g)
-            nc.scalar.activation(
-                sized[g][:, t, :], p_turned[g, t // 2][:, t % 2, :], ACT.Copy, scale=size_cols[:, g, t : t + 1]
-            )
+        def times_size(g):
+            sized[g] = tile([P, PACK, Q], F32, "sized%d" % g)
+            for t in range(PACK):
+                nc.scalar.activation(
+                    sized[g][:, t, :], p_turned[g, t // 2][:, t % 2, :], ACT.Copy, scale=size_cols[:, g, t : t + 1]
+                )
 
-        def gather_values(t, tag=None):
-            picked[t] = tile([P, I], BF16, "picked%d" % t, tag)
-            nc.vector.tensor_copy(picked[t][:], windows[t][:].indirect(offsets[:]))
+        def gather_values(t, g, on_vector, tag=None):
+            picked[t, g] = tile([P, PASS], BF16, "picked%d_%d" % (t, g), tag)
+            listed = windows[t][:].indirect(offsets[:, g * cols : (g + 1) * cols])
+            if on_vector:
+                nc.vector.tensor_copy(picked[t, g][:], listed)
+            else:
+                nc.scalar.activation(picked[t, g][:], listed, ACT.Copy)
 
         def turn_values(t, number):
             v_turned[t] = bank([P, PASSES, 2, P], number, "v_turned%d" % t)
-            words = picked[t][:].bitcast(F32)
             for g in range(PASSES):
+                words = picked[t, g][:].bitcast(F32)
                 for u in range(2):
-                    nc.tensor.transpose(v_turned[t][:, g, u, :], words[:, 2 * P * g + u : 2 * P * (g + 1) : 2], ident[:])
+                    nc.tensor.transpose(v_turned[t][:, g, u, :], words[:, u : 2 * P : 2], ident[:])
 
         def copy_values(t):
             v_bf[t] = tile([P, PASSES, P, 2], F32, "v_bf%d" % t)
@@ -199,9 +215,9 @@ def tile_attend_docmix_pl_kernel(tc, query, keys_words, keys_scales, size, vals,
         def weights(qt, g, tag=None):
             w_bf[qt, g] = tile([P, P, PACK], BF16, "w_bf%d_%d" % (qt, g), tag)
             nc.vector.tensor_tensor(
-                w_bf[qt, g][:].rearrange("p (c i) t -> p c t i", i=4),
-                sized[g][:, :, qt * P : (qt + 1) * P].rearrange("p t (c i) -> p c t i", i=4),
-                f_turned[qt][:, g, :].rearrange("p (c i) -> p c i", i=4).unsqueeze(2).to_broadcast([P, P // 4, PACK, 4]),
+                w_bf[qt, g][:].rearrange("p (c i) t -> p c t i", i=LINE),
+                sized[g][:, :, qt * P : (qt + 1) * P].rearrange("p t (c i) -> p c t i", i=LINE),
+                f_turned[qt][:, g, :].rearrange("p (c i) -> p c i", i=LINE).unsqueeze(2).to_broadcast([P, P // LINE, PACK, LINE]),
                 ALU.mult,
             )
 
@@ -212,18 +228,17 @@ def tile_attend_docmix_pl_kernel(tc, query, keys_words, keys_scales, size, vals,
                 out=w_codes[qt, g][:].bitcast(FP8X4), scales=w_scales[qt, g][:], in_=w_bf[qt, g][:].rearrange("p q t -> p (q t)")
             )
 
-        def product(qt, pair, g):
-            if g == 0:
-                acc[qt, pair] = bank([P, 2, P], (4, 6, 5, 0)[2 * qt + pair], "acc%d_%d" % (qt, pair))
-            for h in range(2):
+        def product(qt, pair, number, steps):
+            acc[qt, pair] = bank([P, 2, P], number, "acc%d_%d" % (qt, pair))
+            for h, g in steps:
                 nc.tensor.matmul_mx(
                     out=acc[qt, pair][:, h, :],
                     lhsT=v_codes[2 * pair + h, g].bitcast(FP8X4),
                     lhsT_scale=v_scales[2 * pair + h, g],
                     rhs=w_codes[qt, g][:].bitcast(FP8X4),
                     rhs_scale=w_scales[qt, g][:],
-                    start=(g == 0 and h == 0),
-                    stop=(g == PASSES - 1 and h == 1),
+                    start=((h, g) == steps[0]),
+                    stop=((h, g) == steps[-1]),
                 )
 
         def copy_y(qt, pair, on_vector):
@@ -239,11 +254,15 @@ def tile_attend_docmix_pl_kernel(tc, query, keys_words, keys_scales, size, vals,
             nc.sync.dma_start(out_rows[:, :, qt * P : (qt + 1) * P], y[qt][:])
 
         def round_y(qt, first, last):
-            dst = y_bf[qt][:, first:last, :].rearrange("p (c i) t -> p c t i", i=4)
-            src = y[qt][:, :, first:last].rearrange("p t (c i) -> p c t i", i=4)
+            if first == 0:
+                y_bf[qt] = tile([P, P, PACK], BF16, "y_bf%d" % qt)
+            dst = y_bf[qt][:, first:last, :].rearrange("p (c i) t -> p c t i", i=LINE)
+            src = y[qt][:, :, first:last].rearrange("p t (c i) -> p c t i", i=LINE)
             nc.vector.tensor_copy(dst, src)
 
         def quantize_y(qt, first, last):
+            if first == 0:
+                y_codes[qt] = tile([P, P], U32, "y_codes%d" % qt)
             nc.vector.quantize_mx(
                 out=y_codes[qt][:, first:last].bitcast(FP8X4),
                 scales=y_scales[:, qt * P + first : qt * P + last],
@@ -263,18 +282,20 @@ def tile_attend_docmix_pl_kernel(tc, query, keys_words, keys_scales, size, vals,
                 keys_scales[0, 4 * quad : 4 * quad + 4, :].bitcast(I32),
             )
         nc.sync.dma_start(q_raw[:], query.rearrange("(p j) q -> p j q", j=PACK))
-        size_cols = tile([P, PASSES, PACK], F32, "size_cols")
-        nc.sync.dma_start(size_cols[:], size.rearrange("o (g p t) -> (o p) g t", p=P, t=PACK))
-        for t in range(PACK):
+        for t in range(PACK - 1):
             load_window(t)
+        nc.sync.dma_start(size_cols[:], size.rearrange("o (g p t) -> (o p) g t", p=P, t=PACK))
+        load_window(PACK - 1)
+        make_identity(nc, ident_sums[:])
         make_identity(nc, ident[:])
 
         gather_words(0)
         gather_words(1)
         for qt in range(QTILES):
             round_queries(qt)
-        for half in range(2):
-            gather_scales(half)
+        gather_values(0, 0, False)
+        for g in range(PASSES):
+            gather_scales(g)
         for qt in range(QTILES):
             quantize_queries(qt)
         for qt in range(QTILES):
@@ -289,48 +310,51 @@ def tile_attend_docmix_pl_kernel(tc, query, keys_words, keys_scales, size, vals,
                 exps(qt, g)
                 quarter_sums(qt, g)
             shares(qt)
-        gather_values(0, "q_codes1")
         for qt in range(QTILES):
-            passage_sums(qt)
-        for qt in range(QTILES):
-            invert(qt)
-            factors(qt)
-        gather_values(1)
-        gather_values(2)
+            turn_sums_back(qt)
+        gather_values(0, 1, True, "neg_top0_1")
+        gather_values(1, 0, True)
+        gather_values(1, 1, True)
+        gather_values(2, 0, False, "ident_sums")
+        passage_sums(0)
+        passage_sums(1)
+        invert(0, "partial_sb1")
+        invert(1)
+        ratios(0)
+        ratios(1)
+        gather_values(2, 1, True)
+        gather_values(3, 0, True)
+        gather_values(3, 1, True)
         turn_probs(0, 0, 6)
         turn_probs(0, 1, 7)
-        for t in range(PACK):
-            times_size(0, t)
+        times_size(0)
         turn_probs(1, 0, 4)
         turn_probs(1, 1, 5)
-        for t in range(PACK):
-            times_size(1, t)
-        gather_values(3)
-        turn_values(0, 0)
-        turn_values(1, 2)
-        turn_values(2, 6)
-        turn_values(3, 7)
-        for t in range(PACK):
+        factors(0, 1)
+        times_size(1)
+        factors(1, 3)
+        for t, number in enumerate((0, 2, 6, 5)):
+            turn_values(t, number)
             copy_values(t)
 
         weights(0, 0)
         weights(0, 1)
-        for t in range(PACK - 1):
-            quantize_values(t)
         quantize_weights(0, 0)
         quantize_weights(0, 1)
-        weights(1, 0, "window3")
-        quantize_values(PACK - 1)
+        quantize_values(0)
+        weights(1, 0)
+        quantize_values(1)
         quantize_weights(1, 0)
-        weights(1, 1, "v_bf3")
+        quantize_values(2)
+        quantize_values(3)
+        weights(1, 1, "v_bf2")
         quantize_weights(1, 1)
-        y_scales = tile([P, Q], U8, "y_scales")
-        for qt in range(QTILES):
-            y_bf[qt] = tile([P, P, PACK], BF16, "y_bf%d" % qt)
-            y_codes[qt] = tile([P, P], U32, "y_codes%d" % qt)
-            for g in range(PASSES):
-                for pair in range(PAIRS):
-                    product(qt, pair, g)
+        plane_by_plane = [(h, g) for h in range(2) for g in range(PASSES)]
+        pass_by_pass = [(h, g) for g in range(PASSES) for h in range(2)]
+        product(0, 0, 4, plane_by_plane)
+        product(0, 1, 7, plane_by_plane)
+        product(1, 0, 0, pass_by_pass)
+        product(1, 1, 2, pass_by_pass)
         copy_y(0, 0, False)
         copy_y(0, 1, False)
         store_y(0)

from contextlib import ExitStack

import concourse.mybir as mybir
from concourse.masks import make_identity

D, T, I, Q, E, G = 512, 2048, 1024, 256, 512, 64
FLOPS = 2 * D * Q * I + 2 * I * E * Q

F32 = mybir.dt.float32
BF16 = mybir.dt.bfloat16
I32 = mybir.dt.int32
U32 = mybir.dt.uint32
U16 = mybir.dt.uint16
U8 = mybir.dt.uint8
FP8X4 = mybir.dt.float8_e4m3fn_x4
FP4X4 = mybir.dt.float4_e2m1fn_x4
ALU = mybir.AluOpType
ACT = mybir.ActivationFunctionType
AXIS_X = mybir.AxisListType.X

P = 128
PACK = 4
PASS = P * PACK
RUN = I // G
PASSES = I // PASS
QTILES = Q // P
PAIRS = 2
LINE = 4
TINY = 1e-30


def tile_attend_docmix_pl_kernel(tc, query, keys_words, keys_scales, size, vals, offs, out_0, out_1, out_2):
    nc = tc.nc
    with ExitStack() as ctx:
        sb = ctx.enter_context(tc.tile_pool(name="sb", bufs=1))
        ps = ctx.enter_context(tc.psum_pool(name="ps", bufs=1))

        def tile(shape, dtype, name, tag=None):
            return sb.tile(shape, dtype, name=name, tag=tag or name, align_bytes=64)

        def bank(shape, number, name):
            return ps.tile(shape, F32, name=name, tag="bank%d" % number)

        cols = PASS // 16
        per = PASS // RUN
        offsets = sb.tile([P, I // 16], U16, name="offsets")
        key_pool = tile([P, T], U16, "key_pool")
        scale_pool = tile([P, T], U8, "scale_pool")
        q_raw = tile([P, PACK, Q], F32, "q_raw")
        ident = tile([P, P], F32, "ident")
        ident_sums = tile([P, P], F32, "ident_sums")
        size_cols = tile([P, PASSES, PACK], F32, "size_cols")
        y_scales = tile([P, Q], U8, "y_scales")
        vals_rows = vals.rearrange("(p t) n -> p t n", t=PACK)
        out_rows = out_0.rearrange("(p t) q -> p t q", t=PACK)
        windows, key_words, key_scales, scores, neg_top, probs = {}, {}, {}, {}, {}, {}
        q_bf, q_codes, q_scales, best, share, sums, inverse, ratio, f_turned = {}, {}, {}, {}, {}, {}, {}, {}, {}
        partial, back = {}, {}
        picked, v_turned, v_bf, v_codes, v_scales = {}, {}, {}, {}, {}
        p_turned, sized, w_bf, w_codes, w_scales, acc, y, y_bf, y_codes = {}, {}, {}, {}, {}, {}, {}, {}, {}

        def load_window(t):
            windows[t] = tile([P, T], F32, "window%d" % t)
            nc.sync.dma_start(windows[t][:], vals_rows[:, t, :])

        def gather_words(g):
            key_words[g] = tile([P, PASS], U16, "key_words%d" % g)
            nc.vector.tensor_copy(key_words[g][:], key_pool[:].indirect(offsets[:, g * cols : (g + 1) * cols]))

        def gather_scales(g):
            key_scales[g] = tile([P, PASS], U8, "key_scales%d" % g)
            nc.vector.tensor_copy(key_scales[g][:], scale_pool[:].indirect(offsets[:, g * cols : (g + 1) * cols]))

        def round_queries(qt):
            q_bf[qt] = tile([P, P, PACK], BF16, "q_bf%d" % qt)
            nc.scalar.copy(
                q_bf[qt][:].rearrange("p (c i) j -> p c j i", i=LINE),
                q_raw[:, :, qt * P : (qt + 1) * P].rearrange("p j (c i) -> p c j i", i=LINE),
            )

        def quantize_queries(qt):
            q_codes[qt] = tile([P, P], U32, "q_codes%d" % qt)
            q_scales[qt] = tile([P, P], U8, "q_scales%d" % qt)
            nc.vector.quantize_mx(
                out=q_codes[qt][:].bitcast(FP8X4), scales=q_scales[qt][:], in_=q_bf[qt][:].rearrange("p q j -> p (q j)")
            )

        def score(qt, g):
            scores[qt, g] = bank([P, PASS], 2 * qt + g, "scores%d_%d" % (qt, g))
            nc.tensor.matmul_mx(
                out=scores[qt, g][:],
                lhsT=q_codes[qt][:].bitcast(FP8X4),
                lhsT_scale=q_scales[qt][:],
                rhs=key_words[g][:].bitcast(FP4X4),
                rhs_scale=key_scales[g][:],
                start=True,
                stop=True,
            )

        def maxima(qt, g):
            if g == 0:
                best[qt] = tile([P, G], F32, "best%d" % qt)
            nc.vector.tensor_reduce(
                best[qt][:, g * per : (g + 1) * per],
                scores[qt, g][:].rearrange("p (s i) -> p s i", i=RUN),
                AXIS_X,
                ALU.max,
            )

        def top(qt, g):
            neg_top[qt, g] = tile([P, 1], F32, "neg_top%d_%d" % (qt, g))
            nc.vector.tensor_reduce(neg_top[qt, g][:], best[qt][:, 0 : (g + 1) * per], AXIS_X, ALU.max, negate=True)

        def exps(qt, g):
            probs[qt, g] = tile([P, PACK, P], F32, "probs%d_%d" % (qt, g))
            nc.scalar.activation(
                probs[qt, g][:],
                scores[qt, g][:].rearrange("q (p t) -> q t p", t=PACK),
                ACT.Exp,
                bias=neg_top[qt, g][:],
            )

        def shares(qt):
            share[qt] = tile([P, G], F32, "share%d" % qt)
            sums[qt] = tile([P, G + 1], F32, "sums%d" % qt)
            nc.scalar.activation(share[qt][:], best[qt][:], ACT.Exp, bias=neg_top[qt, PASSES - 1][:], accum_out=sums[qt][:, G : G + 1])

        def quarter_sums(qt, g):
            if g == 0:
                partial[qt] = bank([P, PASSES, P], 4 + qt, "partial%d" % qt)
            for t in range(PACK):
                nc.tensor.matmul(
                    out=partial[qt][:, g, :],
                    lhsT=probs[qt, g][:, t, :],
                    rhs=ident_sums[:],
                    start=(t == 0),
                    stop=(t == PACK - 1),
                    is_transpose=True,
                )

        def turn_sums_back(qt):
            partial_sb = tile([P, PASSES, P], F32, "partial_sb%d" % qt)
            nc.scalar.activation(partial_sb[:], partial[qt][:], ACT.Copy, bias=TINY)
            back[qt] = bank([P, PASSES, P], 2 * qt, "back%d" % qt)
            for g in range(PASSES):
                nc.tensor.transpose(back[qt][:, g, :], partial_sb[:, g, :], ident[:])

        def passage_sums(qt):
            nc.vector.tensor_reduce(
                sums[qt][:, 0:G], back[qt][:].rearrange("p g (s c) -> p (g s) c", c=RUN // PACK), AXIS_X, ALU.add
            )

        def invert(qt, tag=None):
            inverse[qt] = tile([P, G + 1], F32, "inverse%d" % qt, tag)
            nc.vector.reciprocal(inverse[qt][:], sums[qt][:])

        def ratios(qt):
            ratio[qt] = tile([P, G], F32, "ratio%d" % qt)
            nc.vector.tensor_tensor(ratio[qt][:], inverse[qt][:, 0:G], share[qt][:], ALU.mult)

        def factors(qt, number):
            spread = RUN // PACK
            factor = tile([P, G, spread], F32, "factor%d" % qt)
            nc.scalar.activation(
                factor[:], ratio[qt][:].unsqueeze(2).to_broadcast([P, G, spread]), ACT.Copy, scale=inverse[qt][:, G : G + 1]
            )
            f_turned[qt] = bank([P, PASSES, P], number, "f_turned%d" % qt)
            for g in range(PASSES):
                nc.tensor.transpose(
                    f_turned[qt][:, g, :], factor[:, g * per : (g + 1) * per, :].rearrange("p s c -> p (s c)"), ident[:]
                )

        def turn_probs(g, half, number):
            p_turned[g, half] = bank([P, 2, Q], number, "p_turned%d_%d" % (g, half))
            for qt in range(QTILES):
                for u in range(2):
                    nc.tensor.transpose(p_turned[g, half][:, u, qt * P : (qt + 1) * P], probs[qt, g][:, 2 * half + u, :], ident[:])

        def times_size(g):
            sized[g] = tile([P, PACK, Q], F32, "sized%d" % g)
            for t in range(PACK):
                nc.scalar.activation(
                    sized[g][:, t, :], p_turned[g, t // 2][:, t % 2, :], ACT.Copy, scale=size_cols[:, g, t : t + 1]
                )

        def gather_values(t, g, on_vector, tag=None):
            picked[t, g] = tile([P, PASS], BF16, "picked%d_%d" % (t, g), tag)
            listed = windows[t][:].indirect(offsets[:, g * cols : (g + 1) * cols])
            if on_vector:
                nc.vector.tensor_copy(picked[t, g][:], listed)
            else:
                nc.scalar.activation(picked[t, g][:], listed, ACT.Copy)

        def turn_values(t, number):
            v_turned[t] = bank([P, PASSES, 2, P], number, "v_turned%d" % t)
            for g in range(PASSES):
                words = picked[t, g][:].bitcast(F32)
                for u in range(2):
                    nc.tensor.transpose(v_turned[t][:, g, u, :], words[:, u : 2 * P : 2], ident[:])

        def copy_values(t):
            v_bf[t] = tile([P, PASSES, P, 2], F32, "v_bf%d" % t)
            nc.scalar.copy(v_bf[t][:], v_turned[t][:].rearrange("p g u e -> p g e u"))

        def quantize_values(t):
            codes = tile([P, PASSES * P], U32, "v_codes%d" % t)
            scales = tile([P, PASSES * P], U8, "v_scales%d" % t)
            nc.vector.quantize_mx(
                out=codes[:].bitcast(FP8X4), scales=scales[:], in_=v_bf[t][:].rearrange("p g e u -> p (g e u)").bitcast(BF16)
            )
            for g in range(PASSES):
                v_codes[t, g] = codes[:, g * P : (g + 1) * P]
                v_scales[t, g] = scales[:, g * P : (g + 1) * P]

        def weights(qt, g, tag=None):
            w_bf[qt, g] = tile([P, P, PACK], BF16, "w_bf%d_%d" % (qt, g), tag)
            nc.vector.tensor_tensor(
                w_bf[qt, g][:].rearrange("p (c i) t -> p c t i", i=LINE),
                sized[g][:, :, qt * P : (qt + 1) * P].rearrange("p t (c i) -> p c t i", i=LINE),
                f_turned[qt][:, g, :].rearrange("p (c i) -> p c i", i=LINE).unsqueeze(2).to_broadcast([P, P // LINE, PACK, LINE]),
                ALU.mult,
            )

        def quantize_weights(qt, g):
            w_codes[qt, g] = tile([P, P], U32, "w_codes%d_%d" % (qt, g))
            w_scales[qt, g] = tile([P, P], U8, "w_scales%d_%d" % (qt, g))
            nc.vector.quantize_mx(
                out=w_codes[qt, g][:].bitcast(FP8X4), scales=w_scales[qt, g][:], in_=w_bf[qt, g][:].rearrange("p q t -> p (q t)")
            )

        def product(qt, pair, number, steps):
            acc[qt, pair] = bank([P, 2, P], number, "acc%d_%d" % (qt, pair))
            for h, g in steps:
                nc.tensor.matmul_mx(
                    out=acc[qt, pair][:, h, :],
                    lhsT=v_codes[2 * pair + h, g].bitcast(FP8X4),
                    lhsT_scale=v_scales[2 * pair + h, g],
                    rhs=w_codes[qt, g][:].bitcast(FP8X4),
                    rhs_scale=w_scales[qt, g][:],
                    start=((h, g) == steps[0]),
                    stop=((h, g) == steps[-1]),
                )

        def copy_y(qt, pair, on_vector):
            if pair == 0:
                y[qt] = tile([P, PACK, P], F32, "y%d" % qt)
            rows = slice(2 * pair, 2 * pair + 2)
            if on_vector:
                nc.vector.tensor_copy(y[qt][:, rows, :], acc[qt, pair][:])
            else:
                nc.scalar.copy(y[qt][:, rows, :], acc[qt, pair][:])

        def store_y(qt):
            nc.sync.dma_start(out_rows[:, :, qt * P : (qt + 1) * P], y[qt][:])

        def round_y(qt, first, last):
            if first == 0:
                y_bf[qt] = tile([P, P, PACK], BF16, "y_bf%d" % qt)
            dst = y_bf[qt][:, first:last, :].rearrange("p (c i) t -> p c t i", i=LINE)
            src = y[qt][:, :, first:last].rearrange("p t (c i) -> p c t i", i=LINE)
            nc.vector.tensor_copy(dst, src)

        def quantize_y(qt, first, last):
            if first == 0:
                y_codes[qt] = tile([P, P], U32, "y_codes%d" % qt)
            nc.vector.quantize_mx(
                out=y_codes[qt][:, first:last].bitcast(FP8X4),
                scales=y_scales[:, qt * P + first : qt * P + last],
                in_=y_bf[qt][:, first:last, :].rearrange("p q t -> p (q t)"),
            )

        def store_codes(qt):
            words = out_1[0].rearrange("p q t -> p (q t)").bitcast(I32)
            nc.sync.dma_start(words[:, qt * P : (qt + 1) * P], y_codes[qt][:].bitcast(I32))

        nc.gpsimd.memset(scale_pool[:].bitcast(I32), 0)
        nc.sync.dma_start(offsets[:], offs)
        nc.sync.dma_start(key_pool[:].bitcast(I32), keys_words[0].bitcast(I32))
        for quad in range(4):
            nc.sync.dma_start(
                scale_pool[32 * quad : 32 * quad + 4, :].bitcast(I32),
                keys_scales[0, 4 * quad : 4 * quad + 4, :].bitcast(I32),
            )
        nc.sync.dma_start(q_raw[:], query.rearrange("(p j) q -> p j q", j=PACK))
        for t in range(PACK - 1):
            load_window(t)
        nc.sync.dma_start(size_cols[:], size.rearrange("o (g p t) -> (o p) g t", p=P, t=PACK))
        load_window(PACK - 1)
        make_identity(nc, ident_sums[:])
        make_identity(nc, ident[:])

        gather_words(0)
        gather_words(1)
        for qt in range(QTILES):
            round_queries(qt)
        gather_values(0, 0, False)
        for g in range(PASSES):
            gather_scales(g)
        for qt in range(QTILES):
            quantize_queries(qt)
        for qt in range(QTILES):
            for g in range(PASSES):
                score(qt, g)
        for qt in range(QTILES):
            for g in range(PASSES):
                maxima(qt, g)
                top(qt, g)
        for qt in range(QTILES):
            for g in range(PASSES):
                exps(qt, g)
                quarter_sums(qt, g)
            shares(qt)
        for qt in range(QTILES):
            turn_sums_back(qt)
        gather_values(0, 1, True, "neg_top0_1")
        gather_values(1, 0, True)
        gather_values(1, 1, True)
        gather_values(2, 0, False, "ident_sums")
        passage_sums(0)
        passage_sums(1)
        invert(0, "partial_sb1")
        invert(1)
        ratios(0)
        ratios(1)
        gather_values(2, 1, True)
        gather_values(3, 0, True)
        gather_values(3, 1, True)
        turn_probs(0, 0, 6)
        turn_probs(0, 1, 7)
        times_size(0)
        turn_probs(1, 0, 4)
        turn_probs(1, 1, 5)
        factors(0, 1)
        times_size(1)
        factors(1, 3)
        for t, number in enumerate((0, 2, 6, 5)):
            turn_values(t, number)
            copy_values(t)

        weights(0, 0)
        weights(0, 1)
        quantize_weights(0, 0)
        quantize_weights(0, 1)
        quantize_values(0)
        weights(1, 0)
        quantize_values(1)
        quantize_weights(1, 0)
        quantize_values(2)
        quantize_values(3)
        weights(1, 1, "v_bf2")
        quantize_weights(1, 1)
        plane_by_plane = [(h, g) for h in range(2) for g in range(PASSES)]
        pass_by_pass = [(h, g) for g in range(PASSES) for h in range(2)]
        product(0, 0, 4, plane_by_plane)
        product(0, 1, 7, plane_by_plane)
        product(1, 0, 0, pass_by_pass)
        product(1, 1, 2, pass_by_pass)
        copy_y(0, 0, False)
        copy_y(0, 1, False)
        store_y(0)
        round_y(0, 0, P)
        copy_y(1, 0, False)
        copy_y(1, 1, True)
        store_y(1)
        quantize_y(0, 0, P)
        store_codes(0)
        for half in range(2):
            round_y(1, half * P // 2, (half + 1) * P // 2)
        for half in range(2):
            quantize_y(1, half * P // 2, (half + 1) * P // 2)
        store_codes(1)
        for quad in range(4):
            queue = nc.scalar if quad % 2 == 0 else nc.sync
            queue.dma_start(
                out_2[0, 4 * quad : 4 * quad + 4, :].bitcast(I32),
                y_scales[32 * quad : 32 * quad + 4, :].bitcast(I32),
            )
